import numpy as np
import ml_dtypes


def mxq(x, axis, fmt="e4m3"):
    dtype, down = {"e4m3": (ml_dtypes.float8_e4m3fn, 7), "e5m2": (ml_dtypes.float8_e5m2, 14)}[fmt]
    v = np.moveaxis(np.asarray(x, np.float32).astype(ml_dtypes.bfloat16).astype(np.float64), axis, -1)
    blocks = v.reshape(v.shape[:-1] + (-1, 32))
    amax = np.abs(blocks).max(-1, keepdims=True)
    byte = np.maximum(np.where(amax > 0, np.frexp(amax)[1] - 1 + 127, 0) - down, 1)
    scale = np.exp2(byte - 127.0)
    codes = (blocks / scale).astype(np.float32).astype(dtype).astype(np.float64)
    return np.moveaxis((codes * scale).reshape(v.shape), -1, axis)


WIDE = False


def mx_kscale(k):
    if not WIDE:
        return np.ones(k)
    levels = np.array([10, -10, 5, -5, 0])
    if k % 512:
        return np.exp2(np.random.permutation(np.resize(levels, k // 32))).repeat(32)
    a = np.empty((k // 512, 16))
    for p in range(k // 512):
        a[p, :8] = np.random.permutation(np.resize(levels, 8))
        for g in range(8):
            far = levels[np.abs(levels - a[p, g]) >= 10]
            a[p, g + 8] = far[np.random.randint(len(far))]
    return np.exp2(a.ravel()).repeat(32)


BF16 = ml_dtypes.bfloat16


def bf(x):
    return np.asarray(x, np.float32).astype(BF16)


def f64(x):
    return np.asarray(x).astype(np.float64)


E2M1 = np.array([0.0, 0.5, 1.0, 1.5, 2.0, 3.0, 4.0, 6.0, -0.0, -0.5, -1.0, -1.5, -2.0, -3.0, -4.0, -6.0])


def pack_weight(w, fmt):
    k, n = w.shape
    w = f64(bf(w)).reshape(k // 32, 32, n)
    amax = np.abs(w).max(1)
    if fmt == "e4m3":
        byte = np.frexp(amax)[1] - 1 + 127 - 7
    else:
        mant, ex = np.frexp(amax / 6.0)
        byte = np.where(mant > 0.5, ex, ex - 1) + 127
    byte = np.clip(np.where(amax > 0, byte, 1), 1, 254)
    scaled = (w * np.exp2(127.0 - byte)[:, None, :]).reshape(k, n).astype(np.float32)
    by_word = np.ascontiguousarray(scaled.reshape(k // 512, 128, 4, n).transpose(0, 1, 3, 2))
    if fmt == "e4m3":
        words = by_word.astype(ml_dtypes.float8_e4m3fn).view(np.uint8)
    else:
        c = by_word.astype(ml_dtypes.float4_e2m1fn).view(np.uint8) & 0xF
        words = c[..., 0::2] | (c[..., 1::2] << 4)
    return np.ascontiguousarray(words), np.ascontiguousarray(byte.astype(np.uint8).reshape(k // 512, 16, n))


def unpack_weight(words, scales, fmt):
    g, p, n, _ = words.shape
    if fmt == "e4m3":
        vals = np.ascontiguousarray(words).view(ml_dtypes.float8_e4m3fn).astype(np.float64)
    else:
        nib = np.empty((g, p, n, 4), np.uint8)
        nib[..., 0::2] = words & 0xF
        nib[..., 1::2] = words >> 4
        vals = E2M1[nib]
    vals = vals * np.repeat(np.exp2(scales.astype(np.float64) - 127.0), 8, axis=1)[..., None]
    return vals.transpose(0, 1, 3, 2).reshape(g * 512, n)
def pack4(w):
    words, scales = pack_weight(w, "e2m1")
    return words.reshape(words.shape[0], 128, -1), scales


def unpack4(words, scales):
    return unpack_weight(words.reshape(words.shape[0], 128, -1, 2), scales, "e2m1")


E4M3FN = np.array([(-1.0 if i & 128 else 1.0) * ((1.0 + (i & 7) / 8.0) * 2.0 ** (((i >> 3) & 15) - 7) if i & 120 else (i & 7) * 2.0 ** -9) for i in range(256)])


def e4m3fn_bytes(y):
    return np.clip(np.asarray(y, np.float64), -448.0, 448.0).astype(np.float32).astype(ml_dtypes.float8_e4m3fn).view(np.uint8)


def e4m3fn_values(b):
    return E4M3FN[b]


T, K, B, N, G = 4096, 1024, 512, 1024, 128


def setup_inputs():
    s, t = mx_kscale(K), mx_kscale(T)
    d = np.random.standard_normal((T, K)) * np.exp(0.3 * np.random.standard_normal((T, 1)))
    norms = np.sqrt(np.sum(d ** 2, axis=1))
    x = d * s
    docs_scale = (np.abs(x).reshape(T, K // G, G).max(axis=2) / 448.0).astype(np.float32)
    docs_bytes = e4m3fn_bytes(x / np.repeat(f64(docs_scale), G, axis=1))
    v_words, v_scales = pack4(np.random.standard_normal((T, N)) / np.sqrt(T) / t[:, None])
    return {"docs_bytes": docs_bytes,
            "docs_scale": docs_scale,
            "queries": bf(np.random.standard_normal((B, K)) / s),
            "norms": bf(norms / t),
            "v_words": v_words,
            "v_scales": v_scales}


def reference(docs_bytes, docs_scale, queries, norms, v_words, v_scales):
    docs = e4m3fn_values(docs_bytes) * np.repeat(f64(docs_scale), G, axis=1)
    scores = mxq(docs, 1, "e4m3") @ mxq(f64(queries), 1, "e4m3").T
    rel = np.maximum(scores / f64(norms)[:, None], 0.0)
    return mxq(rel, 0, "e4m3").T @ unpack4(v_words, v_scales)

@@ -1,0 +1,315 @@
+from contextlib import ExitStack
+
+import concourse.mybir as mybir
+from concourse.masks import make_identity
+
+T, K, B, N, G = 4096, 1024, 512, 1024, 128
+FLOPS = 2 * T * K * B + 2 * B * T * N
+
+F32 = mybir.dt.float32
+BF16 = mybir.dt.bfloat16
+I32 = mybir.dt.int32
+U32 = mybir.dt.uint32
+U8 = mybir.dt.uint8
+FP8 = mybir.dt.float8_e4m3fn
+FP8X4 = mybir.dt.float8_e4m3fn_x4
+FP4X4 = mybir.dt.float4_e2m1fn_x4
+ACT = mybir.ActivationFunctionType
+ALU = mybir.AluOpType
+
+P = 128
+PACK = 4
+PASS = P * PACK
+GROUPS = T // PASS
+K_PASSES = K // PASS
+Q_TILES = B // P
+N_TILE = 512
+RUN = 16
+SCALAR_QUERIES = 64
+
+
+def tile_archived_docs_feedback_d4_kernel(tc, docs_bytes, docs_scale, queries, norms, v_words, v_scales, out):
+    nc = tc.nc
+    with ExitStack() as ctx:
+        keep = ctx.enter_context(tc.tile_pool(name="keep", bufs=1))
+        work = ctx.enter_context(tc.tile_pool(name="work", bufs=2))
+        psum = ctx.enter_context(tc.psum_pool(name="psum", bufs=1))
+        ctx.enter_context(tc.manual_schedule())
+
+        docs_rows = docs_bytes.rearrange("(g m t) k -> g m t k", m=P, t=PACK)
+        scale_rows = docs_scale.rearrange("(g m t) i -> m g (t i)", m=P, t=PACK)
+        blocks = K // G
+
+        ident = keep.tile([P, P], F32, name="ident")
+        make_identity(nc, ident[:])
+        v_scale = keep.tile([P, GROUPS, N], U8, name="v_scale", align_bytes=64)
+        nc.vector.memset(v_scale[:].rearrange("p g n -> p (g n)").bitcast(I32), 0)
+
+        doc_bytes = {}
+        v_codes = {}
+        q_raw = {}
+
+        def load_docs(g, h):
+            tile = keep.tile([P, 2, K], U8, name="doc_bytes_%d_%d" % (g, h), align_bytes=64)
+            nc.sync.dma_start(out=tile[:], in_=docs_rows[g, :, 2 * h : 2 * h + 2, :])
+            doc_bytes[(g, h)] = tile
+
+        def load_v(g):
+            tile = keep.tile([P, 2 * N], U8, name="v_codes_%d" % g, align_bytes=64)
+            nc.sync.dma_start(out=tile[:].bitcast(I32), in_=v_words[g].bitcast(I32))
+            v_codes[g] = tile
+
+        def load_queries(h):
+            tile = keep.tile([P, 2, K], BF16, name="q_raw_%d" % h, align_bytes=64)
+            nc.sync.dma_start(out=tile[:], in_=queries[2 * h * P : (2 * h + 2) * P, :].rearrange("(j m) k -> m j k", m=P))
+            q_raw[h] = tile
+
+        scale_first = keep.tile([P, 1, PACK * blocks], F32, name="scale_first")
+        scale_rest = keep.tile([P, GROUPS - 1, PACK * blocks], F32, name="scale_rest")
+        norms_raw = keep.tile([P, GROUPS, PACK], BF16, name="norms_raw")
+        nc.sync.dma_start(out=scale_first[:], in_=scale_rows[:, 0:1, :])
+        nc.scalar.dma_start(out=norms_raw[:], in_=norms.rearrange("(g m t) -> m g t", m=P, t=PACK))
+        load_docs(0, 0)
+        load_queries(0)
+        load_docs(0, 1)
+        load_queries(1)
+        nc.sync.dma_start(out=scale_rest[:], in_=scale_rows[:, 1:GROUPS, :])
+        load_docs(1, 0)
+        load_docs(1, 1)
+        load_docs(2, 0)
+        load_docs(2, 1)
+        for q in range(4):
+            nc.sync.dma_start(
+                out=v_scale[32 * q : 32 * q + 4, :, :].bitcast(I32),
+                in_=v_scales[:, 4 * q : 4 * q + 4, :].rearrange("g r n -> r g n").bitcast(I32),
+            )
+        for g in range(GROUPS):
+            if g + 3 < GROUPS:
+                load_docs(g + 3, 0)
+                load_docs(g + 3, 1)
+            load_v(g)
+
+        norms_f32 = keep.tile([P, GROUPS * PACK], F32, name="norms_f32")
+        nc.scalar.activation(out=norms_f32[:], in_=norms_raw[:].rearrange("p g t -> p (g t)"), func=ACT.Relu)
+        inv_norms = keep.tile([P, GROUPS * PACK], F32, name="inv_norms")
+
+        wide = {}
+        turned = {}
+        banks = {}
+        doc_codes = {}
+        rel_planes = {}
+        rel_packed = {}
+        rel_codes = {}
+        sums = {}
+
+        def widen(g, t):
+            tile = work.tile([P, 2, K // (2 * RUN), RUN], BF16, name="wide", tag="wide", bufs=8, align_bytes=64)
+            wide[(g, t)] = tile
+            src = doc_bytes[(g, t // 2)]
+            scales = scale_first[:, 0, :] if g == 0 else scale_rest[:, g - 1, :]
+            per = G // (2 * RUN)
+            for i in range(blocks):
+                nc.vector.tensor_scalar(
+                    out=tile[:, :, per * i : per * (i + 1), :].rearrange("p u b r -> p b u r"),
+                    in0=src[:, t % 2, G * i : G * (i + 1)].bitcast(FP8).rearrange("p (b u r) -> p b u r", u=2, r=RUN),
+                    scalar1=scales[:, t * blocks + i : t * blocks + i + 1],
+                    scalar2=None,
+                    op0=ALU.mult,
+                )
+
+        def reorder_queries(j, on_scalar):
+            tile = keep.tile([P, 2, K // (2 * RUN), RUN], BF16, name="q_wide_%d" % j, align_bytes=64)
+            wide[("q", j)] = tile
+            src = q_raw[j // 2][:, j % 2, :].rearrange("p (b u r) -> p u b r", u=2, r=RUN)
+            if on_scalar:
+                nc.scalar.copy(out=tile[:], in_=src)
+            else:
+                nc.vector.tensor_copy(out=tile[:], in_=src)
+
+        def transpose(key, tag):
+            bank = psum.tile([P, K_PASSES, 2, P], F32, name=tag, tag=tag)
+            banks[key] = bank
+            words = wide[key][:].rearrange("p u b r -> p (u b r)").bitcast(F32)
+            for s in range(K_PASSES):
+                for u in range(2):
+                    first = (u * K_PASSES + s) * P
+                    nc.tensor.transpose(bank[:, s, u, :], words[:, first : first + P], ident[:])
+
+        def copy_turned(key, dst):
+            nc.scalar.copy(out=dst, in_=banks[key][:].rearrange("p s u d -> p s d u"))
+
+        def copy_docs(g, t):
+            if t % 2 == 0:
+                turned[(g, t // 2)] = work.tile([P, 2, K_PASSES, P, 2], F32, name="turned", tag="turned", bufs=4, align_bytes=64)
+            copy_turned((g, t), turned[(g, t // 2)][:, t % 2, :, :, :])
+
+        def quantize_docs(g, h):
+            codes = work.tile([P, 2 * K_PASSES * P], U32, name="doc_codes", tag="doc_codes", bufs=6, align_bytes=64)
+            scales = work.tile([P, 2 * K_PASSES * P], U8, name="doc_scales", tag="doc_scales", bufs=6, align_bytes=64)
+            doc_codes[(g, h)] = (codes, scales)
+            nc.vector.quantize_mx(
+                out=codes[:].bitcast(FP8X4),
+                scales=scales[:],
+                in_=turned[(g, h)][:].rearrange("p t s d u -> p (t s d u)").bitcast(BF16),
+            )
+
+        q_turned = keep.tile([P, K_PASSES, B, 2], F32, name="q_turned", align_bytes=64)
+        q_codes = keep.tile([P, K_PASSES, B], U32, name="q_codes", align_bytes=64)
+        q_scales = keep.tile([P, K_PASSES, B], U8, name="q_scales", align_bytes=64)
+
+        def quantize_queries(s):
+            nc.vector.quantize_mx(
+                out=q_codes[:, s, :].bitcast(FP8X4),
+                scales=q_scales[:, s, :],
+                in_=q_turned[:, s, :, :].rearrange("p b u -> p (b u)").bitcast(BF16),
+            )
+
+        def scores(g, t, tag):
+            bank = psum.tile([P, B], F32, name=tag, tag=tag)
+            codes, scales = doc_codes[(g, t // 2)]
+            for s in range(K_PASSES):
+                first = ((t % 2) * K_PASSES + s) * P
+                nc.tensor.matmul_mx(
+                    out=bank[:],
+                    lhsT=codes[:, first : first + P].bitcast(FP8X4),
+                    lhsT_scale=scales[:, first : first + P],
+                    rhs=q_codes[:, s, :].bitcast(FP8X4),
+                    rhs_scale=q_scales[:, s, :],
+                    start=(s == 0),
+                    stop=(s == K_PASSES - 1),
+                )
+            if t == 0:
+                rel_planes[g] = work.tile([P, PACK, B], BF16, name="rel_planes", tag="rel_planes", bufs=3, align_bytes=64)
+            nc.scalar.activation(
+                out=rel_planes[g][:, t, :],
+                in_=bank[:],
+                func=ACT.Relu,
+                scale=inv_norms[:, g * PACK + t : g * PACK + t + 1],
+            )
+
+        def interleave(g, scalar_queries):
+            tile = work.tile([P, B, PACK], BF16, name="rel_packed", tag="rel_packed", bufs=2, align_bytes=64)
+            rel_packed[g] = tile
+            split = B - scalar_queries
+            nc.vector.tensor_copy(
+                out=tile[:, 0:split, :].rearrange("p (c i) t -> p c t i", i=4),
+                in_=rel_planes[g][:, :, 0:split].rearrange("p t (c i) -> p c t i", i=4),
+            )
+            if scalar_queries:
+                nc.scalar.copy(
+                    out=tile[:, split:B, :].rearrange("p (c i) t -> p c t i", i=4),
+                    in_=rel_planes[g][:, :, split:B].rearrange("p t (c i) -> p c t i", i=4),
+                )
+
+        def quantize_rel(g):
+            codes = keep.tile([P, B], U32, name="rel_codes_%d" % g, align_bytes=64)
+            scales = keep.tile([P, B], U8, name="rel_scales_%d" % g, align_bytes=64)
+            rel_codes[g] = (codes, scales)
+            nc.vector.quantize_mx(
+                out=codes[:].bitcast(FP8X4), scales=scales[:], in_=rel_packed[g][:].rearrange("p b t -> p (b t)")
+            )
+
+        def pool_pass(g, j, h, tag):
+            if g == 0:
+                sums[(j, h)] = psum.tile([P, N_TILE], F32, name=tag, tag=tag)
+            codes, scales = rel_codes[g]
+            nc.tensor.matmul_mx(
+                out=sums[(j, h)][:],
+                lhsT=codes[:, j * P : (j + 1) * P].bitcast(FP8X4),
+                lhsT_scale=scales[:, j * P : (j + 1) * P],
+                rhs=v_codes[g][:, 2 * h * N_TILE : 2 * (h + 1) * N_TILE].bitcast(FP4X4),
+                rhs_scale=v_scale[:, g, h * N_TILE : (h + 1) * N_TILE],
+                start=(g == 0),
+                stop=(g == GROUPS - 1),
+            )
+
+        def store(j, h, on_scalar):
+            result = work.tile([P, N_TILE], F32, name="result", tag="result", bufs=8)
+            if on_scalar:
+                nc.scalar.copy(out=result[:], in_=sums[(j, h)][:])
+            else:
+                nc.vector.tensor_copy(out=result[:], in_=sums[(j, h)][:])
+            nc.sync.dma_start(out=out[j * P : (j + 1) * P, h * N_TILE : (h + 1) * N_TILE], in_=result[:])
+
+        def rot(t):
+            return "rot%d" % t
+
+        def acc(j):
+            return "acc%d" % j
+
+        for h in range(2):
+            for t in (2 * h, 2 * h + 1):
+                widen(0, t)
+                transpose((0, t), rot(t))
+            reorder_queries(2 * h, True)
+            reorder_queries(2 * h + 1, False)
+            copy_docs(0, 2 * h)
+            copy_docs(0, 2 * h + 1)
+            for j in (2 * h, 2 * h + 1):
+                transpose(("q", j), acc(j))
+            for j in (2 * h, 2 * h + 1):
+                copy_turned(("q", j), q_turned[:, :, j * P : (j + 1) * P, :])
+        nc.vector.reciprocal(out=inv_norms[:], in_=norms_f32[:])
+        quantize_docs(0, 0)
+        widen(1, 0)
+        widen(1, 1)
+        quantize_docs(0, 1)
+        widen(1, 2)
+        quantize_queries(0)
+        quantize_queries(1)
+        widen(1, 3)
+
+        last = GROUPS - 1
+        for c in range(last):
+            for t in range(PACK):
+                transpose((c + 1, t), rot(t))
+            if c + 2 <= last:
+                widen(c + 2, 0)
+                widen(c + 2, 1)
+            for t in range(PACK):
+                copy_docs(c + 1, t)
+            if c >= 1:
+                interleave(c - 1, SCALAR_QUERIES)
+            if c >= 2:
+                for j in range(Q_TILES):
+                    pool_pass(c - 2, j, 0, acc(j))
+            if c + 2 <= last:
+                widen(c + 2, 2)
+                widen(c + 2, 3)
+            if c >= 1:
+                quantize_rel(c - 1)
+            for t in range(PACK):
+                scores(c, t, rot(t))
+            quantize_docs(c + 1, 0)
+            quantize_docs(c + 1, 1)
+
+        interleave(last - 1, 0)
+        for j in range(Q_TILES):
+            pool_pass(last - 2, j, 0, acc(j))
+        scores(last, 0, rot(0))
+        scores(last, 1, rot(1))
+        quantize_rel(last - 1)
+        for g in range(3):
+            pool_pass(g, 2, 1, rot(2))
+        scores(last, 2, rot(0))
+        scores(last, 3, rot(1))
+        interleave(last, 128)
+        quantize_rel(last)
+        for g in range(3, last):
+            pool_pass(g, 2, 1, rot(2))
+        for j in range(Q_TILES):
+            pool_pass(last - 1, j, 0, acc(j))
+        for g in range(3):
+            pool_pass(g, 3, 1, rot(3))
+        for j in range(Q_TILES):
+            pool_pass(last, j, 0, acc(j))
+            store(j, 0, j % 2 == 0)
+        pool_pass(last, 2, 1, rot(2))
+        store(2, 1, True)
+        for g in range(3, GROUPS):
+            pool_pass(g, 3, 1, rot(3))
+        store(3, 1, False)
+        for j in range(2):
+            for g in range(GROUPS):
+                pool_pass(g, j, 1, rot(j))
+            store(j, 1, j % 2 == 0)

@@ -25,7 +25,26 @@ K_PASSES = K // PASS
 Q_TILES = B // P
 N_TILE = 512
 RUN = 16
-SCALAR_QUERIES = 64
+STEPS = 2 * GROUPS
+HALF = B // 2
+SUMS = 5
+SCALAR_QUERIES = 48
+WIDEN_LEAD = 1
+WARM = 7
+V_COPY_FROM = 16
+V_REL_FROM = 16
+S_SHARE_TO = 13
+REL_LAG = 1
+POOL_LAG = 2
+HEAD = 2
+PRE = 1
+SHARE_POS = 0
+FIRST = 0
+Q_EARLY = 0
+LATE_FIRST = 1
+LATE_SECOND = 6
+LATE_THIRD = 6
+TAIL_SHARE = 96
 
 
 def tile_archived_docs_feedback_d4_kernel(tc, docs_bytes, docs_scale, queries, norms, v_words, v_scales, out):
@@ -40,8 +59,12 @@ def tile_archived_docs_feedback_d4_kernel(tc, docs_bytes, docs_scale, queries, n
         scale_rows = docs_scale.rearrange("(g m t) i -> m g (t i)", m=P, t=PACK)
         blocks = K // G
 
+        ident_raw = keep.tile([P, P], F32, name="ident_raw")
+        make_identity(nc, ident_raw[:])
         ident = keep.tile([P, P], F32, name="ident")
-        make_identity(nc, ident[:])
+        nc.scalar.activation(out=ident[:], in_=ident_raw[:], func=ACT.Relu)
+        warm = keep.tile([P, N_TILE], BF16, name="warm")
+        nc.vector.memset(warm[:], 0.0)
         v_scale = keep.tile([P, GROUPS, N], U8, name="v_scale", align_bytes=64)
         nc.vector.memset(v_scale[:].rearrange("p g n -> p (g n)").bitcast(I32), 0)
 
@@ -49,48 +72,55 @@ def tile_archived_docs_feedback_d4_kernel(tc, docs_bytes, docs_scale, queries, n
         v_codes = {}
         q_raw = {}
 
-        def load_docs(g, h):
-            tile = keep.tile([P, 2, K], U8, name="doc_bytes_%d_%d" % (g, h), align_bytes=64)
-            nc.sync.dma_start(out=tile[:], in_=docs_rows[g, :, 2 * h : 2 * h + 2, :])
-            doc_bytes[(g, h)] = tile
+        def load_docs(g, t0, n):
+            tile = keep.tile([P, n, K], U8, name="doc_bytes_%d_%d" % (g, t0), align_bytes=64)
+            nc.sync.dma_start(out=tile[:], in_=docs_rows[g, :, t0 : t0 + n, :])
+            for i in range(n):
+                doc_bytes[(g, t0 + i)] = tile[:, i, :]
 
         def load_v(g):
             tile = keep.tile([P, 2 * N], U8, name="v_codes_%d" % g, align_bytes=64)
             nc.sync.dma_start(out=tile[:].bitcast(I32), in_=v_words[g].bitcast(I32))
             v_codes[g] = tile
 
-        def load_queries(h):
-            tile = keep.tile([P, 2, K], BF16, name="q_raw_%d" % h, align_bytes=64)
-            nc.sync.dma_start(out=tile[:], in_=queries[2 * h * P : (2 * h + 2) * P, :].rearrange("(j m) k -> m j k", m=P))
-            q_raw[h] = tile
+        def load_queries(j):
+            tile = keep.tile([P, K], BF16, name="q_raw_%d" % j, align_bytes=64)
+            nc.sync.dma_start(out=tile[:], in_=queries[j * P : (j + 1) * P, :])
+            q_raw[j] = tile
 
-        scale_first = keep.tile([P, 1, PACK * blocks], F32, name="scale_first")
-        scale_rest = keep.tile([P, GROUPS - 1, PACK * blocks], F32, name="scale_rest")
+        doc_scale = {}
+
+        def load_scales(g0, g1):
+            tile = keep.tile([P, g1 - g0, PACK * blocks], F32, name="doc_scale_%d" % g0)
+            nc.sync.dma_start(out=tile[:], in_=scale_rows[:, g0:g1, :])
+            for g in range(g0, g1):
+                doc_scale[g] = tile[:, g - g0, :]
+
         norms_raw = keep.tile([P, GROUPS, PACK], BF16, name="norms_raw")
-        nc.sync.dma_start(out=scale_first[:], in_=scale_rows[:, 0:1, :])
-        nc.scalar.dma_start(out=norms_raw[:], in_=norms.rearrange("(g m t) -> m g t", m=P, t=PACK))
-        load_docs(0, 0)
+        load_scales(0, 1)
+        load_docs(0, 0, 1)
         load_queries(0)
-        load_docs(0, 1)
         load_queries(1)
-        nc.sync.dma_start(out=scale_rest[:], in_=scale_rows[:, 1:GROUPS, :])
-        load_docs(1, 0)
-        load_docs(1, 1)
-        load_docs(2, 0)
-        load_docs(2, 1)
+        load_docs(0, 1, 1)
+        load_queries(2)
+        load_queries(3)
+        load_docs(0, 2, 2)
+        load_scales(1, 2)
+        load_docs(1, 0, 2)
+        nc.sync.dma_start(out=norms_raw[:], in_=norms.rearrange("(g m t) -> m g t", m=P, t=PACK))
+        load_docs(1, 2, 2)
+        load_scales(2, GROUPS)
+        load_docs(2, 0, PACK)
         for q in range(4):
             nc.sync.dma_start(
                 out=v_scale[32 * q : 32 * q + 4, :, :].bitcast(I32),
                 in_=v_scales[:, 4 * q : 4 * q + 4, :].rearrange("g r n -> r g n").bitcast(I32),
             )
         for g in range(GROUPS):
-            if g + 3 < GROUPS:
-                load_docs(g + 3, 0)
-                load_docs(g + 3, 1)
             load_v(g)
+            if g + 3 < GROUPS:
+                load_docs(g + 3, 0, PACK)
 
-        norms_f32 = keep.tile([P, GROUPS * PACK], F32, name="norms_f32")
-        nc.scalar.activation(out=norms_f32[:], in_=norms_raw[:].rearrange("p g t -> p (g t)"), func=ACT.Relu)
         inv_norms = keep.tile([P, GROUPS * PACK], F32, name="inv_norms")
 
         wide = {}
@@ -105,13 +135,13 @@ def tile_archived_docs_feedback_d4_kernel(tc, docs_bytes, docs_scale, queries, n
         def widen(g, t):
             tile = work.tile([P, 2, K // (2 * RUN), RUN], BF16, name="wide", tag="wide", bufs=8, align_bytes=64)
             wide[(g, t)] = tile
-            src = doc_bytes[(g, t // 2)]
-            scales = scale_first[:, 0, :] if g == 0 else scale_rest[:, g - 1, :]
+            src = doc_bytes[(g, t)]
+            scales = doc_scale[g]
             per = G // (2 * RUN)
             for i in range(blocks):
                 nc.vector.tensor_scalar(
                     out=tile[:, :, per * i : per * (i + 1), :].rearrange("p u b r -> p b u r"),
-                    in0=src[:, t % 2, G * i : G * (i + 1)].bitcast(FP8).rearrange("p (b u r) -> p b u r", u=2, r=RUN),
+                    in0=src[:, G * i : G * (i + 1)].bitcast(FP8).rearrange("p (b u r) -> p b u r", u=2, r=RUN),
                     scalar1=scales[:, t * blocks + i : t * blocks + i + 1],
                     scalar2=None,
                     op0=ALU.mult,
@@ -120,7 +150,7 @@ def tile_archived_docs_feedback_d4_kernel(tc, docs_bytes, docs_scale, queries, n
         def reorder_queries(j, on_scalar):
             tile = keep.tile([P, 2, K // (2 * RUN), RUN], BF16, name="q_wide_%d" % j, align_bytes=64)
             wide[("q", j)] = tile
-            src = q_raw[j // 2][:, j % 2, :].rearrange("p (b u r) -> p u b r", u=2, r=RUN)
+            src = q_raw[j][:].rearrange("p (b u r) -> p u b r", u=2, r=RUN)
             if on_scalar:
                 nc.scalar.copy(out=tile[:], in_=src)
             else:
@@ -135,13 +165,16 @@ def tile_archived_docs_feedback_d4_kernel(tc, docs_bytes, docs_scale, queries, n
                     first = (u * K_PASSES + s) * P
                     nc.tensor.transpose(bank[:, s, u, :], words[:, first : first + P], ident[:])
 
-        def copy_turned(key, dst):
-            nc.scalar.copy(out=dst, in_=banks[key][:].rearrange("p s u d -> p s d u"))
+        def copy_turned(key, dst, on_scalar=True):
+            if on_scalar:
+                nc.scalar.copy(out=dst, in_=banks[key][:].rearrange("p s u d -> p s d u"))
+            else:
+                nc.vector.tensor_copy(out=dst, in_=banks[key][:].rearrange("p s u d -> p s d u"))
 
-        def copy_docs(g, t):
+        def copy_docs(g, t, on_scalar=True):
             if t % 2 == 0:
                 turned[(g, t // 2)] = work.tile([P, 2, K_PASSES, P, 2], F32, name="turned", tag="turned", bufs=4, align_bytes=64)
-            copy_turned((g, t), turned[(g, t // 2)][:, t % 2, :, :, :])
+            copy_turned((g, t), turned[(g, t // 2)][:, t % 2, :, :, :], on_scalar)
 
         def quantize_docs(g, h):
             codes = work.tile([P, 2 * K_PASSES * P], U32, name="doc_codes", tag="doc_codes", bufs=6, align_bytes=64)
@@ -157,15 +190,21 @@ def tile_archived_docs_feedback_d4_kernel(tc, docs_bytes, docs_scale, queries, n
         q_codes = keep.tile([P, K_PASSES, B], U32, name="q_codes", align_bytes=64)
         q_scales = keep.tile([P, K_PASSES, B], U8, name="q_scales", align_bytes=64)
 
-        def quantize_queries(s):
-            nc.vector.quantize_mx(
-                out=q_codes[:, s, :].bitcast(FP8X4),
-                scales=q_scales[:, s, :],
-                in_=q_turned[:, s, :, :].rearrange("p b u -> p (b u)").bitcast(BF16),
-            )
+        def quantize_queries(half):
+            cols = slice(half * HALF, (half + 1) * HALF)
+            for s in range(K_PASSES):
+                nc.vector.quantize_mx(
+                    out=q_codes[:, s, cols].bitcast(FP8X4),
+                    scales=q_scales[:, s, cols],
+                    in_=q_turned[:, s, cols, :].rearrange("p b u -> p (b u)").bitcast(BF16),
+                )
+
+        def copy_queries(j, on_scalar):
+            copy_turned(("q", j), q_turned[:, :, j * P : (j + 1) * P, :], on_scalar)
 
         def scores(g, t, tag):
             bank = psum.tile([P, B], F32, name=tag, tag=tag)
+            banks[("s", g, t)] = bank
             codes, scales = doc_codes[(g, t // 2)]
             for s in range(K_PASSES):
                 first = ((t % 2) * K_PASSES + s) * P
@@ -178,45 +217,49 @@ def tile_archived_docs_feedback_d4_kernel(tc, docs_bytes, docs_scale, queries, n
                     start=(s == 0),
                     stop=(s == K_PASSES - 1),
                 )
+
+        def relevance(g, t, on_scalar=True):
+            bank = banks[("s", g, t)]
             if t == 0:
                 rel_planes[g] = work.tile([P, PACK, B], BF16, name="rel_planes", tag="rel_planes", bufs=3, align_bytes=64)
-            nc.scalar.activation(
-                out=rel_planes[g][:, t, :],
-                in_=bank[:],
-                func=ACT.Relu,
-                scale=inv_norms[:, g * PACK + t : g * PACK + t + 1],
-            )
-
-        def interleave(g, scalar_queries):
-            tile = work.tile([P, B, PACK], BF16, name="rel_packed", tag="rel_packed", bufs=2, align_bytes=64)
-            rel_packed[g] = tile
-            split = B - scalar_queries
-            nc.vector.tensor_copy(
-                out=tile[:, 0:split, :].rearrange("p (c i) t -> p c t i", i=4),
-                in_=rel_planes[g][:, :, 0:split].rearrange("p t (c i) -> p c t i", i=4),
-            )
-            if scalar_queries:
-                nc.scalar.copy(
-                    out=tile[:, split:B, :].rearrange("p (c i) t -> p c t i", i=4),
-                    in_=rel_planes[g][:, :, split:B].rearrange("p t (c i) -> p c t i", i=4),
+            factor = inv_norms[:, g * PACK + t : g * PACK + t + 1]
+            if on_scalar:
+                nc.scalar.activation(out=rel_planes[g][:, t, :], in_=bank[:], func=ACT.Relu, scale=factor)
+            else:
+                nc.vector.tensor_scalar(
+                    out=rel_planes[g][:, t, :], in0=bank[:], scalar1=factor, scalar2=0.0, op0=ALU.mult, op1=ALU.max
                 )
 
-        def quantize_rel(g):
-            codes = keep.tile([P, B], U32, name="rel_codes_%d" % g, align_bytes=64)
-            scales = keep.tile([P, B], U8, name="rel_scales_%d" % g, align_bytes=64)
-            rel_codes[g] = (codes, scales)
+        def interleave(r, lo, hi, on_scalar):
+            if lo == hi:
+                return
+            g, first = r // 2, (r % 2) * HALF
+            if r not in rel_packed:
+                rel_packed[r] = work.tile([P, HALF, PACK], BF16, name="rel_packed", tag="rel_packed", bufs=3, align_bytes=64)
+            dst = rel_packed[r][:, lo:hi, :].rearrange("p (c i) t -> p c t i", i=4)
+            src = rel_planes[g][:, :, first + lo : first + hi].rearrange("p t (c i) -> p c t i", i=4)
+            if on_scalar:
+                nc.scalar.copy(out=dst, in_=src)
+            else:
+                nc.vector.tensor_copy(out=dst, in_=src)
+
+        def quantize_rel(r):
+            codes = keep.tile([P, HALF], U32, name="rel_codes_%d" % r, align_bytes=64)
+            scales = keep.tile([P, HALF], U8, name="rel_scales_%d" % r, align_bytes=64)
+            rel_codes[r] = (codes, scales)
             nc.vector.quantize_mx(
-                out=codes[:].bitcast(FP8X4), scales=scales[:], in_=rel_packed[g][:].rearrange("p b t -> p (b t)")
+                out=codes[:].bitcast(FP8X4), scales=scales[:], in_=rel_packed[r][:].rearrange("p b t -> p (b t)")
             )
 
         def pool_pass(g, j, h, tag):
             if g == 0:
                 sums[(j, h)] = psum.tile([P, N_TILE], F32, name=tag, tag=tag)
-            codes, scales = rel_codes[g]
+            codes, scales = rel_codes[2 * g + j // 2]
+            cols = slice((j % 2) * P, (j % 2 + 1) * P)
             nc.tensor.matmul_mx(
                 out=sums[(j, h)][:],
-                lhsT=codes[:, j * P : (j + 1) * P].bitcast(FP8X4),
-                lhsT_scale=scales[:, j * P : (j + 1) * P],
+                lhsT=codes[:, cols].bitcast(FP8X4),
+                lhsT_scale=scales[:, cols],
                 rhs=v_codes[g][:, 2 * h * N_TILE : 2 * (h + 1) * N_TILE].bitcast(FP4X4),
                 rhs_scale=v_scale[:, g, h * N_TILE : (h + 1) * N_TILE],
                 start=(g == 0),
@@ -231,85 +274,174 @@ def tile_archived_docs_feedback_d4_kernel(tc, docs_bytes, docs_scale, queries, n
                 nc.vector.tensor_copy(out=result[:], in_=sums[(j, h)][:])
             nc.sync.dma_start(out=out[j * P : (j + 1) * P, h * N_TILE : (h + 1) * N_TILE], in_=result[:])
 
-        def rot(t):
-            return "rot%d" % t
+        taken = []
+        free_banks = 8 - SUMS
 
-        def acc(j):
-            return "acc%d" % j
+        def rot():
+            taken.append(0)
+            return "rot%d" % ((len(taken) - 1) % free_banks)
 
-        for h in range(2):
-            for t in (2 * h, 2 * h + 1):
-                widen(0, t)
-                transpose((0, t), rot(t))
-            reorder_queries(2 * h, True)
-            reorder_queries(2 * h + 1, False)
-            copy_docs(0, 2 * h)
-            copy_docs(0, 2 * h + 1)
-            for j in (2 * h, 2 * h + 1):
-                transpose(("q", j), acc(j))
-            for j in (2 * h, 2 * h + 1):
-                copy_turned(("q", j), q_turned[:, :, j * P : (j + 1) * P, :])
-        nc.vector.reciprocal(out=inv_norms[:], in_=norms_f32[:])
-        quantize_docs(0, 0)
-        widen(1, 0)
-        widen(1, 1)
-        quantize_docs(0, 1)
-        widen(1, 2)
-        quantize_queries(0)
-        quantize_queries(1)
-        widen(1, 3)
+        early = [(j, 0) for j in range(Q_TILES)] + [(j, 1) for j in range(SUMS - Q_TILES)]
+        late = [(j, 1) for j in range(SUMS - Q_TILES, Q_TILES)]
 
-        last = GROUPS - 1
-        for c in range(last):
-            for t in range(PACK):
-                transpose((c + 1, t), rot(t))
-            if c + 2 <= last:
-                widen(c + 2, 0)
-                widen(c + 2, 1)
-            for t in range(PACK):
-                copy_docs(c + 1, t)
-            if c >= 1:
-                interleave(c - 1, SCALAR_QUERIES)
-            if c >= 2:
-                for j in range(Q_TILES):
-                    pool_pass(c - 2, j, 0, acc(j))
-            if c + 2 <= last:
-                widen(c + 2, 2)
-                widen(c + 2, 3)
-            if c >= 1:
-                quantize_rel(c - 1)
-            for t in range(PACK):
-                scores(c, t, rot(t))
-            quantize_docs(c + 1, 0)
-            quantize_docs(c + 1, 1)
+        def acc(i):
+            return "acc%d" % i
 
-        interleave(last - 1, 0)
-        for j in range(Q_TILES):
-            pool_pass(last - 2, j, 0, acc(j))
-        scores(last, 0, rot(0))
-        scores(last, 1, rot(1))
-        quantize_rel(last - 1)
-        for g in range(3):
-            pool_pass(g, 2, 1, rot(2))
-        scores(last, 2, rot(0))
-        scores(last, 3, rot(1))
-        interleave(last, 128)
-        quantize_rel(last)
-        for g in range(3, last):
-            pool_pass(g, 2, 1, rot(2))
-        for j in range(Q_TILES):
-            pool_pass(last - 1, j, 0, acc(j))
-        for g in range(3):
-            pool_pass(g, 3, 1, rot(3))
-        for j in range(Q_TILES):
-            pool_pass(last, j, 0, acc(j))
-            store(j, 0, j % 2 == 0)
-        pool_pass(last, 2, 1, rot(2))
-        store(2, 1, True)
-        for g in range(3, GROUPS):
-            pool_pass(g, 3, 1, rot(3))
-        store(3, 1, False)
-        for j in range(2):
+        def tiles(k):
+            return [(k // 2, 2 * (k % 2)), (k // 2, 2 * (k % 2) + 1)]
+
+        def pool_early(r, lo=0, hi=8):
+            for i, (j, h) in [e for e in enumerate(early) if e[1][0] // 2 == r % 2][lo:hi]:
+                pool_pass(r // 2, j, h, acc(i))
+
+        def warm_up(n):
+            for i in range(n):
+                dummy = psum.tile([P, N_TILE], F32, name=acc(SUMS - 1), tag=acc(SUMS - 1))
+                nc.tensor.matmul(out=dummy[:], lhsT=warm[:, 0:P], rhs=warm[:], start=True, stop=True)
+
+        warm_up(WARM)
+        widen(0, 0)
+        transpose((0, 0), rot())
+        reorder_queries(0, True)
+        transpose(("q", 0), acc(0))
+        reorder_queries(1, False)
+        transpose(("q", 1), acc(1))
+        warm_up(2)
+        copy_docs(0, 0)
+        widen(0, 1)
+        transpose((0, 1), rot())
+        copy_queries(0, True)
+        reorder_queries(2, False)
+        transpose(("q", 2), acc(2))
+        copy_queries(1, True)
+        reorder_queries(3, False)
+        transpose(("q", 3), acc(3))
+        warm_up(3)
+        copy_docs(0, 1)
+        if HEAD == 0:
+            widen(0, 2)
+            quantize_queries(0)
+            copy_queries(2, True)
+            copy_queries(3, False)
+            quantize_docs(0, 0)
+            quantize_queries(1)
+            widen(0, 3)
+        if HEAD == 1:
+            copy_queries(2, False)
+            copy_queries(3, True)
+            quantize_queries(0)
+            quantize_docs(0, 0)
+            quantize_queries(1)
+            widen(0, 2)
+            widen(0, 3)
+        if HEAD == 2:
+            widen(0, 2)
+            copy_queries(2, True)
+            copy_queries(3, True)
+            quantize_queries(0)
+            widen(0, 3)
+            quantize_docs(0, 0)
+            quantize_queries(1)
+        nc.vector.reciprocal(out=inv_norms[:], in_=norms_raw[:].rearrange("p g t -> p (g t)"))
+        for k in range(2, WIDEN_LEAD + 1):
+            for g, t in tiles(k):
+                widen(g, t)
+
+        late_tags = {}
+        late_done = [0] * len(late)
+
+        def pool_late(i, upto):
+            if i not in late_tags:
+                if i == 1:
+                    rot()
+                late_tags[i] = rot()
+            for g in range(late_done[i], upto):
+                pool_pass(g, late[i][0], late[i][1], late_tags[i])
+            late_done[i] = max(upto, late_done[i])
+
+        for k in range(STEPS):
+            r = k - 1 - REL_LAG
+            if k == 0 and FIRST:
+                first_tags = [rot(), rot()]
+                for i, (g, t) in enumerate(tiles(k)):
+                    scores(g, t, first_tags[i])
+                    relevance(g, t)
+            if r - POOL_LAG >= 0:
+                pool_early(r - POOL_LAG, 0, PRE)
+            if k + 1 < STEPS:
+                for key in tiles(k + 1):
+                    transpose(key, rot())
+            if k + 1 + WIDEN_LEAD < STEPS:
+                g, t = tiles(k + 1 + WIDEN_LEAD)[0]
+                widen(g, t)
+            split = HALF - (SCALAR_QUERIES if k < S_SHARE_TO else 0)
+            if r >= 0 and SHARE_POS == 1:
+                interleave(r, split, HALF, True)
+            if k + 1 < STEPS:
+                for g, t in tiles(k + 1):
+                    copy_docs(g, t, k + 1 < V_COPY_FROM or t % 2 == 0)
+            if r - 1 >= 0:
+                quantize_rel(r - 1)
+            if Q_EARLY and k + 1 < STEPS:
+                quantize_docs((k + 1) // 2, (k + 1) % 2)
+            if k + 1 + WIDEN_LEAD < STEPS:
+                g, t = tiles(k + 1 + WIDEN_LEAD)[1]
+                widen(g, t)
+            if r >= 0:
+                interleave(r, 0, split, False)
+                if SHARE_POS == 0:
+                    interleave(r, split, HALF, True)
+            if r - POOL_LAG >= 0:
+                pool_early(r - POOL_LAG, PRE)
+            if not Q_EARLY and k + 1 < STEPS:
+                quantize_docs((k + 1) // 2, (k + 1) % 2)
+            if k + 1 == STEPS:
+                pool_late(0, LATE_FIRST)
+            for g, t in tiles(k) if k > 0 or not FIRST else []:
+                scores(g, t, rot())
+                relevance(g, t, k < V_REL_FROM or t % 2 == 0)
+
+        r0 = STEPS - 1 - REL_LAG
+        quantize_rel(r0 - 1)
+        for r in range(r0, STEPS):
+            interleave(r, 0, HALF - TAIL_SHARE, False)
+            interleave(r, HALF - TAIL_SHARE, HALF, True)
+            if r > r0:
+                quantize_rel(r - 1)
+        quantize_rel(STEPS - 1)
+        for r in range(r0 - POOL_LAG, STEPS - 2):
+            pool_early(r)
+        n = 0
+        for r, upto in ((STEPS - 2, LATE_SECOND), (STEPS - 1, LATE_THIRD)):
+            pool_late(0, upto)
+            for i, (j, h) in enumerate(early):
+                if j // 2 == r % 2:
+                    pool_pass(r // 2, j, h, acc(i))
+                    store(j, h, n % 2 == 0)
+                    n += 1
+        for i, (j, h) in enumerate(late[:-1]):
+            pool_late(i, GROUPS)
+            store(j, h, n % 2 == 0)
+            n += 1
+        j, h = late[-1]
+        for piece in range(N_TILE // P):
+            first = h * N_TILE + piece * P
+            bank = psum.tile([P, P], F32, name=acc(piece), tag=acc(piece))
             for g in range(GROUPS):
-                pool_pass(g, j, 1, rot(j))
-            store(j, 1, j % 2 == 0)
+                codes, scales = rel_codes[2 * g + j // 2]
+                cols = slice((j % 2) * P, (j % 2 + 1) * P)
+                nc.tensor.matmul_mx(
+                    out=bank[:],
+                    lhsT=codes[:, cols].bitcast(FP8X4),
+                    lhsT_scale=scales[:, cols],
+                    rhs=v_codes[g][:, 2 * first : 2 * (first + P)].bitcast(FP4X4),
+                    rhs_scale=v_scale[:, g, first : first + P],
+                    start=(g == 0),
+                    stop=(g == GROUPS - 1),
+                )
+            result = work.tile([P, P], F32, name="piece", tag="piece", bufs=4)
+            if piece % 2 == 0:
+                nc.scalar.copy(out=result[:], in_=bank[:])
+            else:
+                nc.vector.tensor_copy(out=result[:], in_=bank[:])
+            nc.sync.dma_start(out=out[j * P : (j + 1) * P, first : first + P], in_=result[:])

@@ -28,16 +28,21 @@ RUN = 16
 STEPS = 2 * GROUPS
 HALF = B // 2
 SUMS = 5
-SCALAR_QUERIES = 48
+SCALAR_QUERIES = 80
 WIDEN_LEAD = 1
-WARM = 7
+WARM = 6
 V_COPY_FROM = 16
-V_REL_FROM = 16
+V_REL_FROM = 13
 S_SHARE_TO = 13
 REL_LAG = 1
 POOL_LAG = 2
-HEAD = 2
-PRE = 1
+HEAD = 1
+PATTERN = 0
+PRE = 2
+LOADS = 1
+BUDGET = 4
+WARM2 = 0
+WARM3 = 0
 SHARE_POS = 0
 FIRST = 0
 Q_EARLY = 0
@@ -100,11 +105,25 @@ def tile_archived_docs_feedback_d4_kernel(tc, docs_bytes, docs_scale, queries, n
         load_scales(0, 1)
         load_docs(0, 0, 1)
         load_queries(0)
-        load_queries(1)
-        load_docs(0, 1, 1)
-        load_queries(2)
-        load_queries(3)
-        load_docs(0, 2, 2)
+        if LOADS == 0:
+            load_queries(1)
+            load_docs(0, 1, 1)
+            load_queries(2)
+            load_queries(3)
+            load_docs(0, 2, 2)
+        if LOADS == 1:
+            load_docs(0, 1, 1)
+            load_queries(1)
+            load_docs(0, 2, 1)
+            load_queries(2)
+            load_queries(3)
+            load_docs(0, 3, 1)
+        if LOADS == 2:
+            load_docs(0, 1, 1)
+            load_queries(1)
+            load_docs(0, 2, 2)
+            load_queries(2)
+            load_queries(3)
         load_scales(1, 2)
         load_docs(1, 0, 2)
         nc.sync.dma_start(out=norms_raw[:], in_=norms.rearrange("(g m t) -> m g t", m=P, t=PACK))
@@ -172,18 +191,35 @@ def tile_archived_docs_feedback_d4_kernel(tc, docs_bytes, docs_scale, queries, n
                 nc.vector.tensor_copy(out=dst, in_=banks[key][:].rearrange("p s u d -> p s d u"))
 
         def copy_docs(g, t, on_scalar=True):
-            if t % 2 == 0:
-                turned[(g, t // 2)] = work.tile([P, 2, K_PASSES, P, 2], F32, name="turned", tag="turned", bufs=4, align_bytes=64)
-            copy_turned((g, t), turned[(g, t // 2)][:, t % 2, :, :, :], on_scalar)
+            turned[(g, t)] = work.tile([P, K_PASSES, P, 2], F32, name="turned", tag="turned", bufs=6, align_bytes=64)
+            copy_turned((g, t), turned[(g, t)][:], on_scalar)
 
-        def quantize_docs(g, h):
-            codes = work.tile([P, 2 * K_PASSES * P], U32, name="doc_codes", tag="doc_codes", bufs=6, align_bytes=64)
-            scales = work.tile([P, 2 * K_PASSES * P], U8, name="doc_scales", tag="doc_scales", bufs=6, align_bytes=64)
-            doc_codes[(g, h)] = (codes, scales)
+        def copy_pair(keys):
+            pair = work.tile([P, 2, K_PASSES, P, 2], F32, name="turned2", tag="turned2", bufs=3, align_bytes=64)
+            for i, key in enumerate(keys):
+                turned[key] = pair
+                copy_turned(key, pair[:, i, :, :, :])
+
+        def quantize_pair(keys):
+            codes = work.tile([P, 2 * K_PASSES * P], U32, name="doc_codes2", tag="doc_codes2", bufs=3, align_bytes=64)
+            scales = work.tile([P, 2 * K_PASSES * P], U8, name="doc_scales2", tag="doc_scales2", bufs=3, align_bytes=64)
+            for i, key in enumerate(keys):
+                cols = slice(i * K_PASSES * P, (i + 1) * K_PASSES * P)
+                doc_codes[key] = (codes[:, cols], scales[:, cols])
             nc.vector.quantize_mx(
                 out=codes[:].bitcast(FP8X4),
                 scales=scales[:],
-                in_=turned[(g, h)][:].rearrange("p t s d u -> p (t s d u)").bitcast(BF16),
+                in_=turned[keys[0]][:].rearrange("p t s d u -> p (t s d u)").bitcast(BF16),
+            )
+
+        def quantize_docs(g, t):
+            codes = work.tile([P, K_PASSES * P], U32, name="doc_codes", tag="doc_codes", bufs=4, align_bytes=64)
+            scales = work.tile([P, K_PASSES * P], U8, name="doc_scales", tag="doc_scales", bufs=4, align_bytes=64)
+            doc_codes[(g, t)] = (codes[:], scales[:])
+            nc.vector.quantize_mx(
+                out=codes[:].bitcast(FP8X4),
+                scales=scales[:],
+                in_=turned[(g, t)][:].rearrange("p s d u -> p (s d u)").bitcast(BF16),
             )
 
         q_turned = keep.tile([P, K_PASSES, B, 2], F32, name="q_turned", align_bytes=64)
@@ -205,9 +241,9 @@ def tile_archived_docs_feedback_d4_kernel(tc, docs_bytes, docs_scale, queries, n
         def scores(g, t, tag):
             bank = psum.tile([P, B], F32, name=tag, tag=tag)
             banks[("s", g, t)] = bank
-            codes, scales = doc_codes[(g, t // 2)]
+            codes, scales = doc_codes[(g, t)]
             for s in range(K_PASSES):
-                first = ((t % 2) * K_PASSES + s) * P
+                first = s * P
                 nc.tensor.matmul_mx(
                     out=bank[:],
                     lhsT=codes[:, first : first + P].bitcast(FP8X4),
@@ -304,113 +340,111 @@ def tile_archived_docs_feedback_d4_kernel(tc, docs_bytes, docs_scale, queries, n
         transpose((0, 0), rot())
         reorder_queries(0, True)
         transpose(("q", 0), acc(0))
-        reorder_queries(1, False)
-        transpose(("q", 1), acc(1))
-        warm_up(2)
-        copy_docs(0, 0)
         widen(0, 1)
         transpose((0, 1), rot())
+        copy_docs(0, 0)
+        reorder_queries(1, HEAD == 3)
+        transpose(("q", 1), acc(1))
         copy_queries(0, True)
+        widen(0, 2)
+        copy_docs(0, 1)
+        if LOADS == 2:
+            widen(0, 3)
         reorder_queries(2, False)
         transpose(("q", 2), acc(2))
         copy_queries(1, True)
+        if HEAD == 1:
+            quantize_docs(0, 0)
         reorder_queries(3, False)
         transpose(("q", 3), acc(3))
-        warm_up(3)
-        copy_docs(0, 1)
-        if HEAD == 0:
-            widen(0, 2)
-            quantize_queries(0)
-            copy_queries(2, True)
-            copy_queries(3, False)
-            quantize_docs(0, 0)
-            quantize_queries(1)
+        warm_up(WARM3)
+        copy_queries(2, True)
+        copy_queries(3, True)
+        if LOADS != 2:
             widen(0, 3)
-        if HEAD == 1:
-            copy_queries(2, False)
-            copy_queries(3, True)
-            quantize_queries(0)
+        if HEAD != 1:
             quantize_docs(0, 0)
-            quantize_queries(1)
-            widen(0, 2)
-            widen(0, 3)
-        if HEAD == 2:
-            widen(0, 2)
-            copy_queries(2, True)
-            copy_queries(3, True)
-            quantize_queries(0)
-            widen(0, 3)
-            quantize_docs(0, 0)
-            quantize_queries(1)
+        quantize_queries(0)
+        if PATTERN == 0:
+            widen(1, 0)
+        quantize_queries(1)
+        quantize_docs(0, 1)
         nc.vector.reciprocal(out=inv_norms[:], in_=norms_raw[:].rearrange("p g t -> p (g t)"))
-        for k in range(2, WIDEN_LEAD + 1):
-            for g, t in tiles(k):
-                widen(g, t)
 
         late_tags = {}
         late_done = [0] * len(late)
 
         def pool_late(i, upto):
-            if i not in late_tags:
-                if i == 1:
-                    rot()
-                late_tags[i] = rot()
             for g in range(late_done[i], upto):
                 pool_pass(g, late[i][0], late[i][1], late_tags[i])
             late_done[i] = max(upto, late_done[i])
 
-        for k in range(STEPS):
-            r = k - 1 - REL_LAG
-            if k == 0 and FIRST:
-                first_tags = [rot(), rot()]
-                for i, (g, t) in enumerate(tiles(k)):
-                    scores(g, t, first_tags[i])
-                    relevance(g, t)
-            if r - POOL_LAG >= 0:
-                pool_early(r - POOL_LAG, 0, PRE)
-            if k + 1 < STEPS:
-                for key in tiles(k + 1):
-                    transpose(key, rot())
-            if k + 1 + WIDEN_LEAD < STEPS:
-                g, t = tiles(k + 1 + WIDEN_LEAD)[0]
-                widen(g, t)
-            split = HALF - (SCALAR_QUERIES if k < S_SHARE_TO else 0)
-            if r >= 0 and SHARE_POS == 1:
-                interleave(r, split, HALF, True)
-            if k + 1 < STEPS:
-                for g, t in tiles(k + 1):
-                    copy_docs(g, t, k + 1 < V_COPY_FROM or t % 2 == 0)
-            if r - 1 >= 0:
-                quantize_rel(r - 1)
-            if Q_EARLY and k + 1 < STEPS:
-                quantize_docs((k + 1) // 2, (k + 1) % 2)
-            if k + 1 + WIDEN_LEAD < STEPS:
-                g, t = tiles(k + 1 + WIDEN_LEAD)[1]
-                widen(g, t)
-            if r >= 0:
-                interleave(r, 0, split, False)
-                if SHARE_POS == 0:
-                    interleave(r, split, HALF, True)
-            if r - POOL_LAG >= 0:
-                pool_early(r - POOL_LAG, PRE)
-            if not Q_EARLY and k + 1 < STEPS:
-                quantize_docs((k + 1) // 2, (k + 1) % 2)
-            if k + 1 == STEPS:
-                pool_late(0, LATE_FIRST)
-            for g, t in tiles(k) if k > 0 or not FIRST else []:
-                scores(g, t, rot())
-                relevance(g, t, k < V_REL_FROM or t % 2 == 0)
+        keys = [(n // PACK, n % PACK) for n in range(GROUPS * PACK)]
+        sizes = [[2] + [3] * 10, [2, 2] + [3] * 8 + [2, 2], [2, 2, 2] + [3] * 8 + [2], [2, 2, 2, 2] + [3] * 8][PATTERN]
+        runs = [keys[sum(sizes[0:i]) : sum(sizes[0 : i + 1])] for i in range(len(sizes))]
+        passes = [(r // 2, j, h, acc(i)) for r in range(STEPS) for i, (j, h) in enumerate(early) if j // 2 == r % 2]
+        packed = 0
+        quantized = 0
+        pooled = 0
+        scored = 0
+        for k in range(len(runs)):
+            turn = runs[k + 1] if k + 1 < len(runs) else []
+            ahead = runs[k + 2] if k + 2 < len(runs) else []
+            ready = len([1 for g, j, h, tag in passes if 2 * g + j // 2 < quantized])
+            can_pack = 2 * (scored // PACK)
+            upto = min(ready, pooled + BUDGET)
+            pre = min(upto, pooled + PRE)
+            for g, j, h, tag in passes[pooled:pre]:
+                pool_pass(g, j, h, tag)
+            for key in turn:
+                transpose(key, rot())
+            if ahead:
+                widen(*ahead[0])
+            if turn:
+                copy_pair(turn[0:2])
+            if len(turn) == 3:
+                copy_docs(*turn[2])
+            share = SCALAR_QUERIES if k < S_SHARE_TO else 0
+            if quantized < packed:
+                quantize_rel(quantized)
+                quantized += 1
+            todo = list(range(packed, min(can_pack, packed + 2)))
+            if todo:
+                interleave(todo[0], 0, HALF, False)
+            if ahead:
+                widen(*ahead[1])
+            if len(todo) == 2:
+                quantize_rel(todo[0])
+                quantized += 1
+                interleave(todo[1], 0, HALF - share, False)
+                interleave(todo[1], HALF - share, HALF, True)
+            packed += len(todo)
+            if len(ahead) == 3:
+                widen(*ahead[2])
+            for g, j, h, tag in passes[pre:upto]:
+                pool_pass(g, j, h, tag)
+            pooled = upto
+            if turn:
+                quantize_pair(turn[0:2])
+            if len(turn) == 3:
+                quantize_docs(*turn[2])
+            for g, t in runs[k]:
+                tag = rot()
+                scores(g, t, tag)
+                relevance(g, t, k < V_REL_FROM or t % 2 == 1)
+            scored += len(runs[k])
 
-        r0 = STEPS - 1 - REL_LAG
-        quantize_rel(r0 - 1)
-        for r in range(r0, STEPS):
+        late_tags.update({0: rot(), 1: rot()})
+        for r in range(quantized, packed):
+            quantize_rel(r)
+        for r in range(packed, STEPS):
             interleave(r, 0, HALF - TAIL_SHARE, False)
             interleave(r, HALF - TAIL_SHARE, HALF, True)
-            if r > r0:
-                quantize_rel(r - 1)
-        quantize_rel(STEPS - 1)
-        for r in range(r0 - POOL_LAG, STEPS - 2):
-            pool_early(r)
+        for r in range(packed, STEPS):
+            quantize_rel(r)
+        for g, j, h, tag in passes[pooled:]:
+            if g < GROUPS - 1:
+                pool_pass(g, j, h, tag)
         n = 0
         for r, upto in ((STEPS - 2, LATE_SECOND), (STEPS - 1, LATE_THIRD)):
             pool_late(0, upto)

@@ -22,34 +22,21 @@ PACK = 4
 PASS = P * PACK
 GROUPS = T // PASS
 K_PASSES = K // PASS
+SCALE_BLOCKS = K // G
+RUN = 16
 Q_TILES = B // P
 N_TILE = 512
-RUN = 16
-STEPS = 2 * GROUPS
 HALF = B // 2
-SUMS = 5
+HALVES = 2 * GROUPS
+
+EARLY_SUMS = 5
+TURN_BANKS = 8 - EARLY_SUMS
+STEP_TILES = TURN_BANKS
+STEP_PASSES = 4
+PASSES_BEFORE_RUN = 2
 SCALAR_QUERIES = 80
-WIDEN_LEAD = 1
-WARM = 6
-V_COPY_FROM = 16
-V_REL_FROM = 13
-S_SHARE_TO = 13
-REL_LAG = 1
-POOL_LAG = 2
-HEAD = 1
-PATTERN = 0
-PRE = 2
-LOADS = 1
-BUDGET = 4
-WARM2 = 0
-WARM3 = 0
-SHARE_POS = 0
-FIRST = 0
-Q_EARLY = 0
-LATE_FIRST = 1
-LATE_SECOND = 6
-LATE_THIRD = 6
-TAIL_SHARE = 96
+SCALAR_QUERIES_LAST = 96
+LATE_PASSES_FIRST = 6
 
 
 def tile_archived_docs_feedback_d4_kernel(tc, docs_bytes, docs_scale, queries, norms, v_words, v_scales, out):
@@ -60,70 +47,53 @@ def tile_archived_docs_feedback_d4_kernel(tc, docs_bytes, docs_scale, queries, n
         psum = ctx.enter_context(tc.psum_pool(name="psum", bufs=1))
         ctx.enter_context(tc.manual_schedule())
 
-        docs_rows = docs_bytes.rearrange("(g m t) k -> g m t k", m=P, t=PACK)
-        scale_rows = docs_scale.rearrange("(g m t) i -> m g (t i)", m=P, t=PACK)
-        blocks = K // G
-
         ident_raw = keep.tile([P, P], F32, name="ident_raw")
         make_identity(nc, ident_raw[:])
         ident = keep.tile([P, P], F32, name="ident")
         nc.scalar.activation(out=ident[:], in_=ident_raw[:], func=ACT.Relu)
-        warm = keep.tile([P, N_TILE], BF16, name="warm")
-        nc.vector.memset(warm[:], 0.0)
+
         v_scale = keep.tile([P, GROUPS, N], U8, name="v_scale", align_bytes=64)
         nc.vector.memset(v_scale[:].rearrange("p g n -> p (g n)").bitcast(I32), 0)
 
+        docs_rows = docs_bytes.rearrange("(g m t) k -> g m t k", m=P, t=PACK)
+        scale_rows = docs_scale.rearrange("(g m t) i -> m g (t i)", m=P, t=PACK)
         doc_bytes = {}
-        v_codes = {}
+        doc_scale = {}
         q_raw = {}
+        v_codes = {}
 
-        def load_docs(g, t0, n):
-            tile = keep.tile([P, n, K], U8, name="doc_bytes_%d_%d" % (g, t0), align_bytes=64)
-            nc.sync.dma_start(out=tile[:], in_=docs_rows[g, :, t0 : t0 + n, :])
-            for i in range(n):
+        def load_docs(g, t0, count):
+            tile = keep.tile([P, count, K], U8, name="doc_bytes_%d_%d" % (g, t0), align_bytes=64)
+            nc.sync.dma_start(out=tile[:], in_=docs_rows[g, :, t0 : t0 + count, :])
+            for i in range(count):
                 doc_bytes[(g, t0 + i)] = tile[:, i, :]
 
-        def load_v(g):
-            tile = keep.tile([P, 2 * N], U8, name="v_codes_%d" % g, align_bytes=64)
-            nc.sync.dma_start(out=tile[:].bitcast(I32), in_=v_words[g].bitcast(I32))
-            v_codes[g] = tile
+        def load_scales(g0, g1):
+            tile = keep.tile([P, g1 - g0, PACK * SCALE_BLOCKS], F32, name="doc_scale_%d" % g0)
+            nc.sync.dma_start(out=tile[:], in_=scale_rows[:, g0:g1, :])
+            for g in range(g0, g1):
+                doc_scale[g] = tile[:, g - g0, :]
 
         def load_queries(j):
             tile = keep.tile([P, K], BF16, name="q_raw_%d" % j, align_bytes=64)
             nc.sync.dma_start(out=tile[:], in_=queries[j * P : (j + 1) * P, :])
             q_raw[j] = tile
 
-        doc_scale = {}
-
-        def load_scales(g0, g1):
-            tile = keep.tile([P, g1 - g0, PACK * blocks], F32, name="doc_scale_%d" % g0)
-            nc.sync.dma_start(out=tile[:], in_=scale_rows[:, g0:g1, :])
-            for g in range(g0, g1):
-                doc_scale[g] = tile[:, g - g0, :]
+        def load_v(g):
+            tile = keep.tile([P, 2 * N], U8, name="v_codes_%d" % g, align_bytes=64)
+            nc.sync.dma_start(out=tile[:].bitcast(I32), in_=v_words[g].bitcast(I32))
+            v_codes[g] = tile
 
         norms_raw = keep.tile([P, GROUPS, PACK], BF16, name="norms_raw")
         load_scales(0, 1)
         load_docs(0, 0, 1)
         load_queries(0)
-        if LOADS == 0:
-            load_queries(1)
-            load_docs(0, 1, 1)
-            load_queries(2)
-            load_queries(3)
-            load_docs(0, 2, 2)
-        if LOADS == 1:
-            load_docs(0, 1, 1)
-            load_queries(1)
-            load_docs(0, 2, 1)
-            load_queries(2)
-            load_queries(3)
-            load_docs(0, 3, 1)
-        if LOADS == 2:
-            load_docs(0, 1, 1)
-            load_queries(1)
-            load_docs(0, 2, 2)
-            load_queries(2)
-            load_queries(3)
+        load_docs(0, 1, 1)
+        load_queries(1)
+        load_docs(0, 2, 1)
+        load_queries(2)
+        load_queries(3)
+        load_docs(0, 3, 1)
         load_scales(1, 2)
         load_docs(1, 0, 2)
         nc.sync.dma_start(out=norms_raw[:], in_=norms.rearrange("(g m t) -> m g t", m=P, t=PACK))
@@ -141,11 +111,15 @@ def tile_archived_docs_feedback_d4_kernel(tc, docs_bytes, docs_scale, queries, n
                 load_docs(g + 3, 0, PACK)
 
         inv_norms = keep.tile([P, GROUPS * PACK], F32, name="inv_norms")
+        q_turned = keep.tile([P, K_PASSES, B, 2], F32, name="q_turned", align_bytes=64)
+        q_codes = keep.tile([P, K_PASSES, B], U32, name="q_codes", align_bytes=64)
+        q_scales = keep.tile([P, K_PASSES, B], U8, name="q_scales", align_bytes=64)
 
-        wide = {}
+        reordered = {}
+        turn_bank = {}
         turned = {}
-        banks = {}
         doc_codes = {}
+        score_bank = {}
         rel_planes = {}
         rel_packed = {}
         rel_codes = {}
@@ -153,78 +127,59 @@ def tile_archived_docs_feedback_d4_kernel(tc, docs_bytes, docs_scale, queries, n
 
         def widen(g, t):
             tile = work.tile([P, 2, K // (2 * RUN), RUN], BF16, name="wide", tag="wide", bufs=8, align_bytes=64)
-            wide[(g, t)] = tile
-            src = doc_bytes[(g, t)]
-            scales = doc_scale[g]
+            reordered[(g, t)] = tile
             per = G // (2 * RUN)
-            for i in range(blocks):
+            for i in range(SCALE_BLOCKS):
+                col = t * SCALE_BLOCKS + i
                 nc.vector.tensor_scalar(
                     out=tile[:, :, per * i : per * (i + 1), :].rearrange("p u b r -> p b u r"),
-                    in0=src[:, G * i : G * (i + 1)].bitcast(FP8).rearrange("p (b u r) -> p b u r", u=2, r=RUN),
-                    scalar1=scales[:, t * blocks + i : t * blocks + i + 1],
+                    in0=doc_bytes[(g, t)][:, G * i : G * (i + 1)].bitcast(FP8).rearrange("p (b u r) -> p b u r", u=2, r=RUN),
+                    scalar1=doc_scale[g][:, col : col + 1],
                     scalar2=None,
                     op0=ALU.mult,
                 )
 
-        def reorder_queries(j, on_scalar):
+        def reorder_queries(j, copy):
             tile = keep.tile([P, 2, K // (2 * RUN), RUN], BF16, name="q_wide_%d" % j, align_bytes=64)
-            wide[("q", j)] = tile
-            src = q_raw[j][:].rearrange("p (b u r) -> p u b r", u=2, r=RUN)
-            if on_scalar:
-                nc.scalar.copy(out=tile[:], in_=src)
-            else:
-                nc.vector.tensor_copy(out=tile[:], in_=src)
+            reordered[("q", j)] = tile
+            copy(out=tile[:], in_=q_raw[j][:].rearrange("p (b u r) -> p u b r", u=2, r=RUN))
 
         def transpose(key, tag):
             bank = psum.tile([P, K_PASSES, 2, P], F32, name=tag, tag=tag)
-            banks[key] = bank
-            words = wide[key][:].rearrange("p u b r -> p (u b r)").bitcast(F32)
+            turn_bank[key] = bank
+            words = reordered[key][:].rearrange("p u b r -> p (u b r)").bitcast(F32)
             for s in range(K_PASSES):
                 for u in range(2):
                     first = (u * K_PASSES + s) * P
                     nc.tensor.transpose(bank[:, s, u, :], words[:, first : first + P], ident[:])
 
-        def copy_turned(key, dst, on_scalar=True):
-            if on_scalar:
-                nc.scalar.copy(out=dst, in_=banks[key][:].rearrange("p s u d -> p s d u"))
-            else:
-                nc.vector.tensor_copy(out=dst, in_=banks[key][:].rearrange("p s u d -> p s d u"))
+        def copy_turned(key, dst):
+            nc.scalar.copy(out=dst, in_=turn_bank[key][:].rearrange("p s u d -> p s d u"))
 
-        def copy_docs(g, t, on_scalar=True):
-            turned[(g, t)] = work.tile([P, K_PASSES, P, 2], F32, name="turned", tag="turned", bufs=6, align_bytes=64)
-            copy_turned((g, t), turned[(g, t)][:], on_scalar)
-
-        def copy_pair(keys):
-            pair = work.tile([P, 2, K_PASSES, P, 2], F32, name="turned2", tag="turned2", bufs=3, align_bytes=64)
+        def copy_docs(keys):
+            tag = "turned%d" % len(keys)
+            tile = work.tile([P, len(keys), K_PASSES, P, 2], F32, name=tag, tag=tag, bufs=6 // len(keys), align_bytes=64)
             for i, key in enumerate(keys):
-                turned[key] = pair
-                copy_turned(key, pair[:, i, :, :, :])
+                turned[key] = tile
+                copy_turned(key, tile[:, i, :, :, :])
 
-        def quantize_pair(keys):
-            codes = work.tile([P, 2 * K_PASSES * P], U32, name="doc_codes2", tag="doc_codes2", bufs=3, align_bytes=64)
-            scales = work.tile([P, 2 * K_PASSES * P], U8, name="doc_scales2", tag="doc_scales2", bufs=3, align_bytes=64)
+        def quantize_docs(keys):
+            width = K_PASSES * P
+            depth = 5 - len(keys)
+            tag = "doc_codes%d" % len(keys)
+            codes = work.tile([P, len(keys) * width], U32, name=tag, tag=tag, bufs=depth, align_bytes=64)
+            tag = "doc_scales%d" % len(keys)
+            scales = work.tile([P, len(keys) * width], U8, name=tag, tag=tag, bufs=depth, align_bytes=64)
             for i, key in enumerate(keys):
-                cols = slice(i * K_PASSES * P, (i + 1) * K_PASSES * P)
-                doc_codes[key] = (codes[:, cols], scales[:, cols])
+                doc_codes[key] = (codes[:, i * width : (i + 1) * width], scales[:, i * width : (i + 1) * width])
             nc.vector.quantize_mx(
                 out=codes[:].bitcast(FP8X4),
                 scales=scales[:],
                 in_=turned[keys[0]][:].rearrange("p t s d u -> p (t s d u)").bitcast(BF16),
             )
 
-        def quantize_docs(g, t):
-            codes = work.tile([P, K_PASSES * P], U32, name="doc_codes", tag="doc_codes", bufs=4, align_bytes=64)
-            scales = work.tile([P, K_PASSES * P], U8, name="doc_scales", tag="doc_scales", bufs=4, align_bytes=64)
-            doc_codes[(g, t)] = (codes[:], scales[:])
-            nc.vector.quantize_mx(
-                out=codes[:].bitcast(FP8X4),
-                scales=scales[:],
-                in_=turned[(g, t)][:].rearrange("p s d u -> p (s d u)").bitcast(BF16),
-            )
-
-        q_turned = keep.tile([P, K_PASSES, B, 2], F32, name="q_turned", align_bytes=64)
-        q_codes = keep.tile([P, K_PASSES, B], U32, name="q_codes", align_bytes=64)
-        q_scales = keep.tile([P, K_PASSES, B], U8, name="q_scales", align_bytes=64)
+        def copy_queries(j):
+            copy_turned(("q", j), q_turned[:, :, j * P : (j + 1) * P, :])
 
         def quantize_queries(half):
             cols = slice(half * HALF, (half + 1) * HALF)
@@ -235,49 +190,40 @@ def tile_archived_docs_feedback_d4_kernel(tc, docs_bytes, docs_scale, queries, n
                     in_=q_turned[:, s, cols, :].rearrange("p b u -> p (b u)").bitcast(BF16),
                 )
 
-        def copy_queries(j, on_scalar):
-            copy_turned(("q", j), q_turned[:, :, j * P : (j + 1) * P, :], on_scalar)
-
         def scores(g, t, tag):
             bank = psum.tile([P, B], F32, name=tag, tag=tag)
-            banks[("s", g, t)] = bank
+            score_bank[(g, t)] = bank
             codes, scales = doc_codes[(g, t)]
             for s in range(K_PASSES):
-                first = s * P
                 nc.tensor.matmul_mx(
                     out=bank[:],
-                    lhsT=codes[:, first : first + P].bitcast(FP8X4),
-                    lhsT_scale=scales[:, first : first + P],
+                    lhsT=codes[:, s * P : (s + 1) * P].bitcast(FP8X4),
+                    lhsT_scale=scales[:, s * P : (s + 1) * P],
                     rhs=q_codes[:, s, :].bitcast(FP8X4),
                     rhs_scale=q_scales[:, s, :],
                     start=(s == 0),
                     stop=(s == K_PASSES - 1),
                 )
 
-        def relevance(g, t, on_scalar=True):
-            bank = banks[("s", g, t)]
+        def relevance(g, t):
             if t == 0:
                 rel_planes[g] = work.tile([P, PACK, B], BF16, name="rel_planes", tag="rel_planes", bufs=3, align_bytes=64)
-            factor = inv_norms[:, g * PACK + t : g * PACK + t + 1]
-            if on_scalar:
-                nc.scalar.activation(out=rel_planes[g][:, t, :], in_=bank[:], func=ACT.Relu, scale=factor)
-            else:
-                nc.vector.tensor_scalar(
-                    out=rel_planes[g][:, t, :], in0=bank[:], scalar1=factor, scalar2=0.0, op0=ALU.mult, op1=ALU.max
-                )
+            col = g * PACK + t
+            nc.scalar.activation(
+                out=rel_planes[g][:, t, :], in_=score_bank[(g, t)][:], func=ACT.Relu, scale=inv_norms[:, col : col + 1]
+            )
 
-        def interleave(r, lo, hi, on_scalar):
-            if lo == hi:
-                return
+        def interleave(r, scalar_queries):
             g, first = r // 2, (r % 2) * HALF
-            if r not in rel_packed:
-                rel_packed[r] = work.tile([P, HALF, PACK], BF16, name="rel_packed", tag="rel_packed", bufs=3, align_bytes=64)
-            dst = rel_packed[r][:, lo:hi, :].rearrange("p (c i) t -> p c t i", i=4)
-            src = rel_planes[g][:, :, first + lo : first + hi].rearrange("p t (c i) -> p c t i", i=4)
-            if on_scalar:
-                nc.scalar.copy(out=dst, in_=src)
-            else:
-                nc.vector.tensor_copy(out=dst, in_=src)
+            tile = work.tile([P, HALF, PACK], BF16, name="rel_packed", tag="rel_packed", bufs=3, align_bytes=64)
+            rel_packed[r] = tile
+            split = HALF - scalar_queries
+            shares = [(nc.vector.tensor_copy, 0, split), (nc.scalar.copy, split, HALF)]
+            for copy, lo, hi in [share for share in shares if share[1] < share[2]]:
+                copy(
+                    out=tile[:, lo:hi, :].rearrange("p (c i) t -> p c t i", i=4),
+                    in_=rel_planes[g][:, :, first + lo : first + hi].rearrange("p t (c i) -> p c t i", i=4),
+                )
 
         def quantize_rel(r):
             codes = keep.tile([P, HALF], U32, name="rel_codes_%d" % r, align_bytes=64)
@@ -287,195 +233,147 @@ def tile_archived_docs_feedback_d4_kernel(tc, docs_bytes, docs_scale, queries, n
                 out=codes[:].bitcast(FP8X4), scales=scales[:], in_=rel_packed[r][:].rearrange("p b t -> p (b t)")
             )
 
-        def pool_pass(g, j, h, tag):
+        def pool_pass(g, j, first, width, tag):
             if g == 0:
-                sums[(j, h)] = psum.tile([P, N_TILE], F32, name=tag, tag=tag)
+                sums[(j, first)] = psum.tile([P, width], F32, name=tag, tag=tag)
             codes, scales = rel_codes[2 * g + j // 2]
             cols = slice((j % 2) * P, (j % 2 + 1) * P)
             nc.tensor.matmul_mx(
-                out=sums[(j, h)][:],
+                out=sums[(j, first)][:],
                 lhsT=codes[:, cols].bitcast(FP8X4),
                 lhsT_scale=scales[:, cols],
-                rhs=v_codes[g][:, 2 * h * N_TILE : 2 * (h + 1) * N_TILE].bitcast(FP4X4),
-                rhs_scale=v_scale[:, g, h * N_TILE : (h + 1) * N_TILE],
+                rhs=v_codes[g][:, 2 * first : 2 * (first + width)].bitcast(FP4X4),
+                rhs_scale=v_scale[:, g, first : first + width],
                 start=(g == 0),
                 stop=(g == GROUPS - 1),
             )
 
-        def store(j, h, on_scalar):
-            result = work.tile([P, N_TILE], F32, name="result", tag="result", bufs=8)
-            if on_scalar:
-                nc.scalar.copy(out=result[:], in_=sums[(j, h)][:])
-            else:
-                nc.vector.tensor_copy(out=result[:], in_=sums[(j, h)][:])
-            nc.sync.dma_start(out=out[j * P : (j + 1) * P, h * N_TILE : (h + 1) * N_TILE], in_=result[:])
+        stored = []
+
+        def store(j, first, width):
+            tag = "result%d" % width
+            result = work.tile([P, width], F32, name=tag, tag=tag, bufs=8 if width == N_TILE else 4)
+            copy = nc.scalar.copy if len([1 for w in stored if w == width]) % 2 == 0 else nc.vector.tensor_copy
+            stored.append(width)
+            copy(out=result[:], in_=sums[(j, first)][:])
+            nc.sync.dma_start(out=out[j * P : (j + 1) * P, first : first + width], in_=result[:])
 
         taken = []
-        free_banks = 8 - SUMS
 
-        def rot():
-            taken.append(0)
-            return "rot%d" % ((len(taken) - 1) % free_banks)
+        def next_bank():
+            taken.append(len(taken) % TURN_BANKS)
+            return "rot%d" % taken[-1]
 
-        early = [(j, 0) for j in range(Q_TILES)] + [(j, 1) for j in range(SUMS - Q_TILES)]
-        late = [(j, 1) for j in range(SUMS - Q_TILES, Q_TILES)]
-
-        def acc(i):
+        def sum_bank(i):
             return "acc%d" % i
 
-        def tiles(k):
-            return [(k // 2, 2 * (k % 2)), (k // 2, 2 * (k % 2) + 1)]
+        all_sums = [(j, first) for first in range(0, N, N_TILE) for j in range(Q_TILES)]
+        early, late = all_sums[:EARLY_SUMS], all_sums[EARLY_SUMS:]
 
-        def pool_early(r, lo=0, hi=8):
-            for i, (j, h) in [e for e in enumerate(early) if e[1][0] // 2 == r % 2][lo:hi]:
-                pool_pass(r // 2, j, h, acc(i))
-
-        def warm_up(n):
-            for i in range(n):
-                dummy = psum.tile([P, N_TILE], F32, name=acc(SUMS - 1), tag=acc(SUMS - 1))
-                nc.tensor.matmul(out=dummy[:], lhsT=warm[:, 0:P], rhs=warm[:], start=True, stop=True)
-
-        warm_up(WARM)
         widen(0, 0)
-        transpose((0, 0), rot())
-        reorder_queries(0, True)
-        transpose(("q", 0), acc(0))
+        transpose((0, 0), next_bank())
+        reorder_queries(0, nc.scalar.copy)
+        transpose(("q", 0), sum_bank(0))
         widen(0, 1)
-        transpose((0, 1), rot())
-        copy_docs(0, 0)
-        reorder_queries(1, HEAD == 3)
-        transpose(("q", 1), acc(1))
-        copy_queries(0, True)
+        transpose((0, 1), next_bank())
+        copy_docs([(0, 0)])
+        reorder_queries(1, nc.vector.tensor_copy)
+        transpose(("q", 1), sum_bank(1))
+        copy_queries(0)
         widen(0, 2)
-        copy_docs(0, 1)
-        if LOADS == 2:
-            widen(0, 3)
-        reorder_queries(2, False)
-        transpose(("q", 2), acc(2))
-        copy_queries(1, True)
-        if HEAD == 1:
-            quantize_docs(0, 0)
-        reorder_queries(3, False)
-        transpose(("q", 3), acc(3))
-        warm_up(WARM3)
-        copy_queries(2, True)
-        copy_queries(3, True)
-        if LOADS != 2:
-            widen(0, 3)
-        if HEAD != 1:
-            quantize_docs(0, 0)
+        copy_docs([(0, 1)])
+        reorder_queries(2, nc.vector.tensor_copy)
+        transpose(("q", 2), sum_bank(2))
+        copy_queries(1)
+        quantize_docs([(0, 0)])
+        reorder_queries(3, nc.vector.tensor_copy)
+        transpose(("q", 3), sum_bank(3))
+        copy_queries(2)
+        copy_queries(3)
+        widen(0, 3)
         quantize_queries(0)
-        if PATTERN == 0:
-            widen(1, 0)
+        widen(1, 0)
         quantize_queries(1)
-        quantize_docs(0, 1)
+        quantize_docs([(0, 1)])
         nc.vector.reciprocal(out=inv_norms[:], in_=norms_raw[:].rearrange("p g t -> p (g t)"))
 
-        late_tags = {}
-        late_done = [0] * len(late)
-
-        def pool_late(i, upto):
-            for g in range(late_done[i], upto):
-                pool_pass(g, late[i][0], late[i][1], late_tags[i])
-            late_done[i] = max(upto, late_done[i])
-
-        keys = [(n // PACK, n % PACK) for n in range(GROUPS * PACK)]
-        sizes = [[2] + [3] * 10, [2, 2] + [3] * 8 + [2, 2], [2, 2, 2] + [3] * 8 + [2], [2, 2, 2, 2] + [3] * 8][PATTERN]
-        runs = [keys[sum(sizes[0:i]) : sum(sizes[0 : i + 1])] for i in range(len(sizes))]
-        passes = [(r // 2, j, h, acc(i)) for r in range(STEPS) for i, (j, h) in enumerate(early) if j // 2 == r % 2]
+        keys = [(g, t) for g in range(GROUPS) for t in range(PACK)]
+        runs = [keys[0:2]] + [keys[n : n + STEP_TILES] for n in range(2, len(keys), STEP_TILES)]
+        passes = [
+            (r // 2, j, first, N_TILE, sum_bank(i))
+            for r in range(HALVES)
+            for i, (j, first) in enumerate(early)
+            if j // 2 == r % 2
+        ]
+        scored = 0
         packed = 0
         quantized = 0
         pooled = 0
-        scored = 0
         for k in range(len(runs)):
             turn = runs[k + 1] if k + 1 < len(runs) else []
             ahead = runs[k + 2] if k + 2 < len(runs) else []
-            ready = len([1 for g, j, h, tag in passes if 2 * g + j // 2 < quantized])
-            can_pack = 2 * (scored // PACK)
-            upto = min(ready, pooled + BUDGET)
-            pre = min(upto, pooled + PRE)
-            for g, j, h, tag in passes[pooled:pre]:
-                pool_pass(g, j, h, tag)
+            ready = len([1 for item in passes if 2 * item[0] + item[1] // 2 < quantized])
+            upto = min(ready, pooled + STEP_PASSES)
+            before = min(upto, pooled + PASSES_BEFORE_RUN)
+            halves = list(range(packed, min(2 * (scored // PACK), packed + 2)))
+
+            for item in passes[pooled:before]:
+                pool_pass(*item)
             for key in turn:
-                transpose(key, rot())
-            if ahead:
-                widen(*ahead[0])
+                transpose(key, next_bank())
+            for key in ahead[0:1]:
+                widen(*key)
             if turn:
-                copy_pair(turn[0:2])
-            if len(turn) == 3:
-                copy_docs(*turn[2])
-            share = SCALAR_QUERIES if k < S_SHARE_TO else 0
+                copy_docs(turn[0:2])
+                copy_docs(turn[2:3])
             if quantized < packed:
                 quantize_rel(quantized)
                 quantized += 1
-            todo = list(range(packed, min(can_pack, packed + 2)))
-            if todo:
-                interleave(todo[0], 0, HALF, False)
-            if ahead:
-                widen(*ahead[1])
-            if len(todo) == 2:
-                quantize_rel(todo[0])
+            if halves:
+                interleave(halves[0], 0)
+            for key in ahead[1:2]:
+                widen(*key)
+            if halves:
+                quantize_rel(halves[0])
                 quantized += 1
-                interleave(todo[1], 0, HALF - share, False)
-                interleave(todo[1], HALF - share, HALF, True)
-            packed += len(todo)
-            if len(ahead) == 3:
-                widen(*ahead[2])
-            for g, j, h, tag in passes[pre:upto]:
-                pool_pass(g, j, h, tag)
+                interleave(halves[1], SCALAR_QUERIES)
+            packed += len(halves)
+            for key in ahead[2:3]:
+                widen(*key)
+            for item in passes[before:upto]:
+                pool_pass(*item)
             pooled = upto
             if turn:
-                quantize_pair(turn[0:2])
-            if len(turn) == 3:
-                quantize_docs(*turn[2])
+                quantize_docs(turn[0:2])
+                quantize_docs(turn[2:3])
             for g, t in runs[k]:
-                tag = rot()
-                scores(g, t, tag)
-                relevance(g, t, k < V_REL_FROM or t % 2 == 1)
+                scores(g, t, next_bank())
+                relevance(g, t)
             scored += len(runs[k])
 
-        late_tags.update({0: rot(), 1: rot()})
+        late_banks = [next_bank(), next_bank()]
         for r in range(quantized, packed):
             quantize_rel(r)
-        for r in range(packed, STEPS):
-            interleave(r, 0, HALF - TAIL_SHARE, False)
-            interleave(r, HALF - TAIL_SHARE, HALF, True)
-        for r in range(packed, STEPS):
+        for r in range(packed, HALVES):
+            interleave(r, SCALAR_QUERIES_LAST)
+        for r in range(packed, HALVES):
             quantize_rel(r)
-        for g, j, h, tag in passes[pooled:]:
-            if g < GROUPS - 1:
-                pool_pass(g, j, h, tag)
-        n = 0
-        for r, upto in ((STEPS - 2, LATE_SECOND), (STEPS - 1, LATE_THIRD)):
-            pool_late(0, upto)
-            for i, (j, h) in enumerate(early):
-                if j // 2 == r % 2:
-                    pool_pass(r // 2, j, h, acc(i))
-                    store(j, h, n % 2 == 0)
-                    n += 1
-        for i, (j, h) in enumerate(late[:-1]):
-            pool_late(i, GROUPS)
-            store(j, h, n % 2 == 0)
-            n += 1
-        j, h = late[-1]
+        for item in passes[pooled:]:
+            if item[0] < GROUPS - 1:
+                pool_pass(*item)
+        for g in range(LATE_PASSES_FIRST):
+            pool_pass(g, *late[0], N_TILE, late_banks[0])
+        for item in passes[-EARLY_SUMS:]:
+            pool_pass(*item)
+            store(*item[1:4])
+        for g in range(LATE_PASSES_FIRST, GROUPS):
+            pool_pass(g, *late[0], N_TILE, late_banks[0])
+        store(*late[0], N_TILE)
+        for g in range(GROUPS):
+            pool_pass(g, *late[1], N_TILE, late_banks[1])
+        store(*late[1], N_TILE)
+        j, first = late[2]
         for piece in range(N_TILE // P):
-            first = h * N_TILE + piece * P
-            bank = psum.tile([P, P], F32, name=acc(piece), tag=acc(piece))
             for g in range(GROUPS):
-                codes, scales = rel_codes[2 * g + j // 2]
-                cols = slice((j % 2) * P, (j % 2 + 1) * P)
-                nc.tensor.matmul_mx(
-                    out=bank[:],
-                    lhsT=codes[:, cols].bitcast(FP8X4),
-                    lhsT_scale=scales[:, cols],
-                    rhs=v_codes[g][:, 2 * first : 2 * (first + P)].bitcast(FP4X4),
-                    rhs_scale=v_scale[:, g, first : first + P],
-                    start=(g == 0),
-                    stop=(g == GROUPS - 1),
-                )
-            result = work.tile([P, P], F32, name="piece", tag="piece", bufs=4)
-            if piece % 2 == 0:
-                nc.scalar.copy(out=result[:], in_=bank[:])
-            else:
-                nc.vector.tensor_copy(out=result[:], in_=bank[:])
-            nc.sync.dma_start(out=out[j * P : (j + 1) * P, first : first + P], in_=result[:])
+                pool_pass(g, j, first + piece * P, P, sum_bank(piece))
+            store(j, first + piece * P, P)

@@ -29,14 +29,9 @@ N_TILE = 512
 HALF = B // 2
 HALVES = 2 * GROUPS
 
-EARLY_SUMS = 5
-TURN_BANKS = 8 - EARLY_SUMS
-STEP_TILES = TURN_BANKS
-STEP_PASSES = 4
-PASSES_BEFORE_RUN = 2
-SCALAR_QUERIES = 80
-SCALAR_QUERIES_LAST = 96
-LATE_PASSES_FIRST = 6
+TURN_BANKS = 4
+SCALAR_QUERIES = 0
+SCALAR_QUERIES_LATE = 64
 
 
 def tile_archived_docs_feedback_d4_kernel(tc, docs_bytes, docs_scale, queries, norms, v_words, v_scales, out):
@@ -85,17 +80,17 @@ def tile_archived_docs_feedback_d4_kernel(tc, docs_bytes, docs_scale, queries, n
             v_codes[g] = tile
 
         norms_raw = keep.tile([P, GROUPS, PACK], BF16, name="norms_raw")
-        load_scales(0, 1)
+        load_scales(0, 2)
         load_docs(0, 0, 1)
-        load_queries(0)
         load_docs(0, 1, 1)
-        load_queries(1)
+        load_queries(0)
         load_docs(0, 2, 1)
-        load_queries(2)
-        load_queries(3)
+        load_queries(1)
         load_docs(0, 3, 1)
-        load_scales(1, 2)
-        load_docs(1, 0, 2)
+        load_queries(2)
+        load_docs(1, 0, 1)
+        load_queries(3)
+        load_docs(1, 1, 1)
         nc.sync.dma_start(out=norms_raw[:], in_=norms.rearrange("(g m t) -> m g t", m=P, t=PACK))
         load_docs(1, 2, 2)
         load_scales(2, GROUPS)
@@ -125,19 +120,19 @@ def tile_archived_docs_feedback_d4_kernel(tc, docs_bytes, docs_scale, queries, n
         rel_codes = {}
         sums = {}
 
-        def widen(g, t):
+        def widen(g, t, on_scalar=False):
             tile = work.tile([P, 2, K // (2 * RUN), RUN], BF16, name="wide", tag="wide", bufs=8, align_bytes=64)
             reordered[(g, t)] = tile
             per = G // (2 * RUN)
             for i in range(SCALE_BLOCKS):
                 col = t * SCALE_BLOCKS + i
-                nc.vector.tensor_scalar(
-                    out=tile[:, :, per * i : per * (i + 1), :].rearrange("p u b r -> p b u r"),
-                    in0=doc_bytes[(g, t)][:, G * i : G * (i + 1)].bitcast(FP8).rearrange("p (b u r) -> p b u r", u=2, r=RUN),
-                    scalar1=doc_scale[g][:, col : col + 1],
-                    scalar2=None,
-                    op0=ALU.mult,
-                )
+                dst = tile[:, :, per * i : per * (i + 1), :].rearrange("p u b r -> p b u r")
+                src = doc_bytes[(g, t)][:, G * i : G * (i + 1)].bitcast(FP8).rearrange("p (b u r) -> p b u r", u=2, r=RUN)
+                scale = doc_scale[g][:, col : col + 1]
+                if on_scalar:
+                    nc.scalar.activation(out=dst, in_=src, func=ACT.Copy, scale=scale)
+                else:
+                    nc.vector.tensor_scalar(out=dst, in0=src, scalar1=scale, scalar2=None, op0=ALU.mult)
 
         def reorder_queries(j, copy):
             tile = keep.tile([P, 2, K // (2 * RUN), RUN], BF16, name="q_wide_%d" % j, align_bytes=64)
@@ -157,15 +152,14 @@ def tile_archived_docs_feedback_d4_kernel(tc, docs_bytes, docs_scale, queries, n
             nc.scalar.copy(out=dst, in_=turn_bank[key][:].rearrange("p s u d -> p s d u"))
 
         def copy_docs(keys):
-            tag = "turned%d" % len(keys)
-            tile = work.tile([P, len(keys), K_PASSES, P, 2], F32, name=tag, tag=tag, bufs=6 // len(keys), align_bytes=64)
-            for i, key in enumerate(keys):
-                turned[key] = tile
-                copy_turned(key, tile[:, i, :, :, :])
+            for g, t in keys:
+                if t % 2 == 0:
+                    turned[(g, t)] = work.tile([P, 2, K_PASSES, P, 2], F32, name="turned", tag="turned", bufs=4, align_bytes=64)
+                copy_turned((g, t), turned[(g, t - t % 2)][:, t % 2, :, :, :])
 
         def quantize_docs(keys):
             width = K_PASSES * P
-            depth = 5 - len(keys)
+            depth = 4
             tag = "doc_codes%d" % len(keys)
             codes = work.tile([P, len(keys) * width], U32, name=tag, tag=tag, bufs=depth, align_bytes=64)
             tag = "doc_scales%d" % len(keys)
@@ -207,7 +201,7 @@ def tile_archived_docs_feedback_d4_kernel(tc, docs_bytes, docs_scale, queries, n
 
         def relevance(g, t):
             if t == 0:
-                rel_planes[g] = work.tile([P, PACK, B], BF16, name="rel_planes", tag="rel_planes", bufs=3, align_bytes=64)
+                rel_planes[g] = keep.tile([P, PACK, B], BF16, name="rel_planes_%d" % g, align_bytes=64)
             col = g * PACK + t
             nc.scalar.activation(
                 out=rel_planes[g][:, t, :], in_=score_bank[(g, t)][:], func=ACT.Relu, scale=inv_norms[:, col : col + 1]
@@ -258,122 +252,127 @@ def tile_archived_docs_feedback_d4_kernel(tc, docs_bytes, docs_scale, queries, n
             copy(out=result[:], in_=sums[(j, first)][:])
             nc.sync.dma_start(out=out[j * P : (j + 1) * P, first : first + width], in_=result[:])
 
-        taken = []
+        def turn_tag(t):
+            return "rot%d" % t
 
-        def next_bank():
-            taken.append(len(taken) % TURN_BANKS)
-            return "rot%d" % taken[-1]
+        def sum_tag(j, first):
+            return "acc%d" % (2 * (j % 2) + first // N_TILE)
 
-        def sum_bank(i):
-            return "acc%d" % i
+        def early_passes(g, j):
+            for first in range(0, N, N_TILE):
+                pool_pass(g, j, first, N_TILE, sum_tag(j, first))
 
-        all_sums = [(j, first) for first in range(0, N, N_TILE) for j in range(Q_TILES)]
-        early, late = all_sums[:EARLY_SUMS], all_sums[EARLY_SUMS:]
+        def score_pair(g, t0, tags):
+            for t in (t0, t0 + 1):
+                scores(g, t, tags[t])
 
+        def relevance_pair(g, t0):
+            for t in (t0, t0 + 1):
+                relevance(g, t)
+
+        def turn_pair(g, t0):
+            for t in (t0, t0 + 1):
+                transpose((g, t), turn_tag(t))
+            copy_docs([(g, t0), (g, t0 + 1)])
+
+        sum_tags = [sum_tag(j, first) for j in range(2) for first in range(0, N, N_TILE)]
         widen(0, 0)
-        transpose((0, 0), next_bank())
-        reorder_queries(0, nc.scalar.copy)
-        transpose(("q", 0), sum_bank(0))
         widen(0, 1)
-        transpose((0, 1), next_bank())
-        copy_docs([(0, 0)])
-        reorder_queries(1, nc.vector.tensor_copy)
-        transpose(("q", 1), sum_bank(1))
-        copy_queries(0)
+        transpose((0, 0), turn_tag(0))
+        transpose((0, 1), turn_tag(1))
+        reorder_queries(0, nc.scalar.copy)
+        transpose(("q", 0), sum_tags[0])
+        copy_docs([(0, 0), (0, 1)])
         widen(0, 2)
-        copy_docs([(0, 1)])
-        reorder_queries(2, nc.vector.tensor_copy)
-        transpose(("q", 2), sum_bank(2))
-        copy_queries(1)
-        quantize_docs([(0, 0)])
+        reorder_queries(1, nc.vector.tensor_copy)
+        transpose(("q", 1), sum_tags[1])
+        reorder_queries(2, nc.scalar.copy)
+        widen(0, 3)
+        transpose((0, 2), turn_tag(2))
+        transpose(("q", 2), sum_tags[2])
+        widen(1, 0)
         reorder_queries(3, nc.vector.tensor_copy)
-        transpose(("q", 3), sum_bank(3))
+        transpose((0, 3), turn_tag(3))
+        transpose(("q", 3), sum_tags[3])
+        copy_queries(0)
+        copy_queries(1)
         copy_queries(2)
         copy_queries(3)
-        widen(0, 3)
+        copy_docs([(0, 2), (0, 3)])
+        widen(1, 1)
+        turn_pair(1, 0)
         quantize_queries(0)
-        widen(1, 0)
+        widen(1, 2)
+        quantize_docs([(0, 0), (0, 1)])
         quantize_queries(1)
-        quantize_docs([(0, 1)])
         nc.vector.reciprocal(out=inv_norms[:], in_=norms_raw[:].rearrange("p g t -> p (g t)"))
+        widen(1, 3)
+        transpose((1, 2), turn_tag(2))
+        copy_docs([(1, 2)])
+        scores(0, 0, sum_tags[0])
+        relevance(0, 0)
+        transpose((1, 3), turn_tag(3))
+        copy_docs([(1, 3)])
+        scores(0, 1, sum_tags[1])
+        relevance(0, 1)
+        quantize_docs([(0, 2), (0, 3)])
+        score_pair(0, 2, sum_tags)
+        relevance_pair(0, 2)
+        widen(2, 0)
+        widen(2, 1)
+        widen(2, 2)
+        widen(2, 3)
 
-        keys = [(g, t) for g in range(GROUPS) for t in range(PACK)]
-        runs = [keys[0:2]] + [keys[n : n + STEP_TILES] for n in range(2, len(keys), STEP_TILES)]
-        passes = [
-            (r // 2, j, first, N_TILE, sum_bank(i))
-            for r in range(HALVES)
-            for i, (j, first) in enumerate(early)
-            if j // 2 == r % 2
-        ]
-        scored = 0
-        packed = 0
-        quantized = 0
-        pooled = 0
-        for k in range(len(runs)):
-            turn = runs[k + 1] if k + 1 < len(runs) else []
-            ahead = runs[k + 2] if k + 2 < len(runs) else []
-            ready = len([1 for item in passes if 2 * item[0] + item[1] // 2 < quantized])
-            upto = min(ready, pooled + STEP_PASSES)
-            before = min(upto, pooled + PASSES_BEFORE_RUN)
-            halves = list(range(packed, min(2 * (scored // PACK), packed + 2)))
-
-            for item in passes[pooled:before]:
-                pool_pass(*item)
-            for key in turn:
-                transpose(key, next_bank())
-            for key in ahead[0:1]:
-                widen(*key)
-            if turn:
-                copy_docs(turn[0:2])
-                copy_docs(turn[2:3])
-            if quantized < packed:
-                quantize_rel(quantized)
-                quantized += 1
-            if halves:
-                interleave(halves[0], 0)
-            for key in ahead[1:2]:
-                widen(*key)
-            if halves:
-                quantize_rel(halves[0])
-                quantized += 1
-                interleave(halves[1], SCALAR_QUERIES)
-            packed += len(halves)
-            for key in ahead[2:3]:
-                widen(*key)
-            for item in passes[before:upto]:
-                pool_pass(*item)
-            pooled = upto
-            if turn:
-                quantize_docs(turn[0:2])
-                quantize_docs(turn[2:3])
-            for g, t in runs[k]:
-                scores(g, t, next_bank())
+        for g in range(1, GROUPS):
+            if g + 1 < GROUPS:
+                turn_pair(g + 1, 0)
+                turn_pair(g + 1, 2)
+            if g >= 2:
+                early_passes(g - 2, 1)
+            quantize_docs([(g, 0), (g, 1)])
+            quantize_docs([(g, 2), (g, 3)])
+            interleave(2 * (g - 1), SCALAR_QUERIES)
+            for t in range(PACK):
+                scores(g, t, turn_tag(t))
                 relevance(g, t)
-            scored += len(runs[k])
+            if g + 2 < GROUPS:
+                widen(g + 2, 0)
+                quantize_rel(2 * (g - 1))
+                for t in range(1, PACK):
+                    widen(g + 2, t)
+            else:
+                late = [0, 1, 2] if g + 2 == GROUPS else [3, 4, 5]
+                interleave(2 * late[0] + 1, 0)
+                quantize_rel(2 * (g - 1))
+                interleave(2 * late[1] + 1, 0)
+                quantize_rel(2 * late[0] + 1)
+                interleave(2 * late[2] + 1, 0)
+                quantize_rel(2 * late[1] + 1)
+                quantize_rel(2 * late[2] + 1)
+            early_passes(g - 1, 0)
 
-        late_banks = [next_bank(), next_bank()]
-        for r in range(quantized, packed):
-            quantize_rel(r)
-        for r in range(packed, HALVES):
-            interleave(r, SCALAR_QUERIES_LAST)
-        for r in range(packed, HALVES):
-            quantize_rel(r)
-        for item in passes[pooled:]:
-            if item[0] < GROUPS - 1:
-                pool_pass(*item)
-        for g in range(LATE_PASSES_FIRST):
-            pool_pass(g, *late[0], N_TILE, late_banks[0])
-        for item in passes[-EARLY_SUMS:]:
-            pool_pass(*item)
-            store(*item[1:4])
-        for g in range(LATE_PASSES_FIRST, GROUPS):
-            pool_pass(g, *late[0], N_TILE, late_banks[0])
-        store(*late[0], N_TILE)
+        last = GROUPS - 1
+        early_passes(last - 1, 1)
+        interleave(2 * last - 1, 0)
+        interleave(2 * last, SCALAR_QUERIES_LATE)
+        quantize_rel(2 * last - 1)
+        interleave(2 * last + 1, SCALAR_QUERIES_LATE)
+        quantize_rel(2 * last)
+        quantize_rel(2 * last + 1)
+        for g in range(last):
+            for first in range(0, N, N_TILE):
+                pool_pass(g, 2, first, N_TILE, turn_tag(first // N_TILE))
+        for j in range(2):
+            early_passes(last, j)
+            for first in range(0, N, N_TILE):
+                store(j, first, N_TILE)
+        for first in range(0, N, N_TILE):
+            pool_pass(last, 2, first, N_TILE, turn_tag(first // N_TILE))
+            store(2, first, N_TILE)
         for g in range(GROUPS):
-            pool_pass(g, *late[1], N_TILE, late_banks[1])
-        store(*late[1], N_TILE)
-        j, first = late[2]
+            pool_pass(g, 3, 0, N_TILE, turn_tag(2))
+        store(3, 0, N_TILE)
         for piece in range(N_TILE // P):
             for g in range(GROUPS):
-                pool_pass(g, j, first + piece * P, P, sum_bank(piece))
-            store(j, first + piece * P, P)
+                pool_pass(g, 3, N_TILE + piece * P, P, "acc%d" % piece)
+            store(3, N_TILE + piece * P, P)

@@ -32,6 +32,7 @@ HALVES = 2 * GROUPS
 TURN_BANKS = 4
 SCALAR_QUERIES = 0
 SCALAR_QUERIES_LATE = 64
+LATE_FIRST = 2
 
 
 def tile_archived_docs_feedback_d4_kernel(tc, docs_bytes, docs_scale, queries, norms, v_words, v_scales, out):
@@ -139,9 +140,11 @@ def tile_archived_docs_feedback_d4_kernel(tc, docs_bytes, docs_scale, queries, n
             reordered[("q", j)] = tile
             copy(out=tile[:], in_=q_raw[j][:].rearrange("p (b u r) -> p u b r", u=2, r=RUN))
 
-        def transpose(key, tag):
+        def transpose(key, tag, warm=0):
             bank = psum.tile([P, K_PASSES, 2, P], F32, name=tag, tag=tag)
             turn_bank[key] = bank
+            for n in range(warm):
+                nc.tensor.matmul(out=bank[:, 0, 0, :], lhsT=ident_raw[:], rhs=ident_raw[:], start=True, stop=True)
             words = reordered[key][:].rearrange("p u b r -> p (u b r)").bitcast(F32)
             for s in range(K_PASSES):
                 for u in range(2):
@@ -278,42 +281,41 @@ def tile_archived_docs_feedback_d4_kernel(tc, docs_bytes, docs_scale, queries, n
         sum_tags = [sum_tag(j, first) for j in range(2) for first in range(0, N, N_TILE)]
         widen(0, 0)
         widen(0, 1)
-        transpose((0, 0), turn_tag(0))
-        transpose((0, 1), turn_tag(1))
+        transpose((0, 0), turn_tag(0), 4)
+        transpose((0, 1), turn_tag(1), 1)
         reorder_queries(0, nc.scalar.copy)
-        transpose(("q", 0), sum_tags[0])
+        transpose(("q", 0), sum_tags[0], 0)
         copy_docs([(0, 0), (0, 1)])
         widen(0, 2)
         reorder_queries(1, nc.vector.tensor_copy)
-        transpose(("q", 1), sum_tags[1])
+        transpose(("q", 1), sum_tags[1], 1)
         reorder_queries(2, nc.scalar.copy)
         widen(0, 3)
-        transpose((0, 2), turn_tag(2))
-        transpose(("q", 2), sum_tags[2])
+        transpose((0, 2), turn_tag(2), 1)
+        transpose(("q", 2), sum_tags[2], 0)
         widen(1, 0)
         reorder_queries(3, nc.vector.tensor_copy)
-        transpose((0, 3), turn_tag(3))
-        transpose(("q", 3), sum_tags[3])
+        transpose(("q", 3), sum_tags[3], 1)
+        transpose((0, 3), turn_tag(3), 1)
         copy_queries(0)
         copy_queries(1)
         copy_queries(2)
         copy_queries(3)
         copy_docs([(0, 2), (0, 3)])
         widen(1, 1)
-        turn_pair(1, 0)
+        transpose((1, 0), turn_tag(0), 0)
+        transpose((1, 1), turn_tag(1), 1)
+        copy_docs([(1, 0), (1, 1)])
         quantize_queries(0)
-        widen(1, 2)
         quantize_docs([(0, 0), (0, 1)])
         quantize_queries(1)
         nc.vector.reciprocal(out=inv_norms[:], in_=norms_raw[:].rearrange("p g t -> p (g t)"))
+        widen(1, 2)
         widen(1, 3)
-        transpose((1, 2), turn_tag(2))
-        copy_docs([(1, 2)])
         scores(0, 0, sum_tags[0])
-        relevance(0, 0)
-        transpose((1, 3), turn_tag(3))
-        copy_docs([(1, 3)])
         scores(0, 1, sum_tags[1])
+        relevance(0, 0)
+        turn_pair(1, 2)
         relevance(0, 1)
         quantize_docs([(0, 2), (0, 3)])
         score_pair(0, 2, sum_tags)
@@ -341,14 +343,13 @@ def tile_archived_docs_feedback_d4_kernel(tc, docs_bytes, docs_scale, queries, n
                 for t in range(1, PACK):
                     widen(g + 2, t)
             else:
-                late = [0, 1, 2] if g + 2 == GROUPS else [3, 4, 5]
-                interleave(2 * late[0] + 1, 0)
-                quantize_rel(2 * (g - 1))
-                interleave(2 * late[1] + 1, 0)
-                quantize_rel(2 * late[0] + 1)
-                interleave(2 * late[2] + 1, 0)
-                quantize_rel(2 * late[1] + 1)
-                quantize_rel(2 * late[2] + 1)
+                late = range(0, LATE_FIRST) if g + 2 == GROUPS else range(LATE_FIRST, GROUPS - 2)
+                waiting = 2 * (g - 1)
+                for r in late:
+                    interleave(2 * r + 1, 0)
+                    quantize_rel(waiting)
+                    waiting = 2 * r + 1
+                quantize_rel(waiting)
             early_passes(g - 1, 0)
 
         last = GROUPS - 1

@@ -30,7 +30,7 @@ HALF = B // 2
 HALVES = 2 * GROUPS
 
 TURN_BANKS = 4
-SCALAR_QUERIES = 0
+SCALAR_QUERIES = 96
 SCALAR_QUERIES_LATE = 64
 LATE_FIRST = 2
 
@@ -210,17 +210,14 @@ def tile_archived_docs_feedback_d4_kernel(tc, docs_bytes, docs_scale, queries, n
                 out=rel_planes[g][:, t, :], in_=score_bank[(g, t)][:], func=ACT.Relu, scale=inv_norms[:, col : col + 1]
             )
 
-        def interleave(r, scalar_queries):
+        def interleave(r, copy, lo, hi):
             g, first = r // 2, (r % 2) * HALF
-            tile = work.tile([P, HALF, PACK], BF16, name="rel_packed", tag="rel_packed", bufs=3, align_bytes=64)
-            rel_packed[r] = tile
-            split = HALF - scalar_queries
-            shares = [(nc.vector.tensor_copy, 0, split), (nc.scalar.copy, split, HALF)]
-            for copy, lo, hi in [share for share in shares if share[1] < share[2]]:
-                copy(
-                    out=tile[:, lo:hi, :].rearrange("p (c i) t -> p c t i", i=4),
-                    in_=rel_planes[g][:, :, first + lo : first + hi].rearrange("p t (c i) -> p c t i", i=4),
-                )
+            if r not in rel_packed:
+                rel_packed[r] = work.tile([P, HALF, PACK], BF16, name="rel_packed", tag="rel_packed", bufs=4, align_bytes=64)
+            copy(
+                out=rel_packed[r][:, lo:hi, :].rearrange("p (c i) t -> p c t i", i=4),
+                in_=rel_planes[g][:, :, first + lo : first + hi].rearrange("p t (c i) -> p c t i", i=4),
+            )
 
         def quantize_rel(r):
             codes = keep.tile([P, HALF], U32, name="rel_codes_%d" % r, align_bytes=64)
@@ -328,12 +325,14 @@ def tile_archived_docs_feedback_d4_kernel(tc, docs_bytes, docs_scale, queries, n
         for g in range(1, GROUPS):
             if g + 1 < GROUPS:
                 turn_pair(g + 1, 0)
+            interleave(2 * (g - 1), nc.scalar.copy, HALF - SCALAR_QUERIES, HALF)
+            if g + 1 < GROUPS:
                 turn_pair(g + 1, 2)
             if g >= 2:
                 early_passes(g - 2, 1)
             quantize_docs([(g, 0), (g, 1)])
             quantize_docs([(g, 2), (g, 3)])
-            interleave(2 * (g - 1), SCALAR_QUERIES)
+            interleave(2 * (g - 1), nc.vector.tensor_copy, 0, HALF - SCALAR_QUERIES)
             for t in range(PACK):
                 scores(g, t, turn_tag(t))
                 relevance(g, t)
@@ -346,7 +345,7 @@ def tile_archived_docs_feedback_d4_kernel(tc, docs_bytes, docs_scale, queries, n
                 late = range(0, LATE_FIRST) if g + 2 == GROUPS else range(LATE_FIRST, GROUPS - 2)
                 waiting = 2 * (g - 1)
                 for r in late:
-                    interleave(2 * r + 1, 0)
+                    interleave(2 * r + 1, nc.vector.tensor_copy, 0, HALF)
                     quantize_rel(waiting)
                     waiting = 2 * r + 1
                 quantize_rel(waiting)
@@ -354,10 +353,12 @@ def tile_archived_docs_feedback_d4_kernel(tc, docs_bytes, docs_scale, queries, n
 
         last = GROUPS - 1
         early_passes(last - 1, 1)
-        interleave(2 * last - 1, 0)
-        interleave(2 * last, SCALAR_QUERIES_LATE)
+        interleave(2 * last - 1, nc.vector.tensor_copy, 0, HALF)
+        interleave(2 * last, nc.vector.tensor_copy, 0, HALF - SCALAR_QUERIES_LATE)
+        interleave(2 * last, nc.scalar.copy, HALF - SCALAR_QUERIES_LATE, HALF)
         quantize_rel(2 * last - 1)
-        interleave(2 * last + 1, SCALAR_QUERIES_LATE)
+        interleave(2 * last + 1, nc.vector.tensor_copy, 0, HALF - SCALAR_QUERIES_LATE)
+        interleave(2 * last + 1, nc.scalar.copy, HALF - SCALAR_QUERIES_LATE, HALF)
         quantize_rel(2 * last)
         quantize_rel(2 * last + 1)
         for g in range(last):

@@ -30,7 +30,7 @@ HALF = B // 2
 HALVES = 2 * GROUPS
 
 TURN_BANKS = 4
-SCALAR_QUERIES = 96
+SCALAR_QUERIES = 32
 SCALAR_QUERIES_LATE = 64
 LATE_FIRST = 2
 
@@ -46,7 +46,6 @@ def tile_archived_docs_feedback_d4_kernel(tc, docs_bytes, docs_scale, queries, n
         ident_raw = keep.tile([P, P], F32, name="ident_raw")
         make_identity(nc, ident_raw[:])
         ident = keep.tile([P, P], F32, name="ident")
-        nc.scalar.activation(out=ident[:], in_=ident_raw[:], func=ACT.Relu)
 
         v_scale = keep.tile([P, GROUPS, N], U8, name="v_scale", align_bytes=64)
         nc.vector.memset(v_scale[:].rearrange("p g n -> p (g n)").bitcast(I32), 0)
@@ -64,9 +63,9 @@ def tile_archived_docs_feedback_d4_kernel(tc, docs_bytes, docs_scale, queries, n
             for i in range(count):
                 doc_bytes[(g, t0 + i)] = tile[:, i, :]
 
-        def load_scales(g0, g1):
+        def load_scales(g0, g1, queue):
             tile = keep.tile([P, g1 - g0, PACK * SCALE_BLOCKS], F32, name="doc_scale_%d" % g0)
-            nc.sync.dma_start(out=tile[:], in_=scale_rows[:, g0:g1, :])
+            queue.dma_start(out=tile[:], in_=scale_rows[:, g0:g1, :])
             for g in range(g0, g1):
                 doc_scale[g] = tile[:, g - g0, :]
 
@@ -81,7 +80,8 @@ def tile_archived_docs_feedback_d4_kernel(tc, docs_bytes, docs_scale, queries, n
             v_codes[g] = tile
 
         norms_raw = keep.tile([P, GROUPS, PACK], BF16, name="norms_raw")
-        load_scales(0, 2)
+        load_scales(0, 1, nc.scalar)
+        nc.scalar.activation(out=ident[:], in_=ident_raw[:], func=ACT.Relu)
         load_docs(0, 0, 1)
         load_docs(0, 1, 1)
         load_queries(0)
@@ -89,22 +89,25 @@ def tile_archived_docs_feedback_d4_kernel(tc, docs_bytes, docs_scale, queries, n
         load_queries(1)
         load_docs(0, 3, 1)
         load_queries(2)
+        load_scales(1, 2, nc.sync)
         load_docs(1, 0, 1)
         load_queries(3)
         load_docs(1, 1, 1)
         nc.sync.dma_start(out=norms_raw[:], in_=norms.rearrange("(g m t) -> m g t", m=P, t=PACK))
         load_docs(1, 2, 2)
-        load_scales(2, GROUPS)
+        load_scales(2, GROUPS, nc.sync)
         load_docs(2, 0, PACK)
+        load_docs(3, 0, PACK)
+        load_v(0)
         for q in range(4):
             nc.sync.dma_start(
                 out=v_scale[32 * q : 32 * q + 4, :, :].bitcast(I32),
                 in_=v_scales[:, 4 * q : 4 * q + 4, :].rearrange("g r n -> r g n").bitcast(I32),
             )
-        for g in range(GROUPS):
-            load_v(g)
+        for g in range(1, GROUPS):
             if g + 3 < GROUPS:
                 load_docs(g + 3, 0, PACK)
+            load_v(g)
 
         inv_norms = keep.tile([P, GROUPS * PACK], F32, name="inv_norms")
         q_turned = keep.tile([P, K_PASSES, B, 2], F32, name="q_turned", align_bytes=64)
@@ -374,7 +377,9 @@ def tile_archived_docs_feedback_d4_kernel(tc, docs_bytes, docs_scale, queries, n
         for g in range(GROUPS):
             pool_pass(g, 3, 0, N_TILE, turn_tag(2))
         store(3, 0, N_TILE)
-        for piece in range(N_TILE // P):
+        first = N_TILE
+        for piece, width in enumerate([2 * P, P, P]):
             for g in range(GROUPS):
-                pool_pass(g, 3, N_TILE + piece * P, P, "acc%d" % piece)
-            store(3, N_TILE + piece * P, P)
+                pool_pass(g, 3, first, width, "acc%d" % piece)
+            store(3, first, width)
+            first = first + width

@@ -31,8 +31,6 @@ HALVES = 2 * GROUPS
 
 TURN_BANKS = 4
 SCALAR_QUERIES = 32
-SCALAR_QUERIES_LATE = 64
-LATE_FIRST = 2
 
 
 def tile_archived_docs_feedback_d4_kernel(tc, docs_bytes, docs_scale, queries, norms, v_words, v_scales, out):
@@ -216,7 +214,7 @@ def tile_archived_docs_feedback_d4_kernel(tc, docs_bytes, docs_scale, queries, n
         def interleave(r, copy, lo, hi):
             g, first = r // 2, (r % 2) * HALF
             if r not in rel_packed:
-                rel_packed[r] = work.tile([P, HALF, PACK], BF16, name="rel_packed", tag="rel_packed", bufs=4, align_bytes=64)
+                rel_packed[r] = work.tile([P, HALF, PACK], BF16, name="rel_packed", tag="rel_packed", bufs=6, align_bytes=64)
             copy(
                 out=rel_packed[r][:, lo:hi, :].rearrange("p (c i) t -> p c t i", i=4),
                 in_=rel_planes[g][:, :, first + lo : first + hi].rearrange("p t (c i) -> p c t i", i=4),
@@ -278,10 +276,16 @@ def tile_archived_docs_feedback_d4_kernel(tc, docs_bytes, docs_scale, queries, n
                 transpose((g, t), turn_tag(t))
             copy_docs([(g, t0), (g, t0 + 1)])
 
+        def early(g):
+            return 2 * g
+
+        def late(g):
+            return 2 * g + 1
+
         sum_tags = [sum_tag(j, first) for j in range(2) for first in range(0, N, N_TILE)]
         widen(0, 0)
         widen(0, 1)
-        transpose((0, 0), turn_tag(0), 4)
+        transpose((0, 0), turn_tag(0), 3)
         transpose((0, 1), turn_tag(1), 1)
         reorder_queries(0, nc.scalar.copy)
         transpose(("q", 0), sum_tags[0], 0)
@@ -314,9 +318,8 @@ def tile_archived_docs_feedback_d4_kernel(tc, docs_bytes, docs_scale, queries, n
         widen(1, 3)
         scores(0, 0, sum_tags[0])
         scores(0, 1, sum_tags[1])
-        relevance(0, 0)
+        relevance_pair(0, 0)
         turn_pair(1, 2)
-        relevance(0, 1)
         quantize_docs([(0, 2), (0, 3)])
         score_pair(0, 2, sum_tags)
         relevance_pair(0, 2)
@@ -325,45 +328,56 @@ def tile_archived_docs_feedback_d4_kernel(tc, docs_bytes, docs_scale, queries, n
         widen(2, 2)
         widen(2, 3)
 
-        for g in range(1, GROUPS):
-            if g + 1 < GROUPS:
-                turn_pair(g + 1, 0)
-            interleave(2 * (g - 1), nc.scalar.copy, HALF - SCALAR_QUERIES, HALF)
-            if g + 1 < GROUPS:
-                turn_pair(g + 1, 2)
+        last = GROUPS - 1
+        for g in range(1, last):
+            turn_pair(g + 1, 0)
+            interleave(early(g - 1), nc.scalar.copy, HALF - SCALAR_QUERIES, HALF)
+            turn_pair(g + 1, 2)
             if g >= 2:
                 early_passes(g - 2, 1)
             quantize_docs([(g, 0), (g, 1)])
             quantize_docs([(g, 2), (g, 3)])
-            interleave(2 * (g - 1), nc.vector.tensor_copy, 0, HALF - SCALAR_QUERIES)
+            interleave(early(g - 1), nc.vector.tensor_copy, 0, HALF - SCALAR_QUERIES)
             for t in range(PACK):
                 scores(g, t, turn_tag(t))
                 relevance(g, t)
             if g + 2 < GROUPS:
                 widen(g + 2, 0)
-                quantize_rel(2 * (g - 1))
+                quantize_rel(early(g - 1))
                 for t in range(1, PACK):
                     widen(g + 2, t)
             else:
-                late = range(0, LATE_FIRST) if g + 2 == GROUPS else range(LATE_FIRST, GROUPS - 2)
-                waiting = 2 * (g - 1)
-                for r in late:
-                    interleave(2 * r + 1, nc.vector.tensor_copy, 0, HALF)
-                    quantize_rel(waiting)
-                    waiting = 2 * r + 1
-                quantize_rel(waiting)
+                interleave(late(0), nc.vector.tensor_copy, 0, HALF)
+                quantize_rel(early(g - 1))
+                interleave(late(1), nc.vector.tensor_copy, 0, HALF)
+                quantize_rel(late(0))
+                quantize_rel(late(1))
             early_passes(g - 1, 0)
 
-        last = GROUPS - 1
+        interleave(late(2), nc.scalar.copy, 0, HALF)
+        early_passes(last - 2, 1)
+        quantize_docs([(last, 0), (last, 1)])
+        quantize_docs([(last, 2), (last, 3)])
+        interleave(early(last - 1), nc.vector.tensor_copy, 0, HALF)
+        for t in range(PACK):
+            scores(last, t, turn_tag(t))
+            relevance(last, t)
+        interleave(late(3), nc.vector.tensor_copy, 0, HALF)
+        quantize_rel(early(last - 1))
+        early_passes(last - 1, 0)
         early_passes(last - 1, 1)
-        interleave(2 * last - 1, nc.vector.tensor_copy, 0, HALF)
-        interleave(2 * last, nc.vector.tensor_copy, 0, HALF - SCALAR_QUERIES_LATE)
-        interleave(2 * last, nc.scalar.copy, HALF - SCALAR_QUERIES_LATE, HALF)
-        quantize_rel(2 * last - 1)
-        interleave(2 * last + 1, nc.vector.tensor_copy, 0, HALF - SCALAR_QUERIES_LATE)
-        interleave(2 * last + 1, nc.scalar.copy, HALF - SCALAR_QUERIES_LATE, HALF)
-        quantize_rel(2 * last)
-        quantize_rel(2 * last + 1)
+        quantize_rel(late(2))
+        interleave(late(4), nc.vector.tensor_copy, 0, HALF)
+        quantize_rel(late(3))
+        interleave(late(5), nc.scalar.copy, 0, HALF)
+        interleave(late(6), nc.vector.tensor_copy, 0, HALF)
+        quantize_rel(late(4))
+        interleave(early(last), nc.vector.tensor_copy, 0, HALF)
+        quantize_rel(late(5))
+        quantize_rel(late(6))
+        interleave(late(last), nc.scalar.copy, 0, HALF)
+        quantize_rel(early(last))
+        quantize_rel(late(last))
         for g in range(last):
             for first in range(0, N, N_TILE):
                 pool_pass(g, 2, first, N_TILE, turn_tag(first // N_TILE))

@@ -30,7 +30,7 @@ HALF = B // 2
 HALVES = 2 * GROUPS
 
 TURN_BANKS = 4
-SCALAR_QUERIES = 32
+SCALAR_QUERIES = 16
 
 
 def tile_archived_docs_feedback_d4_kernel(tc, docs_bytes, docs_scale, queries, norms, v_words, v_scales, out):
@@ -91,8 +91,8 @@ def tile_archived_docs_feedback_d4_kernel(tc, docs_bytes, docs_scale, queries, n
         load_docs(1, 0, 1)
         load_queries(3)
         load_docs(1, 1, 1)
-        nc.sync.dma_start(out=norms_raw[:], in_=norms.rearrange("(g m t) -> m g t", m=P, t=PACK))
         load_docs(1, 2, 2)
+        nc.sync.dma_start(out=norms_raw[:], in_=norms.rearrange("(g m t) -> m g t", m=P, t=PACK))
         load_scales(2, GROUPS, nc.sync)
         load_docs(2, 0, PACK)
         load_docs(3, 0, PACK)
@@ -163,17 +163,18 @@ def tile_archived_docs_feedback_d4_kernel(tc, docs_bytes, docs_scale, queries, n
 
         def quantize_docs(keys):
             width = K_PASSES * P
-            depth = 4
             tag = "doc_codes%d" % len(keys)
-            codes = work.tile([P, len(keys) * width], U32, name=tag, tag=tag, bufs=depth, align_bytes=64)
+            codes = work.tile([P, len(keys) * width], U32, name=tag, tag=tag, bufs=4, align_bytes=64)
             tag = "doc_scales%d" % len(keys)
-            scales = work.tile([P, len(keys) * width], U8, name=tag, tag=tag, bufs=depth, align_bytes=64)
+            scales = work.tile([P, len(keys) * width], U8, name=tag, tag=tag, bufs=4, align_bytes=64)
             for i, key in enumerate(keys):
                 doc_codes[key] = (codes[:, i * width : (i + 1) * width], scales[:, i * width : (i + 1) * width])
+            g, t = keys[0]
+            pair = turned[(g, t - t % 2)]
             nc.vector.quantize_mx(
                 out=codes[:].bitcast(FP8X4),
                 scales=scales[:],
-                in_=turned[keys[0]][:].rearrange("p t s d u -> p (t s d u)").bitcast(BF16),
+                in_=pair[:, t % 2 : t % 2 + len(keys), :, :, :].rearrange("p t s d u -> p (t s d u)").bitcast(BF16),
             )
 
         def copy_queries(j):
@@ -188,9 +189,16 @@ def tile_archived_docs_feedback_d4_kernel(tc, docs_bytes, docs_scale, queries, n
                     in_=q_turned[:, s, cols, :].rearrange("p b u -> p (b u)").bitcast(BF16),
                 )
 
+        def warm_up(bank, count):
+            for n in range(count):
+                nc.tensor.matmul(out=bank[:, 0:P], lhsT=ident_raw[:], rhs=ident_raw[:], start=True, stop=True)
+
+        def open_scores(g, t, tag):
+            score_bank[(g, t)] = psum.tile([P, B], F32, name=tag, tag=tag)
+            return score_bank[(g, t)]
+
         def scores(g, t, tag):
-            bank = psum.tile([P, B], F32, name=tag, tag=tag)
-            score_bank[(g, t)] = bank
+            bank = score_bank[(g, t)] if (g, t) in score_bank else open_scores(g, t, tag)
             codes, scales = doc_codes[(g, t)]
             for s in range(K_PASSES):
                 nc.tensor.matmul_mx(
@@ -285,56 +293,72 @@ def tile_archived_docs_feedback_d4_kernel(tc, docs_bytes, docs_scale, queries, n
         sum_tags = [sum_tag(j, first) for j in range(2) for first in range(0, N, N_TILE)]
         widen(0, 0)
         widen(0, 1)
-        transpose((0, 0), turn_tag(0), 3)
-        transpose((0, 1), turn_tag(1), 1)
+        transpose((0, 0), turn_tag(0), 4)
+        transpose((0, 1), turn_tag(1))
         reorder_queries(0, nc.scalar.copy)
-        transpose(("q", 0), sum_tags[0], 0)
+        transpose(("q", 0), sum_tags[0])
         copy_docs([(0, 0), (0, 1)])
         widen(0, 2)
         reorder_queries(1, nc.vector.tensor_copy)
         transpose(("q", 1), sum_tags[1], 1)
         reorder_queries(2, nc.scalar.copy)
         widen(0, 3)
-        transpose((0, 2), turn_tag(2), 1)
-        transpose(("q", 2), sum_tags[2], 0)
+        transpose((0, 2), turn_tag(2))
+        transpose(("q", 2), sum_tags[2], 1)
         widen(1, 0)
+        copy_queries(0)
         reorder_queries(3, nc.vector.tensor_copy)
         transpose(("q", 3), sum_tags[3], 1)
-        transpose((0, 3), turn_tag(3), 1)
-        copy_queries(0)
+        transpose((0, 3), turn_tag(3))
         copy_queries(1)
         copy_queries(2)
         copy_queries(3)
         copy_docs([(0, 2), (0, 3)])
         widen(1, 1)
-        transpose((1, 0), turn_tag(0), 0)
-        transpose((1, 1), turn_tag(1), 1)
-        copy_docs([(1, 0), (1, 1)])
-        quantize_queries(0)
+        turn_pair(1, 0)
+        warm_up(open_scores(0, 0, sum_tags[0]), 2)
         quantize_docs([(0, 0), (0, 1)])
-        quantize_queries(1)
-        nc.vector.reciprocal(out=inv_norms[:], in_=norms_raw[:].rearrange("p g t -> p (g t)"))
+        quantize_queries(0)
         widen(1, 2)
         widen(1, 3)
-        scores(0, 0, sum_tags[0])
-        scores(0, 1, sum_tags[1])
-        relevance_pair(0, 0)
-        turn_pair(1, 2)
+        quantize_queries(1)
+        nc.vector.reciprocal(out=inv_norms[:], in_=norms_raw[:].rearrange("p g t -> p (g t)"))
         quantize_docs([(0, 2), (0, 3)])
+        turn_pair(1, 2)
+        score_pair(0, 0, sum_tags)
         score_pair(0, 2, sum_tags)
+        relevance_pair(0, 0)
         relevance_pair(0, 2)
         widen(2, 0)
         widen(2, 1)
         widen(2, 2)
         widen(2, 3)
+        turn_pair(2, 0)
+        transpose((2, 2), turn_tag(2))
+        transpose((2, 3), turn_tag(3))
+        quantize_docs([(1, 0)])
+        quantize_docs([(1, 1)])
+        quantize_docs([(1, 2), (1, 3)])
+        interleave(early(0), nc.scalar.copy, HALF - 64, HALF)
+        interleave(early(0), nc.vector.tensor_copy, 0, HALF - 64)
+        score_pair(1, 0, sum_tags)
+        relevance_pair(1, 0)
+        copy_docs([(2, 2), (2, 3)])
+        score_pair(1, 2, sum_tags)
+        relevance_pair(1, 2)
+        widen(3, 0)
+        quantize_rel(early(0))
+        widen(3, 1)
+        widen(3, 2)
+        widen(3, 3)
+        early_passes(0, 0)
 
         last = GROUPS - 1
-        for g in range(1, last):
+        for g in range(2, last):
             turn_pair(g + 1, 0)
             interleave(early(g - 1), nc.scalar.copy, HALF - SCALAR_QUERIES, HALF)
             turn_pair(g + 1, 2)
-            if g >= 2:
-                early_passes(g - 2, 1)
+            early_passes(g - 2, 1)
             quantize_docs([(g, 0), (g, 1)])
             quantize_docs([(g, 2), (g, 3)])
             interleave(early(g - 1), nc.vector.tensor_copy, 0, HALF - SCALAR_QUERIES)

@@ -30,6 +30,9 @@ HALF = B // 2
 HALVES = 2 * GROUPS
 
 TURN_BANKS = 4
+BANK_HALVES = [((0, 0), (1, 0)), ((0, 1), (2, 0)), ((1, 1), (3, 0)), ((2, 1), (3, 1))]
+QA = 4
+SCALAR_QUERIES_FIRST = 64
 SCALAR_QUERIES = 16
 
 
@@ -72,10 +75,11 @@ def tile_archived_docs_feedback_d4_kernel(tc, docs_bytes, docs_scale, queries, n
             nc.sync.dma_start(out=tile[:], in_=queries[j * P : (j + 1) * P, :])
             q_raw[j] = tile
 
-        def load_v(g):
-            tile = keep.tile([P, 2 * N], U8, name="v_codes_%d" % g, align_bytes=64)
-            nc.sync.dma_start(out=tile[:].bitcast(I32), in_=v_words[g].bitcast(I32))
-            v_codes[g] = tile
+        def load_v(g0, g1):
+            tile = keep.tile([P, g1 - g0, 2 * N], U8, name="v_codes_%d" % g0, align_bytes=64)
+            nc.sync.dma_start(out=tile[:].bitcast(I32), in_=v_words[g0:g1].rearrange("g p n -> p g n").bitcast(I32))
+            for g in range(g0, g1):
+                v_codes[g] = tile[:, g - g0, :]
 
         norms_raw = keep.tile([P, GROUPS, PACK], BF16, name="norms_raw")
         load_scales(0, 1, nc.scalar)
@@ -96,16 +100,17 @@ def tile_archived_docs_feedback_d4_kernel(tc, docs_bytes, docs_scale, queries, n
         load_scales(2, GROUPS, nc.sync)
         load_docs(2, 0, PACK)
         load_docs(3, 0, PACK)
-        load_v(0)
+        load_v(0, 2)
         for q in range(4):
             nc.sync.dma_start(
                 out=v_scale[32 * q : 32 * q + 4, :, :].bitcast(I32),
                 in_=v_scales[:, 4 * q : 4 * q + 4, :].rearrange("g r n -> r g n").bitcast(I32),
             )
-        for g in range(1, GROUPS):
-            if g + 3 < GROUPS:
-                load_docs(g + 3, 0, PACK)
-            load_v(g)
+        load_docs(4, 0, PACK)
+        load_docs(5, 0, PACK)
+        load_v(2, GROUPS)
+        load_docs(6, 0, PACK)
+        load_docs(7, 0, PACK)
 
         inv_norms = keep.tile([P, GROUPS * PACK], F32, name="inv_norms")
         q_turned = keep.tile([P, K_PASSES, B, 2], F32, name="q_turned", align_bytes=64)
@@ -122,7 +127,7 @@ def tile_archived_docs_feedback_d4_kernel(tc, docs_bytes, docs_scale, queries, n
         rel_codes = {}
         sums = {}
 
-        def widen(g, t, on_scalar=False):
+        def widen(g, t):
             tile = work.tile([P, 2, K // (2 * RUN), RUN], BF16, name="wide", tag="wide", bufs=8, align_bytes=64)
             reordered[(g, t)] = tile
             per = G // (2 * RUN)
@@ -131,54 +136,51 @@ def tile_archived_docs_feedback_d4_kernel(tc, docs_bytes, docs_scale, queries, n
                 dst = tile[:, :, per * i : per * (i + 1), :].rearrange("p u b r -> p b u r")
                 src = doc_bytes[(g, t)][:, G * i : G * (i + 1)].bitcast(FP8).rearrange("p (b u r) -> p b u r", u=2, r=RUN)
                 scale = doc_scale[g][:, col : col + 1]
-                if on_scalar:
-                    nc.scalar.activation(out=dst, in_=src, func=ACT.Copy, scale=scale)
-                else:
-                    nc.vector.tensor_scalar(out=dst, in0=src, scalar1=scale, scalar2=None, op0=ALU.mult)
+                nc.vector.tensor_scalar(out=dst, in0=src, scalar1=scale, scalar2=None, op0=ALU.mult)
 
         def reorder_queries(j, copy):
             tile = keep.tile([P, 2, K // (2 * RUN), RUN], BF16, name="q_wide_%d" % j, align_bytes=64)
             reordered[("q", j)] = tile
             copy(out=tile[:], in_=q_raw[j][:].rearrange("p (b u r) -> p u b r", u=2, r=RUN))
 
-        def transpose(key, tag, warm=0):
-            bank = psum.tile([P, K_PASSES, 2, P], F32, name=tag, tag=tag)
-            turn_bank[key] = bank
-            for n in range(warm):
-                nc.tensor.matmul(out=bank[:, 0, 0, :], lhsT=ident_raw[:], rhs=ident_raw[:], start=True, stop=True)
-            words = reordered[key][:].rearrange("p u b r -> p (u b r)").bitcast(F32)
-            for s in range(K_PASSES):
+        def turn(halves, tag, warm=0):
+            bank = psum.tile([P, 2, 2, P], F32, name=tag, tag=tag)
+            turn_bank[halves] = bank
+            warm_up(bank[:, 0, 0, :], warm)
+            for i, (key, s) in enumerate(halves):
+                words = reordered[key][:].rearrange("p u b r -> p (u b r)").bitcast(F32)
                 for u in range(2):
                     first = (u * K_PASSES + s) * P
-                    nc.tensor.transpose(bank[:, s, u, :], words[:, first : first + P], ident[:])
+                    nc.tensor.transpose(bank[:, i, u, :], words[:, first : first + P], ident[:])
 
-        def copy_turned(key, dst):
-            nc.scalar.copy(out=dst, in_=turn_bank[key][:].rearrange("p s u d -> p s d u"))
+        def whole(key):
+            return ((key, 0), (key, 1))
 
-        def copy_docs(keys):
-            for g, t in keys:
-                if t % 2 == 0:
-                    turned[(g, t)] = work.tile([P, 2, K_PASSES, P, 2], F32, name="turned", tag="turned", bufs=4, align_bytes=64)
-                copy_turned((g, t), turned[(g, t - t % 2)][:, t % 2, :, :, :])
+        def copy_turned(halves, dst):
+            nc.scalar.copy(out=dst, in_=turn_bank[halves][:].rearrange("p s u d -> p s d u"))
 
-        def quantize_docs(keys):
-            width = K_PASSES * P
-            tag = "doc_codes%d" % len(keys)
-            codes = work.tile([P, len(keys) * width], U32, name=tag, tag=tag, bufs=4, align_bytes=64)
-            tag = "doc_scales%d" % len(keys)
-            scales = work.tile([P, len(keys) * width], U8, name=tag, tag=tag, bufs=4, align_bytes=64)
-            for i, key in enumerate(keys):
-                doc_codes[key] = (codes[:, i * width : (i + 1) * width], scales[:, i * width : (i + 1) * width])
-            g, t = keys[0]
-            pair = turned[(g, t - t % 2)]
+        def copy_docs(piece, i):
+            if i == 0:
+                tag = "turned%d" % len(piece)
+                turned[piece] = work.tile([P, len(piece), 2, P, 2], F32, name=tag, tag=tag, bufs=4, align_bytes=64)
+            copy_turned(piece[i], turned[piece][:, i, :, :, :])
+
+        def quantize_docs(piece):
+            width = 2 * len(piece) * P
+            tag = "doc_codes%d" % len(piece)
+            codes = work.tile([P, width], U32, name=tag, tag=tag, bufs=4, align_bytes=64)
+            tag = "doc_scales%d" % len(piece)
+            scales = work.tile([P, width], U8, name=tag, tag=tag, bufs=4, align_bytes=64)
+            for i, half in enumerate([half for halves in piece for half in halves]):
+                doc_codes[half] = (codes[:, i * P : (i + 1) * P], scales[:, i * P : (i + 1) * P])
             nc.vector.quantize_mx(
                 out=codes[:].bitcast(FP8X4),
                 scales=scales[:],
-                in_=pair[:, t % 2 : t % 2 + len(keys), :, :, :].rearrange("p t s d u -> p (t s d u)").bitcast(BF16),
+                in_=turned[piece][:].rearrange("p t s d u -> p (t s d u)").bitcast(BF16),
             )
 
         def copy_queries(j):
-            copy_turned(("q", j), q_turned[:, :, j * P : (j + 1) * P, :])
+            copy_turned(whole(("q", j)), q_turned[:, :, j * P : (j + 1) * P, :])
 
         def quantize_queries(half):
             cols = slice(half * HALF, (half + 1) * HALF)
@@ -191,7 +193,7 @@ def tile_archived_docs_feedback_d4_kernel(tc, docs_bytes, docs_scale, queries, n
 
         def warm_up(bank, count):
             for n in range(count):
-                nc.tensor.matmul(out=bank[:, 0:P], lhsT=ident_raw[:], rhs=ident_raw[:], start=True, stop=True)
+                nc.tensor.matmul(out=bank, lhsT=ident_raw[:], rhs=ident_raw[:], start=True, stop=True)
 
         def open_scores(g, t, tag):
             score_bank[(g, t)] = psum.tile([P, B], F32, name=tag, tag=tag)
@@ -199,12 +201,12 @@ def tile_archived_docs_feedback_d4_kernel(tc, docs_bytes, docs_scale, queries, n
 
         def scores(g, t, tag):
             bank = score_bank[(g, t)] if (g, t) in score_bank else open_scores(g, t, tag)
-            codes, scales = doc_codes[(g, t)]
             for s in range(K_PASSES):
+                codes, scales = doc_codes[((g, t), s)]
                 nc.tensor.matmul_mx(
                     out=bank[:],
-                    lhsT=codes[:, s * P : (s + 1) * P].bitcast(FP8X4),
-                    lhsT_scale=scales[:, s * P : (s + 1) * P],
+                    lhsT=codes.bitcast(FP8X4),
+                    lhsT_scale=scales,
                     rhs=q_codes[:, s, :].bitcast(FP8X4),
                     rhs_scale=q_scales[:, s, :],
                     start=(s == 0),
@@ -279,10 +281,9 @@ def tile_archived_docs_feedback_d4_kernel(tc, docs_bytes, docs_scale, queries, n
             for t in (t0, t0 + 1):
                 relevance(g, t)
 
-        def turn_pair(g, t0):
-            for t in (t0, t0 + 1):
-                transpose((g, t), turn_tag(t))
-            copy_docs([(g, t0), (g, t0 + 1)])
+        def staggered(g):
+            banks = [tuple(((g, t), s) for t, s in pair) for pair in BANK_HALVES]
+            return [(banks[0],), (banks[1], banks[2]), (banks[3],)]
 
         def early(g):
             return 2 * g
@@ -291,97 +292,104 @@ def tile_archived_docs_feedback_d4_kernel(tc, docs_bytes, docs_scale, queries, n
             return 2 * g + 1
 
         sum_tags = [sum_tag(j, first) for j in range(2) for first in range(0, N, N_TILE)]
+        first_pair = (whole((0, 0)), whole((0, 1)))
+        second_pair = (whole((0, 2)), whole((0, 3)))
+        pieces = {1: [(whole((1, 0)),), (whole((1, 1)),), (whole((1, 2)), whole((1, 3)))]}
         widen(0, 0)
         widen(0, 1)
-        transpose((0, 0), turn_tag(0), 4)
-        transpose((0, 1), turn_tag(1))
+        turn(whole((0, 0)), turn_tag(0), 4)
+        turn(whole((0, 1)), turn_tag(1))
         reorder_queries(0, nc.scalar.copy)
-        transpose(("q", 0), sum_tags[0])
-        copy_docs([(0, 0), (0, 1)])
+        turn(whole(("q", 0)), sum_tags[0])
+        copy_docs(first_pair, 0)
+        copy_docs(first_pair, 1)
         widen(0, 2)
         reorder_queries(1, nc.vector.tensor_copy)
-        transpose(("q", 1), sum_tags[1], 1)
+        turn(whole(("q", 1)), sum_tags[1], 1)
         reorder_queries(2, nc.scalar.copy)
         widen(0, 3)
-        transpose((0, 2), turn_tag(2))
-        transpose(("q", 2), sum_tags[2], 1)
+        turn(whole((0, 2)), turn_tag(2))
+        turn(whole(("q", 2)), sum_tags[2], 1)
         widen(1, 0)
         copy_queries(0)
         reorder_queries(3, nc.vector.tensor_copy)
-        transpose(("q", 3), sum_tags[3], 1)
-        transpose((0, 3), turn_tag(3))
+        turn(whole(("q", 3)), sum_tags[3], 1)
+        turn(whole((0, 3)), turn_tag(3))
         copy_queries(1)
         copy_queries(2)
         copy_queries(3)
-        copy_docs([(0, 2), (0, 3)])
+        copy_docs(second_pair, 0)
+        copy_docs(second_pair, 1)
         widen(1, 1)
-        turn_pair(1, 0)
-        warm_up(open_scores(0, 0, sum_tags[0]), 2)
-        quantize_docs([(0, 0), (0, 1)])
+        turn(whole((1, 0)), turn_tag(0))
+        turn(whole((1, 1)), turn_tag(1))
+        copy_docs(pieces[1][0], 0)
+        copy_docs(pieces[1][1], 0)
+        warm_up(open_scores(0, 0, sum_tags[0])[:, 0:P], 2)
+        quantize_docs(first_pair)
         quantize_queries(0)
         widen(1, 2)
         widen(1, 3)
         quantize_queries(1)
         nc.vector.reciprocal(out=inv_norms[:], in_=norms_raw[:].rearrange("p g t -> p (g t)"))
-        quantize_docs([(0, 2), (0, 3)])
-        turn_pair(1, 2)
+        quantize_docs(second_pair)
+        turn(whole((1, 2)), turn_tag(2))
+        turn(whole((1, 3)), turn_tag(3))
+        copy_docs(pieces[1][2], 0)
+        copy_docs(pieces[1][2], 1)
         score_pair(0, 0, sum_tags)
         score_pair(0, 2, sum_tags)
         relevance_pair(0, 0)
         relevance_pair(0, 2)
-        widen(2, 0)
-        widen(2, 1)
-        widen(2, 2)
-        widen(2, 3)
-        turn_pair(2, 0)
-        transpose((2, 2), turn_tag(2))
-        transpose((2, 3), turn_tag(3))
-        quantize_docs([(1, 0)])
-        quantize_docs([(1, 1)])
-        quantize_docs([(1, 2), (1, 3)])
-        interleave(early(0), nc.scalar.copy, HALF - 64, HALF)
-        interleave(early(0), nc.vector.tensor_copy, 0, HALF - 64)
-        score_pair(1, 0, sum_tags)
-        relevance_pair(1, 0)
-        copy_docs([(2, 2), (2, 3)])
-        score_pair(1, 2, sum_tags)
-        relevance_pair(1, 2)
-        widen(3, 0)
-        quantize_rel(early(0))
-        widen(3, 1)
-        widen(3, 2)
-        widen(3, 3)
-        early_passes(0, 0)
+        for t in range(PACK):
+            widen(2, t)
 
         last = GROUPS - 1
-        for g in range(2, last):
-            turn_pair(g + 1, 0)
-            interleave(early(g - 1), nc.scalar.copy, HALF - SCALAR_QUERIES, HALF)
-            turn_pair(g + 1, 2)
-            early_passes(g - 2, 1)
-            quantize_docs([(g, 0), (g, 1)])
-            quantize_docs([(g, 2), (g, 3)])
-            interleave(early(g - 1), nc.vector.tensor_copy, 0, HALF - SCALAR_QUERIES)
-            for t in range(PACK):
-                scores(g, t, turn_tag(t))
-                relevance(g, t)
+        for g in range(1, last):
+            pieces[g + 1] = staggered(g + 1)
+            slots = [(piece, i) for piece in pieces[g + 1] for i in range(len(piece))]
+            tags = sum_tags if g == 1 else [turn_tag(t) for t in range(PACK)]
+            share = SCALAR_QUERIES_FIRST if g == 1 else SCALAR_QUERIES
+            for t, (piece, i) in enumerate(slots):
+                turn(piece[i], turn_tag(t))
+            for slot in slots[:2]:
+                copy_docs(*slot)
+            interleave(early(g - 1), nc.scalar.copy, HALF - share, HALF)
+            if g >= 2:
+                for slot in slots[2:]:
+                    copy_docs(*slot)
+                early_passes(g - 2, 1)
+            for piece in pieces[g][(0 if g < QA else 1):]:
+                quantize_docs(piece)
+            interleave(early(g - 1), nc.vector.tensor_copy, 0, HALF - share)
+            score_pair(g, 0, tags)
+            relevance_pair(g, 0)
+            if g == 1:
+                for slot in slots[2:]:
+                    copy_docs(*slot)
+            score_pair(g, 2, tags)
+            relevance_pair(g, 2)
             if g + 2 < GROUPS:
                 widen(g + 2, 0)
                 quantize_rel(early(g - 1))
-                for t in range(1, PACK):
-                    widen(g + 2, t)
+                widen(g + 2, 1)
+                widen(g + 2, 2)
+                if g + 1 >= QA:
+                    quantize_docs(pieces[g + 1][0])
+                widen(g + 2, 3)
             else:
                 interleave(late(0), nc.vector.tensor_copy, 0, HALF)
                 quantize_rel(early(g - 1))
                 interleave(late(1), nc.vector.tensor_copy, 0, HALF)
+                quantize_docs(pieces[g + 1][0])
                 quantize_rel(late(0))
                 quantize_rel(late(1))
             early_passes(g - 1, 0)
 
         interleave(late(2), nc.scalar.copy, 0, HALF)
         early_passes(last - 2, 1)
-        quantize_docs([(last, 0), (last, 1)])
-        quantize_docs([(last, 2), (last, 3)])
+        for piece in pieces[last][1:]:
+            quantize_docs(piece)
         interleave(early(last - 1), nc.vector.tensor_copy, 0, HALF)
         for t in range(PACK):
             scores(last, t, turn_tag(t))

@@ -27,13 +27,13 @@ RUN = 16
 Q_TILES = B // P
 N_TILE = 512
 HALF = B // 2
-HALVES = 2 * GROUPS
+EARLY, LATE = 0, 1
 
-TURN_BANKS = 4
-BANK_HALVES = [((0, 0), (1, 0)), ((0, 1), (2, 0)), ((1, 1), (3, 0)), ((2, 1), (3, 1))]
-QA = 4
-SCALAR_QUERIES_FIRST = 64
-SCALAR_QUERIES = 16
+BANK_SLABS = [((0, 0), (1, 0)), ((0, 1), (2, 0)), ((1, 1), (3, 0)), ((2, 1), (3, 1))]
+FIRST_PIECE_AHEAD_FROM = 4
+SCALAR_QUERIES = 64
+FIRST_WARM_UPS = 4
+LAST_WIDTHS = [2 * P, P, P]
 
 
 def tile_archived_docs_feedback_d4_kernel(tc, docs_bytes, docs_scale, queries, norms, v_words, v_scales, out):
@@ -62,7 +62,13 @@ def tile_archived_docs_feedback_d4_kernel(tc, docs_bytes, docs_scale, queries, n
             tile = keep.tile([P, count, K], U8, name="doc_bytes_%d_%d" % (g, t0), align_bytes=64)
             nc.sync.dma_start(out=tile[:], in_=docs_rows[g, :, t0 : t0 + count, :])
             for i in range(count):
-                doc_bytes[(g, t0 + i)] = tile[:, i, :]
+                for s in range(K_PASSES):
+                    doc_bytes[(g, t0 + i, s)] = tile[:, i, s * PASS : (s + 1) * PASS]
+
+        def load_slab(g, t, s):
+            tile = keep.tile([P, PASS], U8, name="doc_bytes_%d_%d_%d" % (g, t, s), align_bytes=64)
+            nc.sync.dma_start(out=tile[:], in_=docs_rows[g, :, t, s * PASS : (s + 1) * PASS])
+            doc_bytes[(g, t, s)] = tile[:]
 
         def load_scales(g0, g1, queue):
             tile = keep.tile([P, g1 - g0, PACK * SCALE_BLOCKS], F32, name="doc_scale_%d" % g0)
@@ -84,7 +90,8 @@ def tile_archived_docs_feedback_d4_kernel(tc, docs_bytes, docs_scale, queries, n
         norms_raw = keep.tile([P, GROUPS, PACK], BF16, name="norms_raw")
         load_scales(0, 1, nc.scalar)
         nc.scalar.activation(out=ident[:], in_=ident_raw[:], func=ACT.Relu)
-        load_docs(0, 0, 1)
+        load_slab(0, 0, 0)
+        load_slab(0, 0, 1)
         load_docs(0, 1, 1)
         load_queries(0)
         load_docs(0, 2, 1)
@@ -113,11 +120,11 @@ def tile_archived_docs_feedback_d4_kernel(tc, docs_bytes, docs_scale, queries, n
         load_docs(7, 0, PACK)
 
         inv_norms = keep.tile([P, GROUPS * PACK], F32, name="inv_norms")
-        q_turned = keep.tile([P, K_PASSES, B, 2], F32, name="q_turned", align_bytes=64)
+        q_turned = [keep.tile([P, K_PASSES, HALF, 2], F32, name="q_turned_%d" % half, align_bytes=64) for half in range(2)]
         q_codes = keep.tile([P, K_PASSES, B], U32, name="q_codes", align_bytes=64)
         q_scales = keep.tile([P, K_PASSES, B], U8, name="q_scales", align_bytes=64)
 
-        reordered = {}
+        to_turn = {}
         turn_bank = {}
         turned = {}
         doc_codes = {}
@@ -128,36 +135,40 @@ def tile_archived_docs_feedback_d4_kernel(tc, docs_bytes, docs_scale, queries, n
         sums = {}
 
         def widen(g, t):
-            tile = work.tile([P, 2, K // (2 * RUN), RUN], BF16, name="wide", tag="wide", bufs=8, align_bytes=64)
-            reordered[(g, t)] = tile
             per = G // (2 * RUN)
-            for i in range(SCALE_BLOCKS):
-                col = t * SCALE_BLOCKS + i
-                dst = tile[:, :, per * i : per * (i + 1), :].rearrange("p u b r -> p b u r")
-                src = doc_bytes[(g, t)][:, G * i : G * (i + 1)].bitcast(FP8).rearrange("p (b u r) -> p b u r", u=2, r=RUN)
-                scale = doc_scale[g][:, col : col + 1]
-                nc.vector.tensor_scalar(out=dst, in0=src, scalar1=scale, scalar2=None, op0=ALU.mult)
+            in_slab = PASS // G
+            for s in range(K_PASSES):
+                tile = work.tile([P, 2, PASS // (2 * RUN), RUN], BF16, name="wide", tag="wide", bufs=16, align_bytes=64)
+                words = tile[:].rearrange("p u b r -> p (u b r)").bitcast(F32)
+                to_turn[((g, t), s)] = [words[:, u * P : (u + 1) * P] for u in range(2)]
+                for i in range(in_slab):
+                    col = t * SCALE_BLOCKS + s * in_slab + i
+                    dst = tile[:, :, per * i : per * (i + 1), :].rearrange("p u b r -> p b u r")
+                    src = doc_bytes[(g, t, s)][:, G * i : G * (i + 1)].bitcast(FP8)
+                    src = src.rearrange("p (b u r) -> p b u r", u=2, r=RUN)
+                    scale = doc_scale[g][:, col : col + 1]
+                    nc.vector.tensor_scalar(out=dst, in0=src, scalar1=scale, scalar2=None, op0=ALU.mult)
 
         def reorder_queries(j, copy):
             tile = keep.tile([P, 2, K // (2 * RUN), RUN], BF16, name="q_wide_%d" % j, align_bytes=64)
-            reordered[("q", j)] = tile
+            words = tile[:].rearrange("p u b r -> p u (b r)").bitcast(F32)
+            for s in range(K_PASSES):
+                to_turn[(("q", j), s)] = [words[:, u, s * P : (s + 1) * P] for u in range(2)]
             copy(out=tile[:], in_=q_raw[j][:].rearrange("p (b u r) -> p u b r", u=2, r=RUN))
 
-        def turn(halves, tag, warm=0):
+        def turn(slabs, tag, warm=0):
             bank = psum.tile([P, 2, 2, P], F32, name=tag, tag=tag)
-            turn_bank[halves] = bank
+            turn_bank[slabs] = bank
             warm_up(bank[:, 0, 0, :], warm)
-            for i, (key, s) in enumerate(halves):
-                words = reordered[key][:].rearrange("p u b r -> p (u b r)").bitcast(F32)
+            for i, slab in enumerate(slabs):
                 for u in range(2):
-                    first = (u * K_PASSES + s) * P
-                    nc.tensor.transpose(bank[:, i, u, :], words[:, first : first + P], ident[:])
+                    nc.tensor.transpose(bank[:, i, u, :], to_turn[slab][u], ident[:])
 
         def whole(key):
             return ((key, 0), (key, 1))
 
-        def copy_turned(halves, dst):
-            nc.scalar.copy(out=dst, in_=turn_bank[halves][:].rearrange("p s u d -> p s d u"))
+        def copy_turned(slabs, dst):
+            nc.scalar.copy(out=dst, in_=turn_bank[slabs][:].rearrange("p s u d -> p s d u"))
 
         def copy_docs(piece, i):
             if i == 0:
@@ -171,8 +182,8 @@ def tile_archived_docs_feedback_d4_kernel(tc, docs_bytes, docs_scale, queries, n
             codes = work.tile([P, width], U32, name=tag, tag=tag, bufs=4, align_bytes=64)
             tag = "doc_scales%d" % len(piece)
             scales = work.tile([P, width], U8, name=tag, tag=tag, bufs=4, align_bytes=64)
-            for i, half in enumerate([half for halves in piece for half in halves]):
-                doc_codes[half] = (codes[:, i * P : (i + 1) * P], scales[:, i * P : (i + 1) * P])
+            for i, slab in enumerate([slab for slabs in piece for slab in slabs]):
+                doc_codes[slab] = (codes[:, i * P : (i + 1) * P], scales[:, i * P : (i + 1) * P])
             nc.vector.quantize_mx(
                 out=codes[:].bitcast(FP8X4),
                 scales=scales[:],
@@ -180,7 +191,7 @@ def tile_archived_docs_feedback_d4_kernel(tc, docs_bytes, docs_scale, queries, n
             )
 
         def copy_queries(j):
-            copy_turned(whole(("q", j)), q_turned[:, :, j * P : (j + 1) * P, :])
+            copy_turned(whole(("q", j)), q_turned[j // 2][:, :, (j % 2) * P : (j % 2 + 1) * P, :])
 
         def quantize_queries(half):
             cols = slice(half * HALF, (half + 1) * HALF)
@@ -188,7 +199,7 @@ def tile_archived_docs_feedback_d4_kernel(tc, docs_bytes, docs_scale, queries, n
                 nc.vector.quantize_mx(
                     out=q_codes[:, s, cols].bitcast(FP8X4),
                     scales=q_scales[:, s, cols],
-                    in_=q_turned[:, s, cols, :].rearrange("p b u -> p (b u)").bitcast(BF16),
+                    in_=q_turned[half][:, s, :, :].rearrange("p b u -> p (b u)").bitcast(BF16),
                 )
 
         def warm_up(bank, count):
@@ -221,8 +232,8 @@ def tile_archived_docs_feedback_d4_kernel(tc, docs_bytes, docs_scale, queries, n
                 out=rel_planes[g][:, t, :], in_=score_bank[(g, t)][:], func=ACT.Relu, scale=inv_norms[:, col : col + 1]
             )
 
-        def interleave(r, copy, lo, hi):
-            g, first = r // 2, (r % 2) * HALF
+        def interleave(g, half, copy, lo=0, hi=HALF):
+            r, first = (g, half), half * HALF
             if r not in rel_packed:
                 rel_packed[r] = work.tile([P, HALF, PACK], BF16, name="rel_packed", tag="rel_packed", bufs=6, align_bytes=64)
             copy(
@@ -230,9 +241,10 @@ def tile_archived_docs_feedback_d4_kernel(tc, docs_bytes, docs_scale, queries, n
                 in_=rel_planes[g][:, :, first + lo : first + hi].rearrange("p t (c i) -> p c t i", i=4),
             )
 
-        def quantize_rel(r):
-            codes = keep.tile([P, HALF], U32, name="rel_codes_%d" % r, align_bytes=64)
-            scales = keep.tile([P, HALF], U8, name="rel_scales_%d" % r, align_bytes=64)
+        def quantize_rel(g, half):
+            r = (g, half)
+            codes = keep.tile([P, HALF], U32, name="rel_codes_%d_%d" % r, align_bytes=64)
+            scales = keep.tile([P, HALF], U8, name="rel_scales_%d_%d" % r, align_bytes=64)
             rel_codes[r] = (codes, scales)
             nc.vector.quantize_mx(
                 out=codes[:].bitcast(FP8X4), scales=scales[:], in_=rel_packed[r][:].rearrange("p b t -> p (b t)")
@@ -241,7 +253,7 @@ def tile_archived_docs_feedback_d4_kernel(tc, docs_bytes, docs_scale, queries, n
         def pool_pass(g, j, first, width, tag):
             if g == 0:
                 sums[(j, first)] = psum.tile([P, width], F32, name=tag, tag=tag)
-            codes, scales = rel_codes[2 * g + j // 2]
+            codes, scales = rel_codes[(g, j // 2)]
             cols = slice((j % 2) * P, (j % 2 + 1) * P)
             nc.tensor.matmul_mx(
                 out=sums[(j, first)][:],
@@ -258,7 +270,7 @@ def tile_archived_docs_feedback_d4_kernel(tc, docs_bytes, docs_scale, queries, n
         def store(j, first, width):
             tag = "result%d" % width
             result = work.tile([P, width], F32, name=tag, tag=tag, bufs=8 if width == N_TILE else 4)
-            copy = nc.scalar.copy if len([1 for w in stored if w == width]) % 2 == 0 else nc.vector.tensor_copy
+            copy = nc.scalar.copy if len(stored) % 2 == 0 else nc.vector.tensor_copy
             stored.append(width)
             copy(out=result[:], in_=sums[(j, first)][:])
             nc.sync.dma_start(out=out[j * P : (j + 1) * P, first : first + width], in_=result[:])
@@ -282,37 +294,34 @@ def tile_archived_docs_feedback_d4_kernel(tc, docs_bytes, docs_scale, queries, n
                 relevance(g, t)
 
         def staggered(g):
-            banks = [tuple(((g, t), s) for t, s in pair) for pair in BANK_HALVES]
+            banks = [tuple(((g, t), s) for t, s in pair) for pair in BANK_SLABS]
             return [(banks[0],), (banks[1], banks[2]), (banks[3],)]
 
-        def early(g):
-            return 2 * g
-
-        def late(g):
-            return 2 * g + 1
-
         sum_tags = [sum_tag(j, first) for j in range(2) for first in range(0, N, N_TILE)]
+        turn_tags = [turn_tag(t) for t in range(PACK)]
+        on_vector, on_scalar = nc.vector.tensor_copy, nc.scalar.copy
+
         first_pair = (whole((0, 0)), whole((0, 1)))
         second_pair = (whole((0, 2)), whole((0, 3)))
         pieces = {1: [(whole((1, 0)),), (whole((1, 1)),), (whole((1, 2)), whole((1, 3)))]}
         widen(0, 0)
         widen(0, 1)
-        turn(whole((0, 0)), turn_tag(0), 4)
+        turn(whole((0, 0)), turn_tag(0), FIRST_WARM_UPS)
         turn(whole((0, 1)), turn_tag(1))
-        reorder_queries(0, nc.scalar.copy)
+        reorder_queries(0, on_scalar)
         turn(whole(("q", 0)), sum_tags[0])
         copy_docs(first_pair, 0)
         copy_docs(first_pair, 1)
         widen(0, 2)
-        reorder_queries(1, nc.vector.tensor_copy)
+        reorder_queries(1, on_vector)
         turn(whole(("q", 1)), sum_tags[1], 1)
-        reorder_queries(2, nc.scalar.copy)
+        reorder_queries(2, on_scalar)
         widen(0, 3)
         turn(whole((0, 2)), turn_tag(2))
         turn(whole(("q", 2)), sum_tags[2], 1)
         widen(1, 0)
         copy_queries(0)
-        reorder_queries(3, nc.vector.tensor_copy)
+        reorder_queries(3, on_vector)
         turn(whole(("q", 3)), sum_tags[3], 1)
         turn(whole((0, 3)), turn_tag(3))
         copy_queries(1)
@@ -348,20 +357,20 @@ def tile_archived_docs_feedback_d4_kernel(tc, docs_bytes, docs_scale, queries, n
         for g in range(1, last):
             pieces[g + 1] = staggered(g + 1)
             slots = [(piece, i) for piece in pieces[g + 1] for i in range(len(piece))]
-            tags = sum_tags if g == 1 else [turn_tag(t) for t in range(PACK)]
-            share = SCALAR_QUERIES_FIRST if g == 1 else SCALAR_QUERIES
             for t, (piece, i) in enumerate(slots):
                 turn(piece[i], turn_tag(t))
             for slot in slots[:2]:
                 copy_docs(*slot)
-            interleave(early(g - 1), nc.scalar.copy, HALF - share, HALF)
-            if g >= 2:
+            if g == 1:
+                interleave(0, EARLY, on_scalar, HALF - SCALAR_QUERIES, HALF)
+            else:
                 for slot in slots[2:]:
                     copy_docs(*slot)
                 early_passes(g - 2, 1)
-            for piece in pieces[g][(0 if g < QA else 1):]:
+            for piece in pieces[g][(0 if g < FIRST_PIECE_AHEAD_FROM else 1) :]:
                 quantize_docs(piece)
-            interleave(early(g - 1), nc.vector.tensor_copy, 0, HALF - share)
+            interleave(g - 1, EARLY, on_vector, 0, HALF - SCALAR_QUERIES if g == 1 else HALF)
+            tags = sum_tags if g == 1 else turn_tags
             score_pair(g, 0, tags)
             relevance_pair(g, 0)
             if g == 1:
@@ -371,45 +380,46 @@ def tile_archived_docs_feedback_d4_kernel(tc, docs_bytes, docs_scale, queries, n
             relevance_pair(g, 2)
             if g + 2 < GROUPS:
                 widen(g + 2, 0)
-                quantize_rel(early(g - 1))
+                quantize_rel(g - 1, EARLY)
                 widen(g + 2, 1)
                 widen(g + 2, 2)
-                if g + 1 >= QA:
+                if g + 1 >= FIRST_PIECE_AHEAD_FROM:
                     quantize_docs(pieces[g + 1][0])
                 widen(g + 2, 3)
             else:
-                interleave(late(0), nc.vector.tensor_copy, 0, HALF)
-                quantize_rel(early(g - 1))
-                interleave(late(1), nc.vector.tensor_copy, 0, HALF)
+                interleave(0, LATE, on_vector)
                 quantize_docs(pieces[g + 1][0])
-                quantize_rel(late(0))
-                quantize_rel(late(1))
+                quantize_rel(g - 1, EARLY)
+                interleave(1, LATE, on_vector)
+                quantize_rel(0, LATE)
+                quantize_rel(1, LATE)
             early_passes(g - 1, 0)
 
-        interleave(late(2), nc.scalar.copy, 0, HALF)
+        interleave(2, LATE, on_scalar)
         early_passes(last - 2, 1)
         for piece in pieces[last][1:]:
             quantize_docs(piece)
-        interleave(early(last - 1), nc.vector.tensor_copy, 0, HALF)
+        interleave(last - 1, EARLY, on_vector)
         for t in range(PACK):
             scores(last, t, turn_tag(t))
             relevance(last, t)
-        interleave(late(3), nc.vector.tensor_copy, 0, HALF)
-        quantize_rel(early(last - 1))
+        interleave(3, LATE, on_vector)
+        quantize_rel(last - 1, EARLY)
         early_passes(last - 1, 0)
         early_passes(last - 1, 1)
-        quantize_rel(late(2))
-        interleave(late(4), nc.vector.tensor_copy, 0, HALF)
-        quantize_rel(late(3))
-        interleave(late(5), nc.scalar.copy, 0, HALF)
-        interleave(late(6), nc.vector.tensor_copy, 0, HALF)
-        quantize_rel(late(4))
-        interleave(early(last), nc.vector.tensor_copy, 0, HALF)
-        quantize_rel(late(5))
-        quantize_rel(late(6))
-        interleave(late(last), nc.scalar.copy, 0, HALF)
-        quantize_rel(early(last))
-        quantize_rel(late(last))
+        quantize_rel(2, LATE)
+        interleave(4, LATE, on_vector)
+        quantize_rel(3, LATE)
+        interleave(5, LATE, on_scalar)
+        interleave(6, LATE, on_vector)
+        quantize_rel(4, LATE)
+        interleave(last, EARLY, on_vector)
+        quantize_rel(5, LATE)
+        quantize_rel(6, LATE)
+        interleave(last, LATE, on_scalar)
+        quantize_rel(last, EARLY)
+        quantize_rel(last, LATE)
+
         for g in range(last):
             for first in range(0, N, N_TILE):
                 pool_pass(g, 2, first, N_TILE, turn_tag(first // N_TILE))
@@ -424,8 +434,8 @@ def tile_archived_docs_feedback_d4_kernel(tc, docs_bytes, docs_scale, queries, n
             pool_pass(g, 3, 0, N_TILE, turn_tag(2))
         store(3, 0, N_TILE)
         first = N_TILE
-        for piece, width in enumerate([2 * P, P, P]):
+        for i, width in enumerate(LAST_WIDTHS):
             for g in range(GROUPS):
-                pool_pass(g, 3, first, width, "acc%d" % piece)
+                pool_pass(g, 3, first, width, sum_tags[i])
             store(3, first, width)
             first = first + width

@@ -31,7 +31,8 @@ EARLY, LATE = 0, 1
 
 BANK_SLABS = [((0, 0), (1, 0)), ((0, 1), (2, 0)), ((1, 1), (3, 0)), ((2, 1), (3, 1))]
 FIRST_PIECE_AHEAD_FROM = 4
-SCALAR_QUERIES = 64
+SCALAR_QUERIES = 32
+SCALAR_QUERIES_FIRST = 64
 FIRST_WARM_UPS = 4
 LAST_WIDTHS = [2 * P, P, P]
 
@@ -361,15 +362,15 @@ def tile_archived_docs_feedback_d4_kernel(tc, docs_bytes, docs_scale, queries, n
                 turn(piece[i], turn_tag(t))
             for slot in slots[:2]:
                 copy_docs(*slot)
-            if g == 1:
-                interleave(0, EARLY, on_scalar, HALF - SCALAR_QUERIES, HALF)
-            else:
+            split = HALF - (SCALAR_QUERIES_FIRST if g == 1 else SCALAR_QUERIES)
+            interleave(g - 1, EARLY, on_scalar, split, HALF)
+            if g > 1:
                 for slot in slots[2:]:
                     copy_docs(*slot)
                 early_passes(g - 2, 1)
             for piece in pieces[g][(0 if g < FIRST_PIECE_AHEAD_FROM else 1) :]:
                 quantize_docs(piece)
-            interleave(g - 1, EARLY, on_vector, 0, HALF - SCALAR_QUERIES if g == 1 else HALF)
+            interleave(g - 1, EARLY, on_vector, 0, split)
             tags = sum_tags if g == 1 else turn_tags
             score_pair(g, 0, tags)
             relevance_pair(g, 0)
@@ -390,23 +391,23 @@ def tile_archived_docs_feedback_d4_kernel(tc, docs_bytes, docs_scale, queries, n
                 interleave(0, LATE, on_vector)
                 quantize_docs(pieces[g + 1][0])
                 quantize_rel(g - 1, EARLY)
-                interleave(1, LATE, on_vector)
                 quantize_rel(0, LATE)
-                quantize_rel(1, LATE)
             early_passes(g - 1, 0)
 
         interleave(2, LATE, on_scalar)
         early_passes(last - 2, 1)
-        for piece in pieces[last][1:]:
-            quantize_docs(piece)
+        quantize_docs(pieces[last][1])
+        interleave(1, LATE, on_vector)
+        quantize_docs(pieces[last][2])
         interleave(last - 1, EARLY, on_vector)
+        quantize_rel(1, LATE)
+        quantize_rel(last - 1, EARLY)
         for t in range(PACK):
             scores(last, t, turn_tag(t))
             relevance(last, t)
-        interleave(3, LATE, on_vector)
-        quantize_rel(last - 1, EARLY)
         early_passes(last - 1, 0)
         early_passes(last - 1, 1)
+        interleave(3, LATE, on_vector)
         quantize_rel(2, LATE)
         interleave(4, LATE, on_vector)
         quantize_rel(3, LATE)

@@ -31,8 +31,6 @@ EARLY, LATE = 0, 1
 
 BANK_SLABS = [((0, 0), (1, 0)), ((0, 1), (2, 0)), ((1, 1), (3, 0)), ((2, 1), (3, 1))]
 FIRST_PIECE_AHEAD_FROM = 4
-SCALAR_QUERIES = 32
-SCALAR_QUERIES_FIRST = 64
 FIRST_WARM_UPS = 4
 LAST_WIDTHS = [2 * P, P, P]
 
@@ -174,15 +172,15 @@ def tile_archived_docs_feedback_d4_kernel(tc, docs_bytes, docs_scale, queries, n
         def copy_docs(piece, i):
             if i == 0:
                 tag = "turned%d" % len(piece)
-                turned[piece] = work.tile([P, len(piece), 2, P, 2], F32, name=tag, tag=tag, bufs=4, align_bytes=64)
+                turned[piece] = work.tile([P, len(piece), 2, P, 2], F32, name=tag, tag=tag, bufs=6 // len(piece), align_bytes=64)
             copy_turned(piece[i], turned[piece][:, i, :, :, :])
 
         def quantize_docs(piece):
             width = 2 * len(piece) * P
             tag = "doc_codes%d" % len(piece)
-            codes = work.tile([P, width], U32, name=tag, tag=tag, bufs=4, align_bytes=64)
+            codes = work.tile([P, width], U32, name=tag, tag=tag, bufs=6, align_bytes=64)
             tag = "doc_scales%d" % len(piece)
-            scales = work.tile([P, width], U8, name=tag, tag=tag, bufs=4, align_bytes=64)
+            scales = work.tile([P, width], U8, name=tag, tag=tag, bufs=6, align_bytes=64)
             for i, slab in enumerate([slab for slabs in piece for slab in slabs]):
                 doc_codes[slab] = (codes[:, i * P : (i + 1) * P], scales[:, i * P : (i + 1) * P])
             nc.vector.quantize_mx(
@@ -233,13 +231,12 @@ def tile_archived_docs_feedback_d4_kernel(tc, docs_bytes, docs_scale, queries, n
                 out=rel_planes[g][:, t, :], in_=score_bank[(g, t)][:], func=ACT.Relu, scale=inv_norms[:, col : col + 1]
             )
 
-        def interleave(g, half, copy, lo=0, hi=HALF):
-            r, first = (g, half), half * HALF
-            if r not in rel_packed:
-                rel_packed[r] = work.tile([P, HALF, PACK], BF16, name="rel_packed", tag="rel_packed", bufs=6, align_bytes=64)
+        def interleave(g, half, copy):
+            tile = work.tile([P, HALF, PACK], BF16, name="rel_packed", tag="rel_packed", bufs=6, align_bytes=64)
+            rel_packed[(g, half)] = tile
             copy(
-                out=rel_packed[r][:, lo:hi, :].rearrange("p (c i) t -> p c t i", i=4),
-                in_=rel_planes[g][:, :, first + lo : first + hi].rearrange("p t (c i) -> p c t i", i=4),
+                out=tile[:].rearrange("p (c i) t -> p c t i", i=4),
+                in_=rel_planes[g][:, :, half * HALF : (half + 1) * HALF].rearrange("p t (c i) -> p c t i", i=4),
             )
 
         def quantize_rel(g, half):
@@ -304,7 +301,7 @@ def tile_archived_docs_feedback_d4_kernel(tc, docs_bytes, docs_scale, queries, n
 
         first_pair = (whole((0, 0)), whole((0, 1)))
         second_pair = (whole((0, 2)), whole((0, 3)))
-        pieces = {1: [(whole((1, 0)),), (whole((1, 1)),), (whole((1, 2)), whole((1, 3)))]}
+        pieces = {1: [(bank,) for piece in staggered(1) for bank in piece]}
         widen(0, 0)
         widen(0, 1)
         turn(whole((0, 0)), turn_tag(0), FIRST_WARM_UPS)
@@ -331,10 +328,8 @@ def tile_archived_docs_feedback_d4_kernel(tc, docs_bytes, docs_scale, queries, n
         copy_docs(second_pair, 0)
         copy_docs(second_pair, 1)
         widen(1, 1)
-        turn(whole((1, 0)), turn_tag(0))
-        turn(whole((1, 1)), turn_tag(1))
+        turn(pieces[1][0][0], turn_tag(0))
         copy_docs(pieces[1][0], 0)
-        copy_docs(pieces[1][1], 0)
         warm_up(open_scores(0, 0, sum_tags[0])[:, 0:P], 2)
         quantize_docs(first_pair)
         quantize_queries(0)
@@ -343,10 +338,9 @@ def tile_archived_docs_feedback_d4_kernel(tc, docs_bytes, docs_scale, queries, n
         quantize_queries(1)
         nc.vector.reciprocal(out=inv_norms[:], in_=norms_raw[:].rearrange("p g t -> p (g t)"))
         quantize_docs(second_pair)
-        turn(whole((1, 2)), turn_tag(2))
-        turn(whole((1, 3)), turn_tag(3))
-        copy_docs(pieces[1][2], 0)
-        copy_docs(pieces[1][2], 1)
+        for t in range(1, PACK):
+            turn(pieces[1][t][0], turn_tag(t))
+            copy_docs(pieces[1][t], 0)
         score_pair(0, 0, sum_tags)
         score_pair(0, 2, sum_tags)
         relevance_pair(0, 0)
@@ -362,15 +356,13 @@ def tile_archived_docs_feedback_d4_kernel(tc, docs_bytes, docs_scale, queries, n
                 turn(piece[i], turn_tag(t))
             for slot in slots[:2]:
                 copy_docs(*slot)
-            split = HALF - (SCALAR_QUERIES_FIRST if g == 1 else SCALAR_QUERIES)
-            interleave(g - 1, EARLY, on_scalar, split, HALF)
             if g > 1:
                 for slot in slots[2:]:
                     copy_docs(*slot)
                 early_passes(g - 2, 1)
             for piece in pieces[g][(0 if g < FIRST_PIECE_AHEAD_FROM else 1) :]:
                 quantize_docs(piece)
-            interleave(g - 1, EARLY, on_vector, 0, split)
+            interleave(g - 1, EARLY, on_vector)
             tags = sum_tags if g == 1 else turn_tags
             score_pair(g, 0, tags)
             relevance_pair(g, 0)
@@ -411,11 +403,11 @@ def tile_archived_docs_feedback_d4_kernel(tc, docs_bytes, docs_scale, queries, n
         quantize_rel(2, LATE)
         interleave(4, LATE, on_vector)
         quantize_rel(3, LATE)
-        interleave(5, LATE, on_scalar)
-        interleave(6, LATE, on_vector)
+        interleave(6, LATE, on_scalar)
+        interleave(5, LATE, on_vector)
         quantize_rel(4, LATE)
-        interleave(last, EARLY, on_vector)
         quantize_rel(5, LATE)
+        interleave(last, EARLY, on_vector)
         quantize_rel(6, LATE)
         interleave(last, LATE, on_scalar)
         quantize_rel(last, EARLY)

@@ -235,8 +235,8 @@ def tile_archived_docs_feedback_d4_kernel(tc, docs_bytes, docs_scale, queries, n
             tile = work.tile([P, HALF, PACK], BF16, name="rel_packed", tag="rel_packed", bufs=6, align_bytes=64)
             rel_packed[(g, half)] = tile
             copy(
-                out=tile[:].rearrange("p (c i) t -> p c t i", i=4),
-                in_=rel_planes[g][:, :, half * HALF : (half + 1) * HALF].rearrange("p t (c i) -> p c t i", i=4),
+                out=tile[:].rearrange("p (c i) t -> p c t i", i=8),
+                in_=rel_planes[g][:, :, half * HALF : (half + 1) * HALF].rearrange("p t (c i) -> p c t i", i=8),
             )
 
         def quantize_rel(g, half):

@@ -31,7 +31,8 @@ EARLY, LATE = 0, 1
 
 BANK_SLABS = [((0, 0), (1, 0)), ((0, 1), (2, 0)), ((1, 1), (3, 0)), ((2, 1), (3, 1))]
 FIRST_PIECE_AHEAD_FROM = 4
-FIRST_WARM_UPS = 4
+FIRST_WARM_UPS = 3
+LATE_BEFORE_CLOSE = 4
 LAST_WIDTHS = [2 * P, P, P]
 
 
@@ -155,10 +156,12 @@ def tile_archived_docs_feedback_d4_kernel(tc, docs_bytes, docs_scale, queries, n
                 to_turn[(("q", j), s)] = [words[:, u, s * P : (s + 1) * P] for u in range(2)]
             copy(out=tile[:], in_=q_raw[j][:].rearrange("p (b u r) -> p u b r", u=2, r=RUN))
 
-        def turn(slabs, tag, warm=0):
-            bank = psum.tile([P, 2, 2, P], F32, name=tag, tag=tag)
-            turn_bank[slabs] = bank
-            warm_up(bank[:, 0, 0, :], warm)
+        def open_turn(slabs, tag):
+            turn_bank[slabs] = psum.tile([P, 2, 2, P], F32, name=tag, tag=tag)
+            return turn_bank[slabs]
+
+        def turn(slabs, tag):
+            bank = turn_bank[slabs] if slabs in turn_bank else open_turn(slabs, tag)
             for i, slab in enumerate(slabs):
                 for u in range(2):
                     nc.tensor.transpose(bank[:, i, u, :], to_turn[slab][u], ident[:])
@@ -201,9 +204,9 @@ def tile_archived_docs_feedback_d4_kernel(tc, docs_bytes, docs_scale, queries, n
                     in_=q_turned[half][:, s, :, :].rearrange("p b u -> p (b u)").bitcast(BF16),
                 )
 
-        def warm_up(bank, count):
-            for n in range(count):
-                nc.tensor.matmul(out=bank, lhsT=ident_raw[:], rhs=ident_raw[:], start=True, stop=True)
+        def warm_up(bank, slots):
+            for n in slots:
+                nc.tensor.matmul(out=bank[:, n * P : (n + 1) * P], lhsT=ident_raw[:], rhs=ident_raw[:], start=True, stop=True)
 
         def open_scores(g, t, tag):
             score_bank[(g, t)] = psum.tile([P, B], F32, name=tag, tag=tag)
@@ -263,15 +266,12 @@ def tile_archived_docs_feedback_d4_kernel(tc, docs_bytes, docs_scale, queries, n
                 stop=(g == GROUPS - 1),
             )
 
-        stored = []
-
-        def store(j, first, width):
+        def store(j, first, width, copy):
             tag = "result%d" % width
             result = work.tile([P, width], F32, name=tag, tag=tag, bufs=8 if width == N_TILE else 4)
-            copy = nc.scalar.copy if len(stored) % 2 == 0 else nc.vector.tensor_copy
-            stored.append(width)
             copy(out=result[:], in_=sums[(j, first)][:])
-            nc.sync.dma_start(out=out[j * P : (j + 1) * P, first : first + width], in_=result[:])
+            queue = nc.scalar if (j, first + width) == (Q_TILES - 1, N) else nc.sync
+            queue.dma_start(out=out[j * P : (j + 1) * P, first : first + width], in_=result[:])
 
         def turn_tag(t):
             return "rot%d" % t
@@ -304,7 +304,9 @@ def tile_archived_docs_feedback_d4_kernel(tc, docs_bytes, docs_scale, queries, n
         pieces = {1: [(bank,) for piece in staggered(1) for bank in piece]}
         widen(0, 0)
         widen(0, 1)
-        turn(whole((0, 0)), turn_tag(0), FIRST_WARM_UPS)
+        spare = open_turn(whole(("q", 3)), sum_tags[3])[:].rearrange("p s u d -> p (s u d)")
+        warm_up(spare, range(FIRST_WARM_UPS))
+        turn(whole((0, 0)), turn_tag(0))
         turn(whole((0, 1)), turn_tag(1))
         reorder_queries(0, on_scalar)
         turn(whole(("q", 0)), sum_tags[0])
@@ -312,15 +314,17 @@ def tile_archived_docs_feedback_d4_kernel(tc, docs_bytes, docs_scale, queries, n
         copy_docs(first_pair, 1)
         widen(0, 2)
         reorder_queries(1, on_vector)
-        turn(whole(("q", 1)), sum_tags[1], 1)
+        warm_up(spare, [3])
+        turn(whole(("q", 1)), sum_tags[1])
         reorder_queries(2, on_scalar)
         widen(0, 3)
         turn(whole((0, 2)), turn_tag(2))
-        turn(whole(("q", 2)), sum_tags[2], 1)
+        warm_up(spare, [2])
+        turn(whole(("q", 2)), sum_tags[2])
         widen(1, 0)
         copy_queries(0)
         reorder_queries(3, on_vector)
-        turn(whole(("q", 3)), sum_tags[3], 1)
+        turn(whole(("q", 3)), sum_tags[3])
         turn(whole((0, 3)), turn_tag(3))
         copy_queries(1)
         copy_queries(2)
@@ -330,7 +334,7 @@ def tile_archived_docs_feedback_d4_kernel(tc, docs_bytes, docs_scale, queries, n
         widen(1, 1)
         turn(pieces[1][0][0], turn_tag(0))
         copy_docs(pieces[1][0], 0)
-        warm_up(open_scores(0, 0, sum_tags[0])[:, 0:P], 2)
+        warm_up(open_scores(0, 0, sum_tags[0])[:], range(2))
         quantize_docs(first_pair)
         quantize_queries(0)
         widen(1, 2)
@@ -386,49 +390,48 @@ def tile_archived_docs_feedback_d4_kernel(tc, docs_bytes, docs_scale, queries, n
                 quantize_rel(0, LATE)
             early_passes(g - 1, 0)
 
-        interleave(2, LATE, on_scalar)
-        early_passes(last - 2, 1)
         quantize_docs(pieces[last][1])
         interleave(1, LATE, on_vector)
         quantize_docs(pieces[last][2])
-        interleave(last - 1, EARLY, on_vector)
-        quantize_rel(1, LATE)
-        quantize_rel(last - 1, EARLY)
+        interleave(2, LATE, on_vector)
         for t in range(PACK):
             scores(last, t, turn_tag(t))
             relevance(last, t)
-        early_passes(last - 1, 0)
-        early_passes(last - 1, 1)
-        interleave(3, LATE, on_vector)
+        interleave(last - 1, EARLY, on_vector)
+        quantize_rel(1, LATE)
+        quantize_rel(last - 1, EARLY)
         quantize_rel(2, LATE)
-        interleave(4, LATE, on_vector)
-        quantize_rel(3, LATE)
-        interleave(6, LATE, on_scalar)
-        interleave(5, LATE, on_vector)
-        quantize_rel(4, LATE)
-        quantize_rel(5, LATE)
+        early_passes(last - 2, 1)
+        interleave(3, LATE, on_vector)
         interleave(last, EARLY, on_vector)
-        quantize_rel(6, LATE)
-        interleave(last, LATE, on_scalar)
+        quantize_rel(3, LATE)
         quantize_rel(last, EARLY)
-        quantize_rel(last, LATE)
+        interleave(5, LATE, on_scalar)
+        interleave(last, LATE, on_scalar)
+        for g in (4, 6):
+            interleave(g, LATE, on_vector)
+            quantize_rel(g + 1, LATE)
+            quantize_rel(g, LATE)
 
-        for g in range(last):
+        for g in range(GROUPS):
+            if g == 1:
+                early_passes(last - 1, 0)
+                early_passes(last - 1, 1)
+            if g == LATE_BEFORE_CLOSE:
+                for j in range(2):
+                    early_passes(last, j)
+                    for first in range(0, N, N_TILE):
+                        store(j, first, N_TILE, on_scalar)
             for first in range(0, N, N_TILE):
                 pool_pass(g, 2, first, N_TILE, turn_tag(first // N_TILE))
-        for j in range(2):
-            early_passes(last, j)
-            for first in range(0, N, N_TILE):
-                store(j, first, N_TILE)
-        for first in range(0, N, N_TILE):
-            pool_pass(last, 2, first, N_TILE, turn_tag(first // N_TILE))
-            store(2, first, N_TILE)
+        store(2, 0, N_TILE, on_vector)
+        store(2, N_TILE, N_TILE, on_scalar)
         for g in range(GROUPS):
             pool_pass(g, 3, 0, N_TILE, turn_tag(2))
-        store(3, 0, N_TILE)
+        store(3, 0, N_TILE, on_scalar)
         first = N_TILE
         for i, width in enumerate(LAST_WIDTHS):
             for g in range(GROUPS):
                 pool_pass(g, 3, first, width, sum_tags[i])
-            store(3, first, width)
+            store(3, first, width, on_scalar)
             first = first + width

@@ -32,6 +32,7 @@ EARLY, LATE = 0, 1
 BANK_SLABS = [((0, 0), (1, 0)), ((0, 1), (2, 0)), ((1, 1), (3, 0)), ((2, 1), (3, 1))]
 FIRST_PIECE_AHEAD_FROM = 4
 FIRST_WARM_UPS = 3
+SHARE = 80
 LATE_BEFORE_CLOSE = 4
 LAST_WIDTHS = [2 * P, P, P]
 
@@ -93,13 +94,13 @@ def tile_archived_docs_feedback_d4_kernel(tc, docs_bytes, docs_scale, queries, n
         load_slab(0, 0, 0)
         load_slab(0, 0, 1)
         load_docs(0, 1, 1)
-        load_queries(0)
         load_docs(0, 2, 1)
-        load_queries(1)
+        load_queries(0)
         load_docs(0, 3, 1)
-        load_queries(2)
+        load_queries(1)
         load_scales(1, 2, nc.sync)
         load_docs(1, 0, 1)
+        load_queries(2)
         load_queries(3)
         load_docs(1, 1, 1)
         load_docs(1, 2, 2)
@@ -134,10 +135,10 @@ def tile_archived_docs_feedback_d4_kernel(tc, docs_bytes, docs_scale, queries, n
         rel_codes = {}
         sums = {}
 
-        def widen(g, t):
+        def widen(g, t, slabs=range(K_PASSES)):
             per = G // (2 * RUN)
             in_slab = PASS // G
-            for s in range(K_PASSES):
+            for s in slabs:
                 tile = work.tile([P, 2, PASS // (2 * RUN), RUN], BF16, name="wide", tag="wide", bufs=16, align_bytes=64)
                 words = tile[:].rearrange("p u b r -> p (u b r)").bitcast(F32)
                 to_turn[((g, t), s)] = [words[:, u * P : (u + 1) * P] for u in range(2)]
@@ -148,6 +149,24 @@ def tile_archived_docs_feedback_d4_kernel(tc, docs_bytes, docs_scale, queries, n
                     src = src.rearrange("p (b u r) -> p b u r", u=2, r=RUN)
                     scale = doc_scale[g][:, col : col + 1]
                     nc.vector.tensor_scalar(out=dst, in0=src, scalar1=scale, scalar2=None, op0=ALU.mult)
+
+        def widen_on_scalar(g, t, s):
+            plain = keep.tile([P, PASS], BF16, name="plain", align_bytes=64)
+            for i in range(PASS // G):
+                col = t * SCALE_BLOCKS + s * (PASS // G) + i
+                nc.scalar.activation(
+                    out=plain[:, G * i : G * (i + 1)],
+                    in_=doc_bytes[(g, t, s)][:, G * i : G * (i + 1)].bitcast(FP8),
+                    func=ACT.Copy,
+                    scale=doc_scale[g][:, col : col + 1],
+                )
+            tile = keep.tile([P, 2, PASS // (2 * RUN), RUN], BF16, name="wide_by_scalar", align_bytes=64)
+            words = tile[:].rearrange("p u b r -> p (u b r)").bitcast(F32)
+            to_turn[((g, t), s)] = [words[:, u * P : (u + 1) * P] for u in range(2)]
+            return tile, plain
+
+        def reorder_plain(tile, plain):
+            nc.scalar.copy(out=tile[:], in_=plain[:].rearrange("p (b u r) -> p u b r", u=2, r=RUN))
 
         def reorder_queries(j, copy):
             tile = keep.tile([P, 2, K // (2 * RUN), RUN], BF16, name="q_wide_%d" % j, align_bytes=64)
@@ -234,12 +253,13 @@ def tile_archived_docs_feedback_d4_kernel(tc, docs_bytes, docs_scale, queries, n
                 out=rel_planes[g][:, t, :], in_=score_bank[(g, t)][:], func=ACT.Relu, scale=inv_norms[:, col : col + 1]
             )
 
-        def interleave(g, half, copy):
-            tile = work.tile([P, HALF, PACK], BF16, name="rel_packed", tag="rel_packed", bufs=6, align_bytes=64)
-            rel_packed[(g, half)] = tile
+        def interleave(g, half, copy, lo=0, hi=HALF):
+            if (g, half) not in rel_packed:
+                rel_packed[(g, half)] = work.tile([P, HALF, PACK], BF16, name="rel_packed", tag="rel_packed", bufs=6, align_bytes=64)
+            tile = rel_packed[(g, half)]
             copy(
-                out=tile[:].rearrange("p (c i) t -> p c t i", i=8),
-                in_=rel_planes[g][:, :, half * HALF : (half + 1) * HALF].rearrange("p t (c i) -> p c t i", i=8),
+                out=tile[:, lo:hi, :].rearrange("p (c i) t -> p c t i", i=8),
+                in_=rel_planes[g][:, :, half * HALF + lo : half * HALF + hi].rearrange("p t (c i) -> p c t i", i=8),
             )
 
         def quantize_rel(g, half):
@@ -268,7 +288,7 @@ def tile_archived_docs_feedback_d4_kernel(tc, docs_bytes, docs_scale, queries, n
 
         def store(j, first, width, copy):
             tag = "result%d" % width
-            result = work.tile([P, width], F32, name=tag, tag=tag, bufs=8 if width == N_TILE else 4)
+            result = work.tile([P, width], F32, name=tag, tag=tag, bufs=7 if width == N_TILE else 2)
             copy(out=result[:], in_=sums[(j, first)][:])
             queue = nc.scalar if (j, first + width) == (Q_TILES - 1, N) else nc.sync
             queue.dma_start(out=out[j * P : (j + 1) * P, first : first + width], in_=result[:])
@@ -303,41 +323,44 @@ def tile_archived_docs_feedback_d4_kernel(tc, docs_bytes, docs_scale, queries, n
         second_pair = (whole((0, 2)), whole((0, 3)))
         pieces = {1: [(bank,) for piece in staggered(1) for bank in piece]}
         widen(0, 0)
-        widen(0, 1)
+        widen(0, 1, [0])
+        by_scalar = widen_on_scalar(0, 1, 1)
+        reorder_plain(*by_scalar)
         spare = open_turn(whole(("q", 3)), sum_tags[3])[:].rearrange("p s u d -> p (s u d)")
         warm_up(spare, range(FIRST_WARM_UPS))
         turn(whole((0, 0)), turn_tag(0))
         turn(whole((0, 1)), turn_tag(1))
         reorder_queries(0, on_scalar)
+        warm_up(spare, [0])
         turn(whole(("q", 0)), sum_tags[0])
         copy_docs(first_pair, 0)
         copy_docs(first_pair, 1)
+        copy_queries(0)
         widen(0, 2)
+        widen(0, 3)
         reorder_queries(1, on_vector)
         warm_up(spare, [3])
-        turn(whole(("q", 1)), sum_tags[1])
-        reorder_queries(2, on_scalar)
-        widen(0, 3)
         turn(whole((0, 2)), turn_tag(2))
+        turn(whole(("q", 1)), sum_tags[1])
+        turn(whole((0, 3)), turn_tag(3))
+        reorder_queries(2, on_scalar)
+        copy_queries(1)
+        widen(1, 0)
         warm_up(spare, [2])
         turn(whole(("q", 2)), sum_tags[2])
-        widen(1, 0)
-        copy_queries(0)
+        quantize_docs(first_pair)
         reorder_queries(3, on_vector)
-        turn(whole(("q", 3)), sum_tags[3])
-        turn(whole((0, 3)), turn_tag(3))
-        copy_queries(1)
-        copy_queries(2)
-        copy_queries(3)
-        copy_docs(second_pair, 0)
-        copy_docs(second_pair, 1)
         widen(1, 1)
+        copy_docs(second_pair, 0)
+        copy_queries(2)
+        turn(whole(("q", 3)), sum_tags[3])
+        copy_queries(3)
+        copy_docs(second_pair, 1)
         turn(pieces[1][0][0], turn_tag(0))
         copy_docs(pieces[1][0], 0)
         warm_up(open_scores(0, 0, sum_tags[0])[:], range(2))
-        quantize_docs(first_pair)
-        quantize_queries(0)
         widen(1, 2)
+        quantize_queries(0)
         widen(1, 3)
         quantize_queries(1)
         nc.vector.reciprocal(out=inv_norms[:], in_=norms_raw[:].rearrange("p g t -> p (g t)"))
@@ -360,13 +383,15 @@ def tile_archived_docs_feedback_d4_kernel(tc, docs_bytes, docs_scale, queries, n
                 turn(piece[i], turn_tag(t))
             for slot in slots[:2]:
                 copy_docs(*slot)
+            if g == 1:
+                interleave(0, EARLY, on_scalar, 0, SHARE)
             if g > 1:
                 for slot in slots[2:]:
                     copy_docs(*slot)
                 early_passes(g - 2, 1)
             for piece in pieces[g][(0 if g < FIRST_PIECE_AHEAD_FROM else 1) :]:
                 quantize_docs(piece)
-            interleave(g - 1, EARLY, on_vector)
+            interleave(g - 1, EARLY, on_vector, SHARE if g == 1 else 0)
             tags = sum_tags if g == 1 else turn_tags
             score_pair(g, 0, tags)
             relevance_pair(g, 0)

@@ -34,6 +34,7 @@ FIRST_PIECE_AHEAD_FROM = 4
 FIRST_WARM_UPS = 3
 SHARE = 80
 LATE_BEFORE_CLOSE = 4
+ODD_WORDS = 351
 LAST_WIDTHS = [2 * P, P, P]
 
 
@@ -50,7 +51,10 @@ def tile_archived_docs_feedback_d4_kernel(tc, docs_bytes, docs_scale, queries, n
         ident = keep.tile([P, P], F32, name="ident")
 
         v_scale = keep.tile([P, GROUPS, N], U8, name="v_scale", align_bytes=64)
-        nc.vector.memset(v_scale[:].rearrange("p g n -> p (g n)").bitcast(I32), 0)
+        filler = v_scale[:].rearrange("p g n -> p (g n)").bitcast(I32)
+        nc.vector.memset(filler[:, 0:ODD_WORDS], 0)
+        nc.vector.memset(filler[:, ODD_WORDS : 2 * ODD_WORDS], 0)
+        nc.vector.memset(filler[:, 2 * ODD_WORDS :], 0)
 
         docs_rows = docs_bytes.rearrange("(g m t) k -> g m t k", m=P, t=PACK)
         scale_rows = docs_scale.rearrange("(g m t) i -> m g (t i)", m=P, t=PACK)

@@ -32,8 +32,8 @@ EARLY, LATE = 0, 1
 BANK_SLABS = [((0, 0), (1, 0)), ((0, 1), (2, 0)), ((1, 1), (3, 0)), ((2, 1), (3, 1))]
 FIRST_PIECE_AHEAD_FROM = 4
 FIRST_WARM_UPS = 3
-SHARE = 80
-LATE_BEFORE_CLOSE = 4
+SHARE = 48
+LATE_BEFORE_CLOSE = 3
 ODD_WORDS = 351
 LAST_WIDTHS = [2 * P, P, P]
 
@@ -92,35 +92,44 @@ def tile_archived_docs_feedback_d4_kernel(tc, docs_bytes, docs_scale, queries, n
             for g in range(g0, g1):
                 v_codes[g] = tile[:, g - g0, :]
 
-        norms_raw = keep.tile([P, GROUPS, PACK], BF16, name="norms_raw")
+        norm_rows = norms.rearrange("(g m t) -> m g t", m=P, t=PACK)
+        norms_raw = {}
+
+        def load_norms(g0, g1):
+            norms_raw[g0] = keep.tile([P, g1 - g0, PACK], BF16, name="norms_raw_%d" % g0)
+            nc.sync.dma_start(out=norms_raw[g0][:], in_=norm_rows[:, g0:g1, :])
+
+        def load_v_scales():
+            for q in range(4):
+                nc.sync.dma_start(
+                    out=v_scale[32 * q : 32 * q + 4, :, :].bitcast(I32),
+                    in_=v_scales[:, 4 * q : 4 * q + 4, :].rearrange("g r n -> r g n").bitcast(I32),
+                )
+
         load_scales(0, 1, nc.scalar)
         nc.scalar.activation(out=ident[:], in_=ident_raw[:], func=ACT.Relu)
-        load_slab(0, 0, 0)
-        load_slab(0, 0, 1)
+        load_docs(0, 0, 1)
         load_docs(0, 1, 1)
-        load_docs(0, 2, 1)
+        load_docs(0, 2, 2)
         load_queries(0)
-        load_docs(0, 3, 1)
         load_queries(1)
         load_scales(1, 2, nc.sync)
-        load_docs(1, 0, 1)
+        load_docs(1, 0, 2)
         load_queries(2)
         load_queries(3)
-        load_docs(1, 1, 1)
         load_docs(1, 2, 2)
-        nc.sync.dma_start(out=norms_raw[:], in_=norms.rearrange("(g m t) -> m g t", m=P, t=PACK))
-        load_scales(2, GROUPS, nc.sync)
-        load_docs(2, 0, PACK)
+        load_scales(2, 4, nc.sync)
+        load_docs(2, 0, 2)
+        load_norms(0, 2)
+        load_docs(2, 2, 2)
         load_docs(3, 0, PACK)
         load_v(0, 2)
-        for q in range(4):
-            nc.sync.dma_start(
-                out=v_scale[32 * q : 32 * q + 4, :, :].bitcast(I32),
-                in_=v_scales[:, 4 * q : 4 * q + 4, :].rearrange("g r n -> r g n").bitcast(I32),
-            )
+        load_v_scales()
+        load_norms(2, GROUPS)
+        load_scales(4, GROUPS, nc.sync)
         load_docs(4, 0, PACK)
-        load_docs(5, 0, PACK)
         load_v(2, GROUPS)
+        load_docs(5, 0, PACK)
         load_docs(6, 0, PACK)
         load_docs(7, 0, PACK)
 
@@ -249,6 +258,9 @@ def tile_archived_docs_feedback_d4_kernel(tc, docs_bytes, docs_scale, queries, n
                     stop=(s == K_PASSES - 1),
                 )
 
+        def invert_norms(g0, g1):
+            nc.vector.reciprocal(out=inv_norms[:, g0 * PACK : g1 * PACK], in_=norms_raw[g0][:].rearrange("p g t -> p (g t)"))
+
         def relevance(g, t):
             if t == 0:
                 rel_planes[g] = keep.tile([P, PACK, B], BF16, name="rel_planes_%d" % g, align_bytes=64)
@@ -335,7 +347,7 @@ def tile_archived_docs_feedback_d4_kernel(tc, docs_bytes, docs_scale, queries, n
         turn(whole((0, 0)), turn_tag(0))
         turn(whole((0, 1)), turn_tag(1))
         reorder_queries(0, on_scalar)
-        warm_up(spare, [0])
+        warm_up(spare, [0, 1])
         turn(whole(("q", 0)), sum_tags[0])
         copy_docs(first_pair, 0)
         copy_docs(first_pair, 1)
@@ -367,7 +379,7 @@ def tile_archived_docs_feedback_d4_kernel(tc, docs_bytes, docs_scale, queries, n
         quantize_queries(0)
         widen(1, 3)
         quantize_queries(1)
-        nc.vector.reciprocal(out=inv_norms[:], in_=norms_raw[:].rearrange("p g t -> p (g t)"))
+        invert_norms(0, 2)
         quantize_docs(second_pair)
         for t in range(1, PACK):
             turn(pieces[1][t][0], turn_tag(t))
@@ -417,6 +429,8 @@ def tile_archived_docs_feedback_d4_kernel(tc, docs_bytes, docs_scale, queries, n
                 quantize_docs(pieces[g + 1][0])
                 quantize_rel(g - 1, EARLY)
                 quantize_rel(0, LATE)
+            if g == 1:
+                invert_norms(2, GROUPS)
             early_passes(g - 1, 0)
 
         quantize_docs(pieces[last][1])
@@ -453,9 +467,12 @@ def tile_archived_docs_feedback_d4_kernel(tc, docs_bytes, docs_scale, queries, n
                         store(j, first, N_TILE, on_scalar)
             for first in range(0, N, N_TILE):
                 pool_pass(g, 2, first, N_TILE, turn_tag(first // N_TILE))
+            if 1 <= g < 6:
+                for late in range(2) if g == 1 else [g]:
+                    pool_pass(late, 3, 0, N_TILE, turn_tag(2))
         store(2, 0, N_TILE, on_vector)
         store(2, N_TILE, N_TILE, on_scalar)
-        for g in range(GROUPS):
+        for g in range(6, GROUPS):
             pool_pass(g, 3, 0, N_TILE, turn_tag(2))
         store(3, 0, N_TILE, on_scalar)
         first = N_TILE

@@ -416,6 +416,8 @@ def tile_archived_docs_feedback_d4_kernel(tc, docs_bytes, docs_scale, queries, n
                     copy_docs(*slot)
             score_pair(g, 2, tags)
             relevance_pair(g, 2)
+            if 3 <= g < last - 1:
+                interleave(0, LATE, on_scalar, SHARE * (g - 3), SHARE * (g - 2))
             if g + 2 < GROUPS:
                 widen(g + 2, 0)
                 quantize_rel(g - 1, EARLY)
@@ -425,18 +427,19 @@ def tile_archived_docs_feedback_d4_kernel(tc, docs_bytes, docs_scale, queries, n
                     quantize_docs(pieces[g + 1][0])
                 widen(g + 2, 3)
             else:
-                interleave(0, LATE, on_vector)
                 quantize_docs(pieces[g + 1][0])
                 quantize_rel(g - 1, EARLY)
-                quantize_rel(0, LATE)
+                interleave(0, LATE, on_vector, 3 * SHARE)
             if g == 1:
                 invert_norms(2, GROUPS)
             early_passes(g - 1, 0)
 
         quantize_docs(pieces[last][1])
+        quantize_rel(0, LATE)
         interleave(1, LATE, on_vector)
         quantize_docs(pieces[last][2])
-        interleave(2, LATE, on_vector)
+        interleave(2, LATE, on_scalar, 0, SHARE)
+        interleave(2, LATE, on_vector, SHARE)
         for t in range(PACK):
             scores(last, t, turn_tag(t))
             relevance(last, t)

@@ -23,18 +23,14 @@ PASS = P * PACK
 GROUPS = T // PASS
 K_PASSES = K // PASS
 SCALE_BLOCKS = K // G
-RUN = 16
 Q_TILES = B // P
 N_TILE = 512
 HALF = B // 2
 EARLY, LATE = 0, 1
-
-BANK_SLABS = [((0, 0), (1, 0)), ((0, 1), (2, 0)), ((1, 1), (3, 0)), ((2, 1), (3, 1))]
-FIRST_PIECE_AHEAD_FROM = 4
-FIRST_WARM_UPS = 3
-SHARE = 48
-LATE_BEFORE_CLOSE = 3
+AHEAD = 4
+HELD = 2
 ODD_WORDS = 351
+LATE_BEFORE_CLOSE = 3
 LAST_WIDTHS = [2 * P, P, P]
 
 
@@ -52,28 +48,29 @@ def tile_archived_docs_feedback_d4_kernel(tc, docs_bytes, docs_scale, queries, n
 
         v_scale = keep.tile([P, GROUPS, N], U8, name="v_scale", align_bytes=64)
         filler = v_scale[:].rearrange("p g n -> p (g n)").bitcast(I32)
-        nc.vector.memset(filler[:, 0:ODD_WORDS], 0)
-        nc.vector.memset(filler[:, ODD_WORDS : 2 * ODD_WORDS], 0)
-        nc.vector.memset(filler[:, 2 * ODD_WORDS :], 0)
+        words = GROUPS * N // 4
+        nc.vector.memset(filler[:, words - ODD_WORDS :], 0)
+        nc.vector.memset(filler[:, words - 2 * ODD_WORDS : words - ODD_WORDS], 0)
+        nc.vector.memset(filler[:, : words - 2 * ODD_WORDS], 0)
+        zeros = v_scale[:, GROUPS - 1, :].bitcast(BF16)
 
         docs_rows = docs_bytes.rearrange("(g m t) k -> g m t k", m=P, t=PACK)
         scale_rows = docs_scale.rearrange("(g m t) i -> m g (t i)", m=P, t=PACK)
+        norm_rows = norms.rearrange("(g m t) -> m g t", m=P, t=PACK)
+        v_scale_rows = v_scales.rearrange("g (q r) n -> r q g n", r=4)
         doc_bytes = {}
         doc_scale = {}
         q_raw = {}
         v_codes = {}
+        norms_raw = {}
 
-        def load_docs(g, t0, count):
-            tile = keep.tile([P, count, K], U8, name="doc_bytes_%d_%d" % (g, t0), align_bytes=64)
+        def load_docs(n0, count):
+            g, t0 = divmod(n0, PACK)
+            tile = keep.tile([P, count, K], U8, name="doc_bytes_%d" % n0, align_bytes=64)
             nc.sync.dma_start(out=tile[:], in_=docs_rows[g, :, t0 : t0 + count, :])
             for i in range(count):
                 for s in range(K_PASSES):
-                    doc_bytes[(g, t0 + i, s)] = tile[:, i, s * PASS : (s + 1) * PASS]
-
-        def load_slab(g, t, s):
-            tile = keep.tile([P, PASS], U8, name="doc_bytes_%d_%d_%d" % (g, t, s), align_bytes=64)
-            nc.sync.dma_start(out=tile[:], in_=docs_rows[g, :, t, s * PASS : (s + 1) * PASS])
-            doc_bytes[(g, t, s)] = tile[:]
+                    doc_bytes[(n0 + i, s)] = tile[:, i, s * PASS : (s + 1) * PASS]
 
         def load_scales(g0, g1, queue):
             tile = keep.tile([P, g1 - g0, PACK * SCALE_BLOCKS], F32, name="doc_scale_%d" % g0)
@@ -92,46 +89,36 @@ def tile_archived_docs_feedback_d4_kernel(tc, docs_bytes, docs_scale, queries, n
             for g in range(g0, g1):
                 v_codes[g] = tile[:, g - g0, :]
 
-        norm_rows = norms.rearrange("(g m t) -> m g t", m=P, t=PACK)
-        norms_raw = {}
-
         def load_norms(g0, g1):
             norms_raw[g0] = keep.tile([P, g1 - g0, PACK], BF16, name="norms_raw_%d" % g0)
             nc.sync.dma_start(out=norms_raw[g0][:], in_=norm_rows[:, g0:g1, :])
 
-        def load_v_scales():
-            for q in range(4):
+        def load_v_scales(g0, g1):
+            for r in range(4):
                 nc.sync.dma_start(
-                    out=v_scale[32 * q : 32 * q + 4, :, :].bitcast(I32),
-                    in_=v_scales[:, 4 * q : 4 * q + 4, :].rearrange("g r n -> r g n").bitcast(I32),
+                    out=v_scale[r:P:32, g0:g1, :].bitcast(I32),
+                    in_=v_scale_rows[r, :, g0:g1, :].bitcast(I32),
                 )
 
         load_scales(0, 1, nc.scalar)
         nc.scalar.activation(out=ident[:], in_=ident_raw[:], func=ACT.Relu)
-        load_docs(0, 0, 1)
-        load_docs(0, 1, 1)
-        load_docs(0, 2, 2)
+        load_docs(0, 1)
+        load_docs(2, 1)
+        load_docs(1, 1)
+        load_docs(3, 1)
+        load_scales(1, 2, nc.sync)
+        load_docs(4, 2)
         load_queries(0)
         load_queries(1)
-        load_scales(1, 2, nc.sync)
-        load_docs(1, 0, 2)
         load_queries(2)
+        load_docs(6, 2)
         load_queries(3)
-        load_docs(1, 2, 2)
         load_scales(2, 4, nc.sync)
-        load_docs(2, 0, 2)
+        load_docs(8, 2)
         load_norms(0, 2)
-        load_docs(2, 2, 2)
-        load_docs(3, 0, PACK)
-        load_v(0, 2)
-        load_v_scales()
-        load_norms(2, GROUPS)
-        load_scales(4, GROUPS, nc.sync)
-        load_docs(4, 0, PACK)
-        load_v(2, GROUPS)
-        load_docs(5, 0, PACK)
-        load_docs(6, 0, PACK)
-        load_docs(7, 0, PACK)
+        load_docs(10, 2)
+        load_docs(12, 4)
+        load_v(0, 1)
 
         inv_norms = keep.tile([P, GROUPS * PACK], F32, name="inv_norms")
         q_turned = [keep.tile([P, K_PASSES, HALF, 2], F32, name="q_turned_%d" % half, align_bytes=64) for half in range(2)]
@@ -148,45 +135,42 @@ def tile_archived_docs_feedback_d4_kernel(tc, docs_bytes, docs_scale, queries, n
         rel_codes = {}
         sums = {}
 
-        def widen(g, t, slabs=range(K_PASSES)):
-            per = G // (2 * RUN)
-            in_slab = PASS // G
-            for s in slabs:
-                tile = work.tile([P, 2, PASS // (2 * RUN), RUN], BF16, name="wide", tag="wide", bufs=16, align_bytes=64)
-                words = tile[:].rearrange("p u b r -> p (u b r)").bitcast(F32)
-                to_turn[((g, t), s)] = [words[:, u * P : (u + 1) * P] for u in range(2)]
-                for i in range(in_slab):
-                    col = t * SCALE_BLOCKS + s * in_slab + i
-                    dst = tile[:, :, per * i : per * (i + 1), :].rearrange("p u b r -> p b u r")
-                    src = doc_bytes[(g, t, s)][:, G * i : G * (i + 1)].bitcast(FP8)
-                    src = src.rearrange("p (b u r) -> p b u r", u=2, r=RUN)
-                    scale = doc_scale[g][:, col : col + 1]
-                    nc.vector.tensor_scalar(out=dst, in0=src, scalar1=scale, scalar2=None, op0=ALU.mult)
-
-        def widen_on_scalar(g, t, s):
-            plain = keep.tile([P, PASS], BF16, name="plain", align_bytes=64)
+        def widen(slab):
+            n, s = slab
+            tile = work.tile([P, 2, P, 2], BF16, name="wide", tag="wide", bufs=16, align_bytes=64)
+            words = tile[:].rearrange("p u w e -> p (u w e)").bitcast(F32)
+            to_turn[slab] = [words[:, u * P : (u + 1) * P] for u in range(2)]
+            per = G // PACK
             for i in range(PASS // G):
-                col = t * SCALE_BLOCKS + s * (PASS // G) + i
+                col = (n % PACK) * SCALE_BLOCKS + s * (PASS // G) + i
+                src = doc_bytes[slab][:, G * i : G * (i + 1)].bitcast(FP8).rearrange("p (w u e) -> p u w e", u=2, e=2)
+                nc.vector.tensor_scalar(
+                    out=tile[:, :, per * i : per * (i + 1), :],
+                    in0=src,
+                    scalar1=doc_scale[n // PACK][:, col : col + 1],
+                    scalar2=None,
+                    op0=ALU.mult,
+                )
+
+        def widen_on_scalar(slab):
+            n, s = slab
+            plain = keep.tile([P, PASS], BF16, name="plain_%d_%d" % slab, align_bytes=64)
+            words = plain[:].bitcast(F32)
+            to_turn[slab] = [words[:, u : 2 * P : 2] for u in range(2)]
+            for i in range(PASS // G):
+                col = (n % PACK) * SCALE_BLOCKS + s * (PASS // G) + i
                 nc.scalar.activation(
                     out=plain[:, G * i : G * (i + 1)],
-                    in_=doc_bytes[(g, t, s)][:, G * i : G * (i + 1)].bitcast(FP8),
+                    in_=doc_bytes[slab][:, G * i : G * (i + 1)].bitcast(FP8),
                     func=ACT.Copy,
-                    scale=doc_scale[g][:, col : col + 1],
+                    scale=doc_scale[n // PACK][:, col : col + 1],
                 )
-            tile = keep.tile([P, 2, PASS // (2 * RUN), RUN], BF16, name="wide_by_scalar", align_bytes=64)
-            words = tile[:].rearrange("p u b r -> p (u b r)").bitcast(F32)
-            to_turn[((g, t), s)] = [words[:, u * P : (u + 1) * P] for u in range(2)]
-            return tile, plain
 
-        def reorder_plain(tile, plain):
-            nc.scalar.copy(out=tile[:], in_=plain[:].rearrange("p (b u r) -> p u b r", u=2, r=RUN))
-
-        def reorder_queries(j, copy):
-            tile = keep.tile([P, 2, K // (2 * RUN), RUN], BF16, name="q_wide_%d" % j, align_bytes=64)
-            words = tile[:].rearrange("p u b r -> p u (b r)").bitcast(F32)
+        def query_slabs(j):
+            words = q_raw[j][:].bitcast(F32)
             for s in range(K_PASSES):
-                to_turn[(("q", j), s)] = [words[:, u, s * P : (s + 1) * P] for u in range(2)]
-            copy(out=tile[:], in_=q_raw[j][:].rearrange("p (b u r) -> p u b r", u=2, r=RUN))
+                to_turn[(("q", j), s)] = [words[:, 2 * P * s + u : 2 * P * (s + 1) : 2] for u in range(2)]
+            return whole(("q", j))
 
         def open_turn(slabs, tag):
             turn_bank[slabs] = psum.tile([P, 2, 2, P], F32, name=tag, tag=tag)
@@ -204,32 +188,33 @@ def tile_archived_docs_feedback_d4_kernel(tc, docs_bytes, docs_scale, queries, n
         def copy_turned(slabs, dst):
             nc.scalar.copy(out=dst, in_=turn_bank[slabs][:].rearrange("p s u d -> p s d u"))
 
-        def copy_docs(piece, i):
-            if i == 0:
-                tag = "turned%d" % len(piece)
-                turned[piece] = work.tile([P, len(piece), 2, P, 2], F32, name=tag, tag=tag, bufs=6 // len(piece), align_bytes=64)
-            copy_turned(piece[i], turned[piece][:, i, :, :, :])
+        def copy_docs(slabs):
+            tile = work.tile([P, 2, P, 2], F32, name="turned", tag="turned", bufs=10, align_bytes=64)
+            for i, slab in enumerate(slabs):
+                turned[slab] = (tile, i)
+            copy_turned(slabs, tile[:])
 
-        def quantize_docs(piece):
-            width = 2 * len(piece) * P
-            tag = "doc_codes%d" % len(piece)
-            codes = work.tile([P, width], U32, name=tag, tag=tag, bufs=6, align_bytes=64)
-            tag = "doc_scales%d" % len(piece)
-            scales = work.tile([P, width], U8, name=tag, tag=tag, bufs=6, align_bytes=64)
-            for i, slab in enumerate([slab for slabs in piece for slab in slabs]):
-                doc_codes[slab] = (codes[:, i * P : (i + 1) * P], scales[:, i * P : (i + 1) * P])
+        def quantize_docs(*slabs):
+            tile, i = turned[slabs[0]]
+            width = len(slabs) * P
+            tag = "doc_codes%d" % len(slabs)
+            codes = work.tile([P, width], U32, name=tag, tag=tag, bufs=10, align_bytes=64)
+            tag = "doc_scales%d" % len(slabs)
+            scales = work.tile([P, width], U8, name=tag, tag=tag, bufs=10, align_bytes=64)
+            for m, slab in enumerate(slabs):
+                doc_codes[slab] = (codes[:, m * P : (m + 1) * P], scales[:, m * P : (m + 1) * P])
             nc.vector.quantize_mx(
                 out=codes[:].bitcast(FP8X4),
                 scales=scales[:],
-                in_=turned[piece][:].rearrange("p t s d u -> p (t s d u)").bitcast(BF16),
+                in_=tile[:, i : i + len(slabs), :, :].rearrange("p s d u -> p (s d u)").bitcast(BF16),
             )
 
         def copy_queries(j):
             copy_turned(whole(("q", j)), q_turned[j // 2][:, :, (j % 2) * P : (j % 2 + 1) * P, :])
 
-        def quantize_queries(half):
+        def quantize_queries(half, passes=range(K_PASSES)):
             cols = slice(half * HALF, (half + 1) * HALF)
-            for s in range(K_PASSES):
+            for s in passes:
                 nc.vector.quantize_mx(
                     out=q_codes[:, s, cols].bitcast(FP8X4),
                     scales=q_scales[:, s, cols],
@@ -238,22 +223,22 @@ def tile_archived_docs_feedback_d4_kernel(tc, docs_bytes, docs_scale, queries, n
 
         def warm_up(bank, slots):
             for n in slots:
-                nc.tensor.matmul(out=bank[:, n * P : (n + 1) * P], lhsT=ident_raw[:], rhs=ident_raw[:], start=True, stop=True)
+                nc.tensor.matmul(out=bank, lhsT=zeros[:, 0:P], rhs=zeros[:, 0:N_TILE], start=True, stop=True)
 
-        def open_scores(g, t, tag):
-            score_bank[(g, t)] = psum.tile([P, B], F32, name=tag, tag=tag)
-            return score_bank[(g, t)]
+        def open_scores(n, tag):
+            score_bank[n] = psum.tile([P, B], F32, name=tag, tag=tag)
+            return score_bank[n]
 
-        def scores(g, t, tag):
-            bank = score_bank[(g, t)] if (g, t) in score_bank else open_scores(g, t, tag)
+        def scores(n, tag, cols=slice(0, B)):
+            bank = score_bank[n] if n in score_bank else open_scores(n, tag)
             for s in range(K_PASSES):
-                codes, scales = doc_codes[((g, t), s)]
+                codes, scales = doc_codes[(n, s)]
                 nc.tensor.matmul_mx(
-                    out=bank[:],
+                    out=bank[:, cols],
                     lhsT=codes.bitcast(FP8X4),
                     lhsT_scale=scales,
-                    rhs=q_codes[:, s, :].bitcast(FP8X4),
-                    rhs_scale=q_scales[:, s, :],
+                    rhs=q_codes[:, s, cols].bitcast(FP8X4),
+                    rhs_scale=q_scales[:, s, cols],
                     start=(s == 0),
                     stop=(s == K_PASSES - 1),
                 )
@@ -261,12 +246,12 @@ def tile_archived_docs_feedback_d4_kernel(tc, docs_bytes, docs_scale, queries, n
         def invert_norms(g0, g1):
             nc.vector.reciprocal(out=inv_norms[:, g0 * PACK : g1 * PACK], in_=norms_raw[g0][:].rearrange("p g t -> p (g t)"))
 
-        def relevance(g, t):
+        def relevance(n):
+            g, t = divmod(n, PACK)
             if t == 0:
                 rel_planes[g] = keep.tile([P, PACK, B], BF16, name="rel_planes_%d" % g, align_bytes=64)
-            col = g * PACK + t
             nc.scalar.activation(
-                out=rel_planes[g][:, t, :], in_=score_bank[(g, t)][:], func=ACT.Relu, scale=inv_norms[:, col : col + 1]
+                out=rel_planes[g][:, t, :], in_=score_bank[n][:], func=ACT.Relu, scale=inv_norms[:, n : n + 1]
             )
 
         def interleave(g, half, copy, lo=0, hi=HALF):
@@ -309,145 +294,141 @@ def tile_archived_docs_feedback_d4_kernel(tc, docs_bytes, docs_scale, queries, n
             queue = nc.scalar if (j, first + width) == (Q_TILES - 1, N) else nc.sync
             queue.dma_start(out=out[j * P : (j + 1) * P, first : first + width], in_=result[:])
 
-        def turn_tag(t):
-            return "rot%d" % t
+        early_sums = [(j, first) for j in range(2) for first in range(0, N, N_TILE)]
+        sum_tags = ["acc%d" % i for i in range(4)]
+        turn_tags = ["rot%d" % i for i in range(4)]
 
-        def sum_tag(j, first):
-            return "acc%d" % (2 * (j % 2) + first // N_TILE)
+        def early_passes(g, lo, hi):
+            for i in range(lo, hi):
+                pool_pass(g, early_sums[i][0], early_sums[i][1], N_TILE, sum_tags[i])
 
-        def early_passes(g, j):
-            for first in range(0, N, N_TILE):
-                pool_pass(g, j, first, N_TILE, sum_tag(j, first))
+        def pair_banks(n):
+            return [((n, s), (n + 1, s)) for s in range(K_PASSES)]
 
-        def score_pair(g, t0, tags):
-            for t in (t0, t0 + 1):
-                scores(g, t, tags[t])
-
-        def relevance_pair(g, t0):
-            for t in (t0, t0 + 1):
-                relevance(g, t)
-
-        def staggered(g):
-            banks = [tuple(((g, t), s) for t, s in pair) for pair in BANK_SLABS]
-            return [(banks[0],), (banks[1], banks[2]), (banks[3],)]
-
-        sum_tags = [sum_tag(j, first) for j in range(2) for first in range(0, N, N_TILE)]
-        turn_tags = [turn_tag(t) for t in range(PACK)]
         on_vector, on_scalar = nc.vector.tensor_copy, nc.scalar.copy
 
-        first_pair = (whole((0, 0)), whole((0, 1)))
-        second_pair = (whole((0, 2)), whole((0, 3)))
-        pieces = {1: [(bank,) for piece in staggered(1) for bank in piece]}
-        widen(0, 0)
-        widen(0, 1, [0])
-        by_scalar = widen_on_scalar(0, 1, 1)
-        reorder_plain(*by_scalar)
-        spare = open_turn(whole(("q", 3)), sum_tags[3])[:].rearrange("p s u d -> p (s u d)")
-        warm_up(spare, range(FIRST_WARM_UPS))
-        turn(whole((0, 0)), turn_tag(0))
-        turn(whole((0, 1)), turn_tag(1))
-        reorder_queries(0, on_scalar)
-        warm_up(spare, [0, 1])
-        turn(whole(("q", 0)), sum_tags[0])
-        copy_docs(first_pair, 0)
-        copy_docs(first_pair, 1)
+        def widen_tile(n):
+            for slab in whole(n):
+                widen(slab)
+
+        def staggered(g):
+            n = PACK * g
+            return [((n, 0), (n + 1, 0)), ((n, 1), (n + 2, 0)), ((n + 1, 1), (n + 3, 0)), ((n + 2, 1), (n + 3, 1))]
+
+        widen_tile(0)
+        widen_on_scalar((1, 0))
+        widen_on_scalar((1, 1))
+        spare = open_turn(query_slabs(3), sum_tags[3])[:].rearrange("p s u d -> p (s u d)")
+        warm_up(spare, range(4))
+        turn(whole(0), turn_tags[0])
+        copy_docs(whole(0))
+        warm_up(spare, range(2))
+        widen_tile(2)
+        widen_tile(3)
+        turn(whole(2), turn_tags[2])
+        copy_docs(whole(2))
+        turn(whole(1), turn_tags[1])
+        copy_docs(whole(1))
+        turn(whole(3), turn_tags[3])
+        copy_docs(whole(3))
+        turn(query_slabs(0), sum_tags[0])
         copy_queries(0)
-        widen(0, 2)
-        widen(0, 3)
-        reorder_queries(1, on_vector)
-        warm_up(spare, [3])
-        turn(whole((0, 2)), turn_tag(2))
-        turn(whole(("q", 1)), sum_tags[1])
-        turn(whole((0, 3)), turn_tag(3))
-        reorder_queries(2, on_scalar)
+        warm_up(spare, range(1))
+        turn(query_slabs(1), sum_tags[1])
         copy_queries(1)
-        widen(1, 0)
-        warm_up(spare, [2])
-        turn(whole(("q", 2)), sum_tags[2])
-        quantize_docs(first_pair)
-        reorder_queries(3, on_vector)
-        widen(1, 1)
-        copy_docs(second_pair, 0)
+        widen_tile(4)
+        widen_tile(5)
+        for n in (0, 2, 1, 3):
+            quantize_docs(*whole(n))
+        banks = {1: staggered(1)}
+        turn(banks[1][0], turn_tags[0])
+        copy_docs(banks[1][0])
+        turn(query_slabs(2), sum_tags[2])
         copy_queries(2)
+        warm_up(spare, range(1))
         turn(whole(("q", 3)), sum_tags[3])
         copy_queries(3)
-        copy_docs(second_pair, 1)
-        turn(pieces[1][0][0], turn_tag(0))
-        copy_docs(pieces[1][0], 0)
-        warm_up(open_scores(0, 0, sum_tags[0])[:], range(2))
-        widen(1, 2)
+        widen_tile(6)
+        widen_tile(7)
         quantize_queries(0)
-        widen(1, 3)
-        quantize_queries(1)
+        spare = open_scores(0, sum_tags[0])[:]
+        for i in range(1, PACK):
+            turn(banks[1][i], turn_tags[i])
+            copy_docs(banks[1][i])
+            if i <= 0:
+                warm_up(spare, range(1))
         invert_norms(0, 2)
-        quantize_docs(second_pair)
-        for t in range(1, PACK):
-            turn(pieces[1][t][0], turn_tag(t))
-            copy_docs(pieces[1][t], 0)
-        score_pair(0, 0, sum_tags)
-        score_pair(0, 2, sum_tags)
-        relevance_pair(0, 0)
-        relevance_pair(0, 2)
-        for t in range(PACK):
-            widen(2, t)
+        widen_tile(8)
+        quantize_queries(1)
+        for n in range(PACK):
+            scores(n, sum_tags[n], slice(0, HALF))
+        for n in range(PACK):
+            scores(n, sum_tags[n], slice(HALF, B))
+            relevance(n)
+        for n in range(9, 12):
+            widen_tile(n)
+
+        load_v_scales(0, 8)
+        load_norms(2, 8)
+        load_scales(4, 8, nc.sync)
+        load_v(1, 2)
+        load_docs(16, 4)
+        load_v(2, 4)
+        load_docs(20, 4)
+        load_docs(24, 4)
+        load_docs(28, 4)
+        load_v(4, 8)
 
         last = GROUPS - 1
         for g in range(1, last):
-            pieces[g + 1] = staggered(g + 1)
-            slots = [(piece, i) for piece in pieces[g + 1] for i in range(len(piece))]
-            for t, (piece, i) in enumerate(slots):
-                turn(piece[i], turn_tag(t))
-            for slot in slots[:2]:
-                copy_docs(*slot)
-            if g == 1:
-                interleave(0, EARLY, on_scalar, 0, SHARE)
+            banks[g + 1] = staggered(g + 1)
+            for i, slabs in enumerate(banks[g + 1]):
+                turn(slabs, turn_tags[i])
+                if g > 1 or i < 2:
+                    copy_docs(slabs)
             if g > 1:
-                for slot in slots[2:]:
-                    copy_docs(*slot)
-                early_passes(g - 2, 1)
-            for piece in pieces[g][(0 if g < FIRST_PIECE_AHEAD_FROM else 1) :]:
-                quantize_docs(piece)
-            interleave(g - 1, EARLY, on_vector, SHARE if g == 1 else 0)
+                early_passes(g - 2, 4 - HELD, 4)
+            for slabs in banks[g][(0 if g < AHEAD else 1) :]:
+                quantize_docs(*slabs)
+            interleave(g - 1, EARLY, on_vector)
             tags = sum_tags if g == 1 else turn_tags
-            score_pair(g, 0, tags)
-            relevance_pair(g, 0)
-            if g == 1:
-                for slot in slots[2:]:
-                    copy_docs(*slot)
-            score_pair(g, 2, tags)
-            relevance_pair(g, 2)
-            if 3 <= g < last - 1:
-                interleave(0, LATE, on_scalar, SHARE * (g - 3), SHARE * (g - 2))
+            for t in range(PACK):
+                if g == 1 and t == 2:
+                    for slabs in banks[2][2:]:
+                        copy_docs(slabs)
+                scores(PACK * g + t, tags[t])
+                relevance(PACK * g + t)
             if g + 2 < GROUPS:
-                widen(g + 2, 0)
+                n = PACK * (g + 2)
+                widen_tile(n)
                 quantize_rel(g - 1, EARLY)
-                widen(g + 2, 1)
-                widen(g + 2, 2)
-                if g + 1 >= FIRST_PIECE_AHEAD_FROM:
-                    quantize_docs(pieces[g + 1][0])
-                widen(g + 2, 3)
+                widen_tile(n + 1)
+                widen_tile(n + 2)
+                if g + 1 >= AHEAD:
+                    quantize_docs(*banks[g + 1][0])
+                widen_tile(n + 3)
             else:
-                quantize_docs(pieces[g + 1][0])
+                quantize_docs(*banks[g + 1][0])
                 quantize_rel(g - 1, EARLY)
-                interleave(0, LATE, on_vector, 3 * SHARE)
+                interleave(0, LATE, on_vector)
             if g == 1:
                 invert_norms(2, GROUPS)
-            early_passes(g - 1, 0)
+            early_passes(g - 1, 0, 4 - HELD)
 
-        quantize_docs(pieces[last][1])
+        quantize_docs(*banks[last][1])
+        quantize_docs(*banks[last][2])
         quantize_rel(0, LATE)
         interleave(1, LATE, on_vector)
-        quantize_docs(pieces[last][2])
-        interleave(2, LATE, on_scalar, 0, SHARE)
-        interleave(2, LATE, on_vector, SHARE)
+        quantize_docs(*banks[last][3])
+        interleave(2, LATE, on_vector)
         for t in range(PACK):
-            scores(last, t, turn_tag(t))
-            relevance(last, t)
+            scores(PACK * last + t, turn_tags[t])
+            relevance(PACK * last + t)
         interleave(last - 1, EARLY, on_vector)
         quantize_rel(1, LATE)
         quantize_rel(last - 1, EARLY)
         quantize_rel(2, LATE)
-        early_passes(last - 2, 1)
+        early_passes(last - 2, 4 - HELD, 4)
         interleave(3, LATE, on_vector)
         interleave(last, EARLY, on_vector)
         quantize_rel(3, LATE)
@@ -461,22 +442,20 @@ def tile_archived_docs_feedback_d4_kernel(tc, docs_bytes, docs_scale, queries, n
 
         for g in range(GROUPS):
             if g == 1:
-                early_passes(last - 1, 0)
-                early_passes(last - 1, 1)
+                early_passes(last - 1, 0, 4)
             if g == LATE_BEFORE_CLOSE:
-                for j in range(2):
-                    early_passes(last, j)
-                    for first in range(0, N, N_TILE):
-                        store(j, first, N_TILE, on_scalar)
+                early_passes(last, 0, 4)
+                for j, first in early_sums:
+                    store(j, first, N_TILE, on_scalar)
             for first in range(0, N, N_TILE):
-                pool_pass(g, 2, first, N_TILE, turn_tag(first // N_TILE))
+                pool_pass(g, 2, first, N_TILE, turn_tags[first // N_TILE])
             if 1 <= g < 6:
                 for late in range(2) if g == 1 else [g]:
-                    pool_pass(late, 3, 0, N_TILE, turn_tag(2))
+                    pool_pass(late, 3, 0, N_TILE, turn_tags[2])
         store(2, 0, N_TILE, on_vector)
         store(2, N_TILE, N_TILE, on_scalar)
         for g in range(6, GROUPS):
-            pool_pass(g, 3, 0, N_TILE, turn_tag(2))
+            pool_pass(g, 3, 0, N_TILE, turn_tags[2])
         store(3, 0, N_TILE, on_scalar)
         first = N_TILE
         for i, width in enumerate(LAST_WIDTHS):

@@ -103,22 +103,20 @@ def tile_archived_docs_feedback_d4_kernel(tc, docs_bytes, docs_scale, queries, n
         load_scales(0, 1, nc.scalar)
         nc.scalar.activation(out=ident[:], in_=ident_raw[:], func=ACT.Relu)
         load_docs(0, 1)
-        load_docs(2, 1)
         load_docs(1, 1)
-        load_docs(3, 1)
+        load_docs(2, 2)
+        load_queries(0)
         load_scales(1, 2, nc.sync)
         load_docs(4, 2)
-        load_queries(0)
         load_queries(1)
-        load_queries(2)
         load_docs(6, 2)
-        load_queries(3)
-        load_scales(2, 4, nc.sync)
-        load_docs(8, 2)
+        load_scales(2, 3, nc.sync)
         load_norms(0, 2)
+        load_docs(8, 2)
         load_docs(10, 2)
+        load_queries(2)
+        load_queries(3)
         load_docs(12, 4)
-        load_v(0, 1)
 
         inv_norms = keep.tile([P, GROUPS * PACK], F32, name="inv_norms")
         q_turned = [keep.tile([P, K_PASSES, HALF, 2], F32, name="q_turned_%d" % half, align_bytes=64) for half in range(2)]
@@ -131,6 +129,7 @@ def tile_archived_docs_feedback_d4_kernel(tc, docs_bytes, docs_scale, queries, n
         doc_codes = {}
         score_bank = {}
         rel_planes = {}
+        rel_half = {}
         rel_packed = {}
         rel_codes = {}
         sums = {}
@@ -185,8 +184,8 @@ def tile_archived_docs_feedback_d4_kernel(tc, docs_bytes, docs_scale, queries, n
         def whole(key):
             return ((key, 0), (key, 1))
 
-        def copy_turned(slabs, dst):
-            nc.scalar.copy(out=dst, in_=turn_bank[slabs][:].rearrange("p s u d -> p s d u"))
+        def copy_turned(slabs, dst, copy=nc.scalar.copy):
+            copy(out=dst, in_=turn_bank[slabs][:].rearrange("p s u d -> p s d u"))
 
         def copy_docs(slabs):
             tile = work.tile([P, 2, P, 2], F32, name="turned", tag="turned", bufs=10, align_bytes=64)
@@ -209,8 +208,8 @@ def tile_archived_docs_feedback_d4_kernel(tc, docs_bytes, docs_scale, queries, n
                 in_=tile[:, i : i + len(slabs), :, :].rearrange("p s d u -> p (s d u)").bitcast(BF16),
             )
 
-        def copy_queries(j):
-            copy_turned(whole(("q", j)), q_turned[j // 2][:, :, (j % 2) * P : (j % 2 + 1) * P, :])
+        def copy_queries(j, copy=nc.scalar.copy):
+            copy_turned(whole(("q", j)), q_turned[j // 2][:, :, (j % 2) * P : (j % 2 + 1) * P, :], copy)
 
         def quantize_queries(half, passes=range(K_PASSES)):
             cols = slice(half * HALF, (half + 1) * HALF)
@@ -249,9 +248,40 @@ def tile_archived_docs_feedback_d4_kernel(tc, docs_bytes, docs_scale, queries, n
         def relevance(n):
             g, t = divmod(n, PACK)
             if t == 0:
-                rel_planes[g] = keep.tile([P, PACK, B], BF16, name="rel_planes_%d" % g, align_bytes=64)
+                planes = keep.tile([P, PACK, B], BF16, name="rel_planes_%d" % g, align_bytes=64)
+                rel_planes[g] = planes
+                for half in range(2):
+                    rel_half[(g, half)] = planes[:, :, half * HALF : (half + 1) * HALF]
             nc.scalar.activation(
                 out=rel_planes[g][:, t, :], in_=score_bank[n][:], func=ACT.Relu, scale=inv_norms[:, n : n + 1]
+            )
+
+        def half_scores(n, half, tag):
+            if n % 2 == 0:
+                score_bank[(n // 2, half)] = psum.tile([P, 2, HALF], F32, name=tag, tag=tag)
+            cols = slice(half * HALF, (half + 1) * HALF)
+            for s in range(K_PASSES):
+                codes, scales = doc_codes[(n, s)]
+                nc.tensor.matmul_mx(
+                    out=score_bank[(n // 2, half)][:, n % 2, :],
+                    lhsT=codes.bitcast(FP8X4),
+                    lhsT_scale=scales,
+                    rhs=q_codes[:, s, cols].bitcast(FP8X4),
+                    rhs_scale=q_scales[:, s, cols],
+                    start=(s == 0),
+                    stop=(s == K_PASSES - 1),
+                )
+
+        def half_relevance(n, half):
+            g, t = divmod(n, PACK)
+            if t == 0:
+                planes = keep.tile([P, PACK, HALF], BF16, name="rel_planes_%d_%d" % (g, half), align_bytes=64)
+                rel_half[(g, half)] = planes[:]
+            nc.scalar.activation(
+                out=rel_half[(g, half)][:, t, :],
+                in_=score_bank[(n // 2, half)][:, n % 2, :],
+                func=ACT.Relu,
+                scale=inv_norms[:, n : n + 1],
             )
 
         def interleave(g, half, copy, lo=0, hi=HALF):
@@ -260,7 +290,7 @@ def tile_archived_docs_feedback_d4_kernel(tc, docs_bytes, docs_scale, queries, n
             tile = rel_packed[(g, half)]
             copy(
                 out=tile[:, lo:hi, :].rearrange("p (c i) t -> p c t i", i=8),
-                in_=rel_planes[g][:, :, half * HALF + lo : half * HALF + hi].rearrange("p t (c i) -> p c t i", i=8),
+                in_=rel_half[(g, half)][:, :, lo:hi].rearrange("p t (c i) -> p c t i", i=8),
             )
 
         def quantize_rel(g, half):
@@ -300,7 +330,7 @@ def tile_archived_docs_feedback_d4_kernel(tc, docs_bytes, docs_scale, queries, n
 
         def early_passes(g, lo, hi):
             for i in range(lo, hi):
-                pool_pass(g, early_sums[i][0], early_sums[i][1], N_TILE, sum_tags[i])
+                pool_pass(g, early_sums[i][0], early_sums[i][1], N_TILE, sum_tags[(i + 2) % 4])
 
         def pair_banks(n):
             return [((n, s), (n + 1, s)) for s in range(K_PASSES)]
@@ -316,58 +346,47 @@ def tile_archived_docs_feedback_d4_kernel(tc, docs_bytes, docs_scale, queries, n
             return [((n, 0), (n + 1, 0)), ((n, 1), (n + 2, 0)), ((n + 1, 1), (n + 3, 0)), ((n + 2, 1), (n + 3, 1))]
 
         widen_tile(0)
-        widen_on_scalar((1, 0))
-        widen_on_scalar((1, 1))
-        spare = open_turn(query_slabs(3), sum_tags[3])[:].rearrange("p s u d -> p (s u d)")
+        widen_tile(1)
+        spare = psum.tile([P, N_TILE], F32, name=sum_tags[0], tag=sum_tags[0])[:]
         warm_up(spare, range(4))
         turn(whole(0), turn_tags[0])
         copy_docs(whole(0))
-        warm_up(spare, range(2))
+        warm_up(spare, range(1))
+        turn(whole(1), turn_tags[1])
+        copy_docs(whole(1))
+        warm_up(spare, range(1))
         widen_tile(2)
         widen_tile(3)
         turn(whole(2), turn_tags[2])
         copy_docs(whole(2))
-        turn(whole(1), turn_tags[1])
-        copy_docs(whole(1))
+        turn(query_slabs(0), sum_tags[2])
+        copy_queries(0)
         turn(whole(3), turn_tags[3])
         copy_docs(whole(3))
-        turn(query_slabs(0), sum_tags[0])
-        copy_queries(0)
-        warm_up(spare, range(1))
-        turn(query_slabs(1), sum_tags[1])
-        copy_queries(1)
+        warm_up(spare, range(2))
+        quantize_docs(*whole(0))
+        quantize_docs(*whole(1))
         widen_tile(4)
         widen_tile(5)
-        for n in (0, 2, 1, 3):
-            quantize_docs(*whole(n))
-        banks = {1: staggered(1)}
+        banks = {1: staggered(1), 2: staggered(2)}
+        turn(query_slabs(1), sum_tags[3])
+        copy_queries(1)
+        warm_up(spare, range(0))
         turn(banks[1][0], turn_tags[0])
         copy_docs(banks[1][0])
-        turn(query_slabs(2), sum_tags[2])
-        copy_queries(2)
-        warm_up(spare, range(1))
-        turn(whole(("q", 3)), sum_tags[3])
-        copy_queries(3)
+        quantize_docs(*whole(2))
         widen_tile(6)
         widen_tile(7)
         quantize_queries(0)
-        spare = open_scores(0, sum_tags[0])[:]
+        quantize_docs(*whole(3))
+        invert_norms(0, 2)
         for i in range(1, PACK):
+            warm_up(spare, range([1,1,0][i - 1]))
             turn(banks[1][i], turn_tags[i])
             copy_docs(banks[1][i])
-            if i <= 0:
-                warm_up(spare, range(1))
-        invert_norms(0, 2)
-        widen_tile(8)
-        quantize_queries(1)
-        for n in range(PACK):
-            scores(n, sum_tags[n], slice(0, HALF))
-        for n in range(PACK):
-            scores(n, sum_tags[n], slice(HALF, B))
-            relevance(n)
-        for n in range(9, 12):
-            widen_tile(n)
 
+        load_scales(3, 4, nc.sync)
+        load_v(0, 1)
         load_v_scales(0, 8)
         load_norms(2, 8)
         load_scales(4, 8, nc.sync)
@@ -378,25 +397,58 @@ def tile_archived_docs_feedback_d4_kernel(tc, docs_bytes, docs_scale, queries, n
         load_docs(24, 4)
         load_docs(28, 4)
         load_v(4, 8)
+        for n in range(PACK):
+            half_scores(n, EARLY, sum_tags[n // 2])
+        widen_tile(8)
+        widen_tile(9)
+        for slabs in banks[1]:
+            quantize_docs(*slabs)
+        widen_tile(10)
+        widen_tile(11)
+        for n in range(PACK):
+            half_relevance(n, EARLY)
+        for j in (2, 3):
+            turn(query_slabs(j), sum_tags[j])
+            copy_queries(j)
+        for n in range(PACK, 2 * PACK):
+            half_scores(n, EARLY, sum_tags[n // 2 % 2])
+        for i in range(PACK):
+            turn(banks[2][i], turn_tags[i])
+        quantize_queries(1)
+        interleave(0, EARLY, on_vector)
+        for n in range(PACK, 2 * PACK):
+            half_relevance(n, EARLY)
+        copy_docs(banks[2][0])
+        copy_docs(banks[2][1])
+        for n in range(PACK):
+            half_scores(n, LATE, sum_tags[2 + n // 2])
+        for n in range(PACK):
+            half_relevance(n, LATE)
+        for n in range(PACK, 2 * PACK):
+            half_scores(n, LATE, sum_tags[n // 2 % 2])
+        copy_docs(banks[2][2])
+        copy_docs(banks[2][3])
+        for n in range(PACK, 2 * PACK):
+            half_relevance(n, LATE)
+        widen_tile(12)
+        quantize_rel(0, EARLY)
+        for n in range(13, 16):
+            widen_tile(n)
+        invert_norms(2, GROUPS)
 
         last = GROUPS - 1
-        for g in range(1, last):
+        early_passes(0, 0, 4 - HELD)
+        for g in range(2, last):
             banks[g + 1] = staggered(g + 1)
             for i, slabs in enumerate(banks[g + 1]):
                 turn(slabs, turn_tags[i])
-                if g > 1 or i < 2:
-                    copy_docs(slabs)
-            if g > 1:
-                early_passes(g - 2, 4 - HELD, 4)
+                copy_docs(slabs)
+            early_passes(g - 2, 4 - HELD, 4)
             for slabs in banks[g][(0 if g < AHEAD else 1) :]:
                 quantize_docs(*slabs)
             interleave(g - 1, EARLY, on_vector)
-            tags = sum_tags if g == 1 else turn_tags
             for t in range(PACK):
-                if g == 1 and t == 2:
-                    for slabs in banks[2][2:]:
-                        copy_docs(slabs)
-                scores(PACK * g + t, tags[t])
+                scores(PACK * g + t, turn_tags[t])
                 relevance(PACK * g + t)
             if g + 2 < GROUPS:
                 n = PACK * (g + 2)
@@ -411,8 +463,6 @@ def tile_archived_docs_feedback_d4_kernel(tc, docs_bytes, docs_scale, queries, n
                 quantize_docs(*banks[g + 1][0])
                 quantize_rel(g - 1, EARLY)
                 interleave(0, LATE, on_vector)
-            if g == 1:
-                invert_norms(2, GROUPS)
             early_passes(g - 1, 0, 4 - HELD)
 
         quantize_docs(*banks[last][1])
@@ -460,6 +510,6 @@ def tile_archived_docs_feedback_d4_kernel(tc, docs_bytes, docs_scale, queries, n
         first = N_TILE
         for i, width in enumerate(LAST_WIDTHS):
             for g in range(GROUPS):
-                pool_pass(g, 3, first, width, sum_tags[i])
+                pool_pass(g, 3, first, width, sum_tags[(i + 2) % 4])
             store(3, first, width, on_scalar)
             first = first + width

@@ -27,7 +27,7 @@ Q_TILES = B // P
 N_TILE = 512
 HALF = B // 2
 EARLY, LATE = 0, 1
-AHEAD = 4
+AHEAD = 3
 HELD = 2
 ODD_WORDS = 351
 LATE_BEFORE_CLOSE = 3
@@ -386,17 +386,15 @@ def tile_archived_docs_feedback_d4_kernel(tc, docs_bytes, docs_scale, queries, n
             copy_docs(banks[1][i])
 
         load_scales(3, 4, nc.sync)
-        load_v(0, 1)
+        load_v(0, 2)
         load_v_scales(0, 8)
         load_norms(2, 8)
         load_scales(4, 8, nc.sync)
-        load_v(1, 2)
         load_docs(16, 4)
-        load_v(2, 4)
         load_docs(20, 4)
+        load_v(2, 8)
         load_docs(24, 4)
         load_docs(28, 4)
-        load_v(4, 8)
         for n in range(PACK):
             half_scores(n, EARLY, sum_tags[n // 2])
         widen_tile(8)
@@ -437,23 +435,24 @@ def tile_archived_docs_feedback_d4_kernel(tc, docs_bytes, docs_scale, queries, n
         invert_norms(2, GROUPS)
 
         last = GROUPS - 1
-        early_passes(0, 0, 4 - HELD)
-        for g in range(2, last):
+        HOLD = [2,2,1,1,2]
+        early_passes(0, 0, 4 - HOLD[0])
+        for g in range(2, last - 1):
             banks[g + 1] = staggered(g + 1)
             for i, slabs in enumerate(banks[g + 1]):
                 turn(slabs, turn_tags[i])
                 copy_docs(slabs)
-            early_passes(g - 2, 4 - HELD, 4)
+            early_passes(g - 2, 4 - HOLD[g - 2], 4)
             for slabs in banks[g][(0 if g < AHEAD else 1) :]:
                 quantize_docs(*slabs)
             interleave(g - 1, EARLY, on_vector)
             for t in range(PACK):
                 scores(PACK * g + t, turn_tags[t])
                 relevance(PACK * g + t)
-            if g + 2 < GROUPS:
-                n = PACK * (g + 2)
-                widen_tile(n)
-                quantize_rel(g - 1, EARLY)
+            n = PACK * (g + 2)
+            widen_tile(n)
+            quantize_rel(g - 1, EARLY)
+            if g < last - 2:
                 widen_tile(n + 1)
                 widen_tile(n + 2)
                 if g + 1 >= AHEAD:
@@ -461,25 +460,42 @@ def tile_archived_docs_feedback_d4_kernel(tc, docs_bytes, docs_scale, queries, n
                 widen_tile(n + 3)
             else:
                 quantize_docs(*banks[g + 1][0])
-                quantize_rel(g - 1, EARLY)
-                interleave(0, LATE, on_vector)
-            early_passes(g - 1, 0, 4 - HELD)
+                quantize_docs(*banks[g + 1][1])
+                widen_tile(n + 1)
+                quantize_docs(*banks[g + 1][2])
+                quantize_docs(*banks[g + 1][3])
+                widen_tile(n + 2)
+                widen_tile(n + 3)
+            early_passes(g - 1, 0, 4 - HOLD[g - 1])
+        g = last - 1
+        for t in range(PACK):
+            scores(PACK * g + t, turn_tags[t])
+            relevance(PACK * g + t)
+        early_passes(g - 2, 4 - HOLD[g - 2], 4)
+        banks[last] = staggered(last)
+        for i, slabs in enumerate(banks[last]):
+            turn(slabs, turn_tags[i])
+            copy_docs(slabs)
+        interleave(g - 1, EARLY, on_vector)
+        interleave(0, LATE, on_vector)
+        quantize_rel(g - 1, EARLY)
 
-        quantize_docs(*banks[last][1])
-        quantize_docs(*banks[last][2])
+        interleave(g, EARLY, on_vector)
         quantize_rel(0, LATE)
-        interleave(1, LATE, on_vector)
+        quantize_docs(*banks[last][0])
+        quantize_docs(*banks[last][1])
+        quantize_rel(g, EARLY)
+        quantize_docs(*banks[last][2])
         quantize_docs(*banks[last][3])
-        interleave(2, LATE, on_vector)
+        early_passes(g - 1, 0, 4)
         for t in range(PACK):
             scores(PACK * last + t, turn_tags[t])
             relevance(PACK * last + t)
-        interleave(last - 1, EARLY, on_vector)
+        interleave(1, LATE, on_vector)
+        interleave(2, LATE, on_vector)
         quantize_rel(1, LATE)
-        quantize_rel(last - 1, EARLY)
-        quantize_rel(2, LATE)
-        early_passes(last - 2, 4 - HELD, 4)
         interleave(3, LATE, on_vector)
+        quantize_rel(2, LATE)
         interleave(last, EARLY, on_vector)
         quantize_rel(3, LATE)
         quantize_rel(last, EARLY)
@@ -490,18 +506,16 @@ def tile_archived_docs_feedback_d4_kernel(tc, docs_bytes, docs_scale, queries, n
             quantize_rel(g + 1, LATE)
             quantize_rel(g, LATE)
 
+        early_passes(last - 1, 0, 4)
         for g in range(GROUPS):
-            if g == 1:
-                early_passes(last - 1, 0, 4)
             if g == LATE_BEFORE_CLOSE:
                 early_passes(last, 0, 4)
                 for j, first in early_sums:
                     store(j, first, N_TILE, on_scalar)
             for first in range(0, N, N_TILE):
                 pool_pass(g, 2, first, N_TILE, turn_tags[first // N_TILE])
-            if 1 <= g < 6:
-                for late in range(2) if g == 1 else [g]:
-                    pool_pass(late, 3, 0, N_TILE, turn_tags[2])
+            if g < 6:
+                pool_pass(g, 3, 0, N_TILE, turn_tags[2])
         store(2, 0, N_TILE, on_vector)
         store(2, N_TILE, N_TILE, on_scalar)
         for g in range(6, GROUPS):

@@ -346,9 +346,10 @@ def tile_archived_docs_feedback_d4_kernel(tc, docs_bytes, docs_scale, queries, n
             return [((n, 0), (n + 1, 0)), ((n, 1), (n + 2, 0)), ((n + 1, 1), (n + 3, 0)), ((n + 2, 1), (n + 3, 1))]
 
         widen_tile(0)
-        widen_tile(1)
+        widen((1, 0))
+        widen_on_scalar((1, 1))
         spare = psum.tile([P, N_TILE], F32, name=sum_tags[0], tag=sum_tags[0])[:]
-        warm_up(spare, range(4))
+        warm_up(spare, range(5))
         turn(whole(0), turn_tags[0])
         copy_docs(whole(0))
         warm_up(spare, range(1))
@@ -363,10 +364,10 @@ def tile_archived_docs_feedback_d4_kernel(tc, docs_bytes, docs_scale, queries, n
         copy_queries(0)
         turn(whole(3), turn_tags[3])
         copy_docs(whole(3))
-        warm_up(spare, range(2))
+        warm_up(spare, range(1))
         quantize_docs(*whole(0))
-        quantize_docs(*whole(1))
         widen_tile(4)
+        quantize_docs(*whole(1))
         widen_tile(5)
         banks = {1: staggered(1), 2: staggered(2)}
         turn(query_slabs(1), sum_tags[3])
@@ -418,13 +419,13 @@ def tile_archived_docs_feedback_d4_kernel(tc, docs_bytes, docs_scale, queries, n
             half_relevance(n, EARLY)
         copy_docs(banks[2][0])
         copy_docs(banks[2][1])
+        copy_docs(banks[2][2])
         for n in range(PACK):
             half_scores(n, LATE, sum_tags[2 + n // 2])
         for n in range(PACK):
             half_relevance(n, LATE)
         for n in range(PACK, 2 * PACK):
             half_scores(n, LATE, sum_tags[n // 2 % 2])
-        copy_docs(banks[2][2])
         copy_docs(banks[2][3])
         for n in range(PACK, 2 * PACK):
             half_relevance(n, LATE)
@@ -435,7 +436,7 @@ def tile_archived_docs_feedback_d4_kernel(tc, docs_bytes, docs_scale, queries, n
         invert_norms(2, GROUPS)
 
         last = GROUPS - 1
-        HOLD = [2,2,1,1,2]
+        HOLD = [2,1,1,1,2]
         early_passes(0, 0, 4 - HOLD[0])
         for g in range(2, last - 1):
             banks[g + 1] = staggered(g + 1)

@@ -18,19 +18,27 @@ ACT = mybir.ActivationFunctionType
 ALU = mybir.AluOpType
 
 P = 128
+QUADRANT = 32
+SCALE_ROWS = 4
 PACK = 4
 PASS = P * PACK
 GROUPS = T // PASS
+LAST = GROUPS - 1
 K_PASSES = K // PASS
-SCALE_BLOCKS = K // G
+SLAB_BLOCKS = PASS // G
 Q_TILES = B // P
 N_TILE = 512
+BANKS = 4
 HALF = B // 2
 EARLY, LATE = 0, 1
-AHEAD = 3
-HELD = 2
-ODD_WORDS = 351
+ALIGN = 64
+
+FIRST_WORDS = 513
+SECOND_WORDS = 189
+HELD_LONG, HELD = 2, 1
+AHEAD_FROM = 3
 LATE_BEFORE_CLOSE = 3
+LATE_STAGGER = 2
 LAST_WIDTHS = [2 * P, P, P]
 
 
@@ -46,45 +54,48 @@ def tile_archived_docs_feedback_d4_kernel(tc, docs_bytes, docs_scale, queries, n
         make_identity(nc, ident_raw[:])
         ident = keep.tile([P, P], F32, name="ident")
 
-        v_scale = keep.tile([P, GROUPS, N], U8, name="v_scale", align_bytes=64)
+        v_scale = keep.tile([P, GROUPS, N], U8, name="v_scale", align_bytes=ALIGN)
         filler = v_scale[:].rearrange("p g n -> p (g n)").bitcast(I32)
-        words = GROUPS * N // 4
-        nc.vector.memset(filler[:, words - ODD_WORDS :], 0)
-        nc.vector.memset(filler[:, words - 2 * ODD_WORDS : words - ODD_WORDS], 0)
-        nc.vector.memset(filler[:, : words - 2 * ODD_WORDS], 0)
-        zeros = v_scale[:, GROUPS - 1, :].bitcast(BF16)
+        filler_words = GROUPS * N // 4
+        second_end = filler_words - FIRST_WORDS
+        nc.vector.memset(filler[:, second_end:], 0)
+        nc.vector.memset(filler[:, second_end - SECOND_WORDS : second_end], 0)
+        nc.vector.memset(filler[:, : second_end - SECOND_WORDS], 0)
+        zeros = filler[:, filler_words - N_TILE :]
 
         docs_rows = docs_bytes.rearrange("(g m t) k -> g m t k", m=P, t=PACK)
         scale_rows = docs_scale.rearrange("(g m t) i -> m g (t i)", m=P, t=PACK)
         norm_rows = norms.rearrange("(g m t) -> m g t", m=P, t=PACK)
-        v_scale_rows = v_scales.rearrange("g (q r) n -> r q g n", r=4)
+        v_scale_rows = v_scales.rearrange("g (q r) n -> r q g n", r=SCALE_ROWS)
         doc_bytes = {}
         doc_scale = {}
         q_raw = {}
         v_codes = {}
         norms_raw = {}
 
-        def load_docs(n0, count):
-            g, t0 = divmod(n0, PACK)
-            tile = keep.tile([P, count, K], U8, name="doc_bytes_%d" % n0, align_bytes=64)
-            nc.sync.dma_start(out=tile[:], in_=docs_rows[g, :, t0 : t0 + count, :])
+        def load_docs(first_tile, count):
+            g, t = divmod(first_tile, PACK)
+            tile = keep.tile([P, count, K], U8, name="doc_bytes_%d" % first_tile, align_bytes=ALIGN)
+            nc.sync.dma_start(out=tile[:], in_=docs_rows[g, :, t : t + count, :])
             for i in range(count):
                 for s in range(K_PASSES):
-                    doc_bytes[(n0 + i, s)] = tile[:, i, s * PASS : (s + 1) * PASS]
+                    doc_bytes[(first_tile + i, s)] = tile[:, i, s * PASS : (s + 1) * PASS]
+
+        def load_group(g):
+            load_docs(PACK * g, PACK)
 
         def load_scales(g0, g1, queue):
-            tile = keep.tile([P, g1 - g0, PACK * SCALE_BLOCKS], F32, name="doc_scale_%d" % g0)
+            tile = keep.tile([P, g1 - g0, PACK * K // G], F32, name="doc_scale_%d" % g0)
             queue.dma_start(out=tile[:], in_=scale_rows[:, g0:g1, :])
             for g in range(g0, g1):
                 doc_scale[g] = tile[:, g - g0, :]
 
         def load_queries(j):
-            tile = keep.tile([P, K], BF16, name="q_raw_%d" % j, align_bytes=64)
-            nc.sync.dma_start(out=tile[:], in_=queries[j * P : (j + 1) * P, :])
-            q_raw[j] = tile
+            q_raw[j] = keep.tile([P, K], BF16, name="q_raw_%d" % j, align_bytes=ALIGN)
+            nc.sync.dma_start(out=q_raw[j][:], in_=queries[j * P : (j + 1) * P, :])
 
         def load_v(g0, g1):
-            tile = keep.tile([P, g1 - g0, 2 * N], U8, name="v_codes_%d" % g0, align_bytes=64)
+            tile = keep.tile([P, g1 - g0, 2 * N], U8, name="v_codes_%d" % g0, align_bytes=ALIGN)
             nc.sync.dma_start(out=tile[:].bitcast(I32), in_=v_words[g0:g1].rearrange("g p n -> p g n").bitcast(I32))
             for g in range(g0, g1):
                 v_codes[g] = tile[:, g - g0, :]
@@ -93,12 +104,9 @@ def tile_archived_docs_feedback_d4_kernel(tc, docs_bytes, docs_scale, queries, n
             norms_raw[g0] = keep.tile([P, g1 - g0, PACK], BF16, name="norms_raw_%d" % g0)
             nc.sync.dma_start(out=norms_raw[g0][:], in_=norm_rows[:, g0:g1, :])
 
-        def load_v_scales(g0, g1):
-            for r in range(4):
-                nc.sync.dma_start(
-                    out=v_scale[r:P:32, g0:g1, :].bitcast(I32),
-                    in_=v_scale_rows[r, :, g0:g1, :].bitcast(I32),
-                )
+        def load_v_scales():
+            for r in range(SCALE_ROWS):
+                nc.sync.dma_start(out=v_scale[r:P:QUADRANT, :, :].bitcast(I32), in_=v_scale_rows[r].bitcast(I32))
 
         load_scales(0, 1, nc.scalar)
         nc.scalar.activation(out=ident[:], in_=ident_raw[:], func=ACT.Relu)
@@ -116,124 +124,131 @@ def tile_archived_docs_feedback_d4_kernel(tc, docs_bytes, docs_scale, queries, n
         load_docs(10, 2)
         load_queries(2)
         load_queries(3)
-        load_docs(12, 4)
+        load_group(3)
+
+        def load_the_rest():
+            load_scales(3, 4, nc.sync)
+            load_v(0, 2)
+            load_v_scales()
+            load_norms(2, GROUPS)
+            load_scales(4, GROUPS, nc.sync)
+            load_group(4)
+            load_group(5)
+            load_v(2, GROUPS)
+            load_group(6)
+            load_group(7)
 
         inv_norms = keep.tile([P, GROUPS * PACK], F32, name="inv_norms")
-        q_turned = [keep.tile([P, K_PASSES, HALF, 2], F32, name="q_turned_%d" % half, align_bytes=64) for half in range(2)]
-        q_codes = keep.tile([P, K_PASSES, B], U32, name="q_codes", align_bytes=64)
-        q_scales = keep.tile([P, K_PASSES, B], U8, name="q_scales", align_bytes=64)
+        q_turned = [keep.tile([P, K_PASSES, HALF, 2], F32, name="q_turned_%d" % half, align_bytes=ALIGN) for half in range(2)]
+        q_codes = keep.tile([P, K_PASSES, B], U32, name="q_codes", align_bytes=ALIGN)
+        q_scales = keep.tile([P, K_PASSES, B], U8, name="q_scales", align_bytes=ALIGN)
 
         to_turn = {}
         turn_bank = {}
         turned = {}
         doc_codes = {}
         score_bank = {}
+        half_bank = {}
         rel_planes = {}
         rel_half = {}
         rel_packed = {}
         rel_codes = {}
         sums = {}
 
-        def widen(slab):
+        def scale_of(slab, i):
             n, s = slab
-            tile = work.tile([P, 2, P, 2], BF16, name="wide", tag="wide", bufs=16, align_bytes=64)
+            col = (n % PACK) * (K // G) + s * SLAB_BLOCKS + i
+            return doc_scale[n // PACK][:, col : col + 1]
+
+        def widen(slab):
+            tile = work.tile([P, 2, P, 2], BF16, name="wide", tag="wide", bufs=4 * PACK, align_bytes=ALIGN)
             words = tile[:].rearrange("p u w e -> p (u w e)").bitcast(F32)
             to_turn[slab] = [words[:, u * P : (u + 1) * P] for u in range(2)]
             per = G // PACK
-            for i in range(PASS // G):
-                col = (n % PACK) * SCALE_BLOCKS + s * (PASS // G) + i
+            for i in range(SLAB_BLOCKS):
                 src = doc_bytes[slab][:, G * i : G * (i + 1)].bitcast(FP8).rearrange("p (w u e) -> p u w e", u=2, e=2)
                 nc.vector.tensor_scalar(
                     out=tile[:, :, per * i : per * (i + 1), :],
                     in0=src,
-                    scalar1=doc_scale[n // PACK][:, col : col + 1],
+                    scalar1=scale_of(slab, i),
                     scalar2=None,
                     op0=ALU.mult,
                 )
 
         def widen_on_scalar(slab):
-            n, s = slab
-            plain = keep.tile([P, PASS], BF16, name="plain_%d_%d" % slab, align_bytes=64)
+            plain = keep.tile([P, PASS], BF16, name="plain_%d_%d" % slab, align_bytes=ALIGN)
             words = plain[:].bitcast(F32)
             to_turn[slab] = [words[:, u : 2 * P : 2] for u in range(2)]
-            for i in range(PASS // G):
-                col = (n % PACK) * SCALE_BLOCKS + s * (PASS // G) + i
+            for i in range(SLAB_BLOCKS):
                 nc.scalar.activation(
                     out=plain[:, G * i : G * (i + 1)],
                     in_=doc_bytes[slab][:, G * i : G * (i + 1)].bitcast(FP8),
                     func=ACT.Copy,
-                    scale=doc_scale[n // PACK][:, col : col + 1],
+                    scale=scale_of(slab, i),
                 )
-
-        def query_slabs(j):
-            words = q_raw[j][:].bitcast(F32)
-            for s in range(K_PASSES):
-                to_turn[(("q", j), s)] = [words[:, 2 * P * s + u : 2 * P * (s + 1) : 2] for u in range(2)]
-            return whole(("q", j))
-
-        def open_turn(slabs, tag):
-            turn_bank[slabs] = psum.tile([P, 2, 2, P], F32, name=tag, tag=tag)
-            return turn_bank[slabs]
-
-        def turn(slabs, tag):
-            bank = turn_bank[slabs] if slabs in turn_bank else open_turn(slabs, tag)
-            for i, slab in enumerate(slabs):
-                for u in range(2):
-                    nc.tensor.transpose(bank[:, i, u, :], to_turn[slab][u], ident[:])
 
         def whole(key):
             return ((key, 0), (key, 1))
 
-        def copy_turned(slabs, dst, copy=nc.scalar.copy):
-            copy(out=dst, in_=turn_bank[slabs][:].rearrange("p s u d -> p s d u"))
+        def widen_tile(n):
+            for slab in whole(n):
+                widen(slab)
+
+        def staggered(g):
+            n = PACK * g
+            return [((n, 0), (n + 1, 0)), ((n, 1), (n + 2, 0)), ((n + 1, 1), (n + 3, 0)), ((n + 2, 1), (n + 3, 1))]
+
+        def turn(slabs, tag):
+            turn_bank[slabs] = psum.tile([P, 2, 2, P], F32, name=tag, tag=tag)
+            for i, slab in enumerate(slabs):
+                for u in range(2):
+                    nc.tensor.transpose(turn_bank[slabs][:, i, u, :], to_turn[slab][u], ident[:])
+
+        def copy_turned(slabs, dst):
+            nc.scalar.copy(out=dst, in_=turn_bank[slabs][:].rearrange("p s u d -> p s d u"))
 
         def copy_docs(slabs):
-            tile = work.tile([P, 2, P, 2], F32, name="turned", tag="turned", bufs=10, align_bytes=64)
-            for i, slab in enumerate(slabs):
-                turned[slab] = (tile, i)
-            copy_turned(slabs, tile[:])
+            turned[slabs] = work.tile([P, 2, P, 2], F32, name="turned", tag="turned", bufs=2 * BANKS + 2, align_bytes=ALIGN)
+            copy_turned(slabs, turned[slabs][:])
 
-        def quantize_docs(*slabs):
-            tile, i = turned[slabs[0]]
-            width = len(slabs) * P
-            tag = "doc_codes%d" % len(slabs)
-            codes = work.tile([P, width], U32, name=tag, tag=tag, bufs=10, align_bytes=64)
-            tag = "doc_scales%d" % len(slabs)
-            scales = work.tile([P, width], U8, name=tag, tag=tag, bufs=10, align_bytes=64)
-            for m, slab in enumerate(slabs):
-                doc_codes[slab] = (codes[:, m * P : (m + 1) * P], scales[:, m * P : (m + 1) * P])
+        def quantize_docs(slabs):
+            codes = work.tile([P, 2 * P], U32, name="doc_codes", tag="doc_codes", bufs=2 * BANKS + 2, align_bytes=ALIGN)
+            scales = work.tile([P, 2 * P], U8, name="doc_scales", tag="doc_scales", bufs=2 * BANKS + 2, align_bytes=ALIGN)
+            for i, slab in enumerate(slabs):
+                doc_codes[slab] = (codes[:, i * P : (i + 1) * P], scales[:, i * P : (i + 1) * P])
             nc.vector.quantize_mx(
                 out=codes[:].bitcast(FP8X4),
                 scales=scales[:],
-                in_=tile[:, i : i + len(slabs), :, :].rearrange("p s d u -> p (s d u)").bitcast(BF16),
+                in_=turned[slabs][:].rearrange("p s d u -> p (s d u)").bitcast(BF16),
             )
 
-        def copy_queries(j, copy=nc.scalar.copy):
-            copy_turned(whole(("q", j)), q_turned[j // 2][:, :, (j % 2) * P : (j % 2 + 1) * P, :], copy)
+        def turn_queries(j, tag):
+            words = q_raw[j][:].bitcast(F32)
+            for s in range(K_PASSES):
+                to_turn[(("q", j), s)] = [words[:, 2 * P * s + u : 2 * P * (s + 1) : 2] for u in range(2)]
+            turn(whole(("q", j)), tag)
 
-        def quantize_queries(half, passes=range(K_PASSES)):
+        def copy_queries(j):
+            copy_turned(whole(("q", j)), q_turned[j // 2][:, :, (j % 2) * P : (j % 2 + 1) * P, :])
+
+        def quantize_queries(half):
             cols = slice(half * HALF, (half + 1) * HALF)
-            for s in passes:
+            for s in range(K_PASSES):
                 nc.vector.quantize_mx(
                     out=q_codes[:, s, cols].bitcast(FP8X4),
                     scales=q_scales[:, s, cols],
                     in_=q_turned[half][:, s, :, :].rearrange("p b u -> p (b u)").bitcast(BF16),
                 )
 
-        def warm_up(bank, slots):
-            for n in slots:
-                nc.tensor.matmul(out=bank, lhsT=zeros[:, 0:P], rhs=zeros[:, 0:N_TILE], start=True, stop=True)
+        def warm_up(dtype):
+            operand = zeros.bitcast(dtype)
+            nc.tensor.matmul(out=spare, lhsT=operand[:, 0:P], rhs=operand[:, 0:N_TILE], start=True, stop=True)
 
-        def open_scores(n, tag):
-            score_bank[n] = psum.tile([P, B], F32, name=tag, tag=tag)
-            return score_bank[n]
-
-        def scores(n, tag, cols=slice(0, B)):
-            bank = score_bank[n] if n in score_bank else open_scores(n, tag)
+        def score_passes(n, dst, cols):
             for s in range(K_PASSES):
                 codes, scales = doc_codes[(n, s)]
                 nc.tensor.matmul_mx(
-                    out=bank[:, cols],
+                    out=dst,
                     lhsT=codes.bitcast(FP8X4),
                     lhsT_scale=scales,
                     rhs=q_codes[:, s, cols].bitcast(FP8X4),
@@ -241,6 +256,17 @@ def tile_archived_docs_feedback_d4_kernel(tc, docs_bytes, docs_scale, queries, n
                     start=(s == 0),
                     stop=(s == K_PASSES - 1),
                 )
+
+        def scores(n, tag):
+            score_bank[n] = psum.tile([P, B], F32, name=tag, tag=tag)
+            score_passes(n, score_bank[n][:], slice(0, B))
+
+        def half_scores(g, half, tags):
+            for n in range(PACK * g, PACK * (g + 1)):
+                if n % 2 == 0:
+                    tag = tags[n % PACK // 2]
+                    half_bank[(n // 2, half)] = psum.tile([P, 2, HALF], F32, name=tag, tag=tag)
+                score_passes(n, half_bank[(n // 2, half)][:, n % 2, :], slice(half * HALF, (half + 1) * HALF))
 
         def invert_norms(g0, g1):
             nc.vector.reciprocal(out=inv_norms[:, g0 * PACK : g1 * PACK], in_=norms_raw[g0][:].rearrange("p g t -> p (g t)"))
@@ -248,58 +274,44 @@ def tile_archived_docs_feedback_d4_kernel(tc, docs_bytes, docs_scale, queries, n
         def relevance(n):
             g, t = divmod(n, PACK)
             if t == 0:
-                planes = keep.tile([P, PACK, B], BF16, name="rel_planes_%d" % g, align_bytes=64)
-                rel_planes[g] = planes
-                for half in range(2):
-                    rel_half[(g, half)] = planes[:, :, half * HALF : (half + 1) * HALF]
+                rel_planes[g] = keep.tile([P, PACK, B], BF16, name="rel_planes_%d" % g, align_bytes=ALIGN)
+                for half in (EARLY, LATE):
+                    rel_half[(g, half)] = rel_planes[g][:, :, half * HALF : (half + 1) * HALF]
             nc.scalar.activation(
                 out=rel_planes[g][:, t, :], in_=score_bank[n][:], func=ACT.Relu, scale=inv_norms[:, n : n + 1]
             )
 
-        def half_scores(n, half, tag):
-            if n % 2 == 0:
-                score_bank[(n // 2, half)] = psum.tile([P, 2, HALF], F32, name=tag, tag=tag)
-            cols = slice(half * HALF, (half + 1) * HALF)
-            for s in range(K_PASSES):
-                codes, scales = doc_codes[(n, s)]
-                nc.tensor.matmul_mx(
-                    out=score_bank[(n // 2, half)][:, n % 2, :],
-                    lhsT=codes.bitcast(FP8X4),
-                    lhsT_scale=scales,
-                    rhs=q_codes[:, s, cols].bitcast(FP8X4),
-                    rhs_scale=q_scales[:, s, cols],
-                    start=(s == 0),
-                    stop=(s == K_PASSES - 1),
+        def half_relevance(g, half):
+            planes = keep.tile([P, PACK, HALF], BF16, name="rel_planes_%d_%d" % (g, half), align_bytes=ALIGN)
+            rel_half[(g, half)] = planes[:]
+            for t in range(PACK):
+                n = PACK * g + t
+                nc.scalar.activation(
+                    out=planes[:, t, :],
+                    in_=half_bank[(n // 2, half)][:, n % 2, :],
+                    func=ACT.Relu,
+                    scale=inv_norms[:, n : n + 1],
                 )
 
-        def half_relevance(n, half):
-            g, t = divmod(n, PACK)
-            if t == 0:
-                planes = keep.tile([P, PACK, HALF], BF16, name="rel_planes_%d_%d" % (g, half), align_bytes=64)
-                rel_half[(g, half)] = planes[:]
-            nc.scalar.activation(
-                out=rel_half[(g, half)][:, t, :],
-                in_=score_bank[(n // 2, half)][:, n % 2, :],
-                func=ACT.Relu,
-                scale=inv_norms[:, n : n + 1],
-            )
+        def score_group(g):
+            for t in range(PACK):
+                scores(PACK * g + t, turn_tags[t])
+                relevance(PACK * g + t)
 
-        def interleave(g, half, copy, lo=0, hi=HALF):
-            if (g, half) not in rel_packed:
-                rel_packed[(g, half)] = work.tile([P, HALF, PACK], BF16, name="rel_packed", tag="rel_packed", bufs=6, align_bytes=64)
-            tile = rel_packed[(g, half)]
+        def interleave(g, half, copy):
+            tile = work.tile([P, HALF, PACK], BF16, name="rel_packed", tag="rel_packed", bufs=6, align_bytes=ALIGN)
+            rel_packed[(g, half)] = tile
             copy(
-                out=tile[:, lo:hi, :].rearrange("p (c i) t -> p c t i", i=8),
-                in_=rel_half[(g, half)][:, :, lo:hi].rearrange("p t (c i) -> p c t i", i=8),
+                out=tile[:].rearrange("p (c i) t -> p c t i", i=8),
+                in_=rel_half[(g, half)].rearrange("p t (c i) -> p c t i", i=8),
             )
 
         def quantize_rel(g, half):
-            r = (g, half)
-            codes = keep.tile([P, HALF], U32, name="rel_codes_%d_%d" % r, align_bytes=64)
-            scales = keep.tile([P, HALF], U8, name="rel_scales_%d_%d" % r, align_bytes=64)
-            rel_codes[r] = (codes, scales)
+            codes = keep.tile([P, HALF], U32, name="rel_codes_%d_%d" % (g, half), align_bytes=ALIGN)
+            scales = keep.tile([P, HALF], U8, name="rel_scales_%d_%d" % (g, half), align_bytes=ALIGN)
+            rel_codes[(g, half)] = (codes, scales)
             nc.vector.quantize_mx(
-                out=codes[:].bitcast(FP8X4), scales=scales[:], in_=rel_packed[r][:].rearrange("p b t -> p (b t)")
+                out=codes[:].bitcast(FP8X4), scales=scales[:], in_=rel_packed[(g, half)][:].rearrange("p b t -> p (b t)")
             )
 
         def pool_pass(g, j, first, width, tag):
@@ -314,7 +326,7 @@ def tile_archived_docs_feedback_d4_kernel(tc, docs_bytes, docs_scale, queries, n
                 rhs=v_codes[g][:, 2 * first : 2 * (first + width)].bitcast(FP4X4),
                 rhs_scale=v_scale[:, g, first : first + width],
                 start=(g == 0),
-                stop=(g == GROUPS - 1),
+                stop=(g == LAST),
             )
 
         def store(j, first, width, copy):
@@ -324,207 +336,178 @@ def tile_archived_docs_feedback_d4_kernel(tc, docs_bytes, docs_scale, queries, n
             queue = nc.scalar if (j, first + width) == (Q_TILES - 1, N) else nc.sync
             queue.dma_start(out=out[j * P : (j + 1) * P, first : first + width], in_=result[:])
 
-        early_sums = [(j, first) for j in range(2) for first in range(0, N, N_TILE)]
-        sum_tags = ["acc%d" % i for i in range(4)]
-        turn_tags = ["rot%d" % i for i in range(4)]
+        turn_tags = ["rot%d" % i for i in range(BANKS)]
+        sum_tags = ["acc%d" % i for i in range(BANKS)]
+        first_free, last_free = sum_tags[:2], sum_tags[2:]
+        early_sums = [(j, first) for j in range(Q_TILES // 2) for first in range(0, N, N_TILE)]
 
         def early_passes(g, lo, hi):
             for i in range(lo, hi):
-                pool_pass(g, early_sums[i][0], early_sums[i][1], N_TILE, sum_tags[(i + 2) % 4])
+                j, first = early_sums[i]
+                pool_pass(g, j, first, N_TILE, sum_tags[i])
 
-        def pair_banks(n):
-            return [((n, s), (n + 1, s)) for s in range(K_PASSES)]
+        def held(g):
+            return HELD_LONG if g in (0, LAST - 3) else HELD
+
+        def turn_group(g):
+            for i, slabs in enumerate(staggered(g)):
+                turn(slabs, turn_tags[i])
+                copy_docs(slabs)
 
         on_vector, on_scalar = nc.vector.tensor_copy, nc.scalar.copy
-
-        def widen_tile(n):
-            for slab in whole(n):
-                widen(slab)
-
-        def staggered(g):
-            n = PACK * g
-            return [((n, 0), (n + 1, 0)), ((n, 1), (n + 2, 0)), ((n + 1, 1), (n + 3, 0)), ((n + 2, 1), (n + 3, 1))]
 
         widen_tile(0)
         widen((1, 0))
         widen_on_scalar((1, 1))
-        spare = psum.tile([P, N_TILE], F32, name=sum_tags[0], tag=sum_tags[0])[:]
-        warm_up(spare, range(5))
+        spare = psum.tile([P, N_TILE], F32, name=last_free[0], tag=last_free[0])[:]
+        warm_up(F32)
         turn(whole(0), turn_tags[0])
         copy_docs(whole(0))
-        warm_up(spare, range(1))
+        warm_up(BF16)
         turn(whole(1), turn_tags[1])
         copy_docs(whole(1))
-        warm_up(spare, range(1))
+        warm_up(BF16)
         widen_tile(2)
         widen_tile(3)
         turn(whole(2), turn_tags[2])
         copy_docs(whole(2))
-        turn(query_slabs(0), sum_tags[2])
+        turn_queries(0, first_free[0])
         copy_queries(0)
         turn(whole(3), turn_tags[3])
-        copy_docs(whole(3))
-        warm_up(spare, range(1))
-        quantize_docs(*whole(0))
+        warm_up(BF16)
+        quantize_docs(whole(0))
         widen_tile(4)
-        quantize_docs(*whole(1))
-        widen_tile(5)
-        banks = {1: staggered(1), 2: staggered(2)}
-        turn(query_slabs(1), sum_tags[3])
+        quantize_docs(whole(1))
+        widen((5, 0))
+        widen_on_scalar((5, 1))
+        turn_queries(1, first_free[1])
         copy_queries(1)
-        warm_up(spare, range(0))
-        turn(banks[1][0], turn_tags[0])
-        copy_docs(banks[1][0])
-        quantize_docs(*whole(2))
+        copy_docs(whole(3))
+        group_1, group_2 = staggered(1), staggered(2)
+        turn(group_1[0], turn_tags[0])
+        copy_docs(group_1[0])
+        quantize_docs(whole(2))
         widen_tile(6)
         widen_tile(7)
-        quantize_queries(0)
-        quantize_docs(*whole(3))
+        quantize_queries(EARLY)
+        quantize_docs(whole(3))
         invert_norms(0, 2)
-        for i in range(1, PACK):
-            warm_up(spare, range([1,1,0][i - 1]))
-            turn(banks[1][i], turn_tags[i])
-            copy_docs(banks[1][i])
+        for i in range(1, BANKS):
+            if i < BANKS - 1:
+                warm_up(BF16)
+            turn(group_1[i], turn_tags[i])
+            copy_docs(group_1[i])
+        load_the_rest()
 
-        load_scales(3, 4, nc.sync)
-        load_v(0, 2)
-        load_v_scales(0, 8)
-        load_norms(2, 8)
-        load_scales(4, 8, nc.sync)
-        load_docs(16, 4)
-        load_docs(20, 4)
-        load_v(2, 8)
-        load_docs(24, 4)
-        load_docs(28, 4)
-        for n in range(PACK):
-            half_scores(n, EARLY, sum_tags[n // 2])
+        half_scores(0, EARLY, last_free)
         widen_tile(8)
         widen_tile(9)
-        for slabs in banks[1]:
-            quantize_docs(*slabs)
+        for slabs in group_1:
+            quantize_docs(slabs)
         widen_tile(10)
         widen_tile(11)
-        for n in range(PACK):
-            half_relevance(n, EARLY)
-        for j in (2, 3):
-            turn(query_slabs(j), sum_tags[j])
+        half_relevance(0, EARLY)
+        for j, tag in zip((2, 3), first_free):
+            turn_queries(j, tag)
             copy_queries(j)
-        for n in range(PACK, 2 * PACK):
-            half_scores(n, EARLY, sum_tags[n // 2 % 2])
-        for i in range(PACK):
-            turn(banks[2][i], turn_tags[i])
-        quantize_queries(1)
+        half_scores(1, EARLY, last_free)
+        for i, slabs in enumerate(group_2):
+            turn(slabs, turn_tags[i])
+        quantize_queries(LATE)
         interleave(0, EARLY, on_vector)
-        for n in range(PACK, 2 * PACK):
-            half_relevance(n, EARLY)
-        copy_docs(banks[2][0])
-        copy_docs(banks[2][1])
-        copy_docs(banks[2][2])
-        for n in range(PACK):
-            half_scores(n, LATE, sum_tags[2 + n // 2])
-        for n in range(PACK):
-            half_relevance(n, LATE)
-        for n in range(PACK, 2 * PACK):
-            half_scores(n, LATE, sum_tags[n // 2 % 2])
-        copy_docs(banks[2][3])
-        for n in range(PACK, 2 * PACK):
-            half_relevance(n, LATE)
+        half_relevance(1, EARLY)
+        copy_docs(group_2[0])
+        copy_docs(group_2[1])
+        half_scores(0, LATE, first_free)
+        half_relevance(0, LATE)
+        half_scores(1, LATE, last_free)
+        copy_docs(group_2[2])
+        copy_docs(group_2[3])
+        half_relevance(1, LATE)
         widen_tile(12)
         quantize_rel(0, EARLY)
         for n in range(13, 16):
             widen_tile(n)
         invert_norms(2, GROUPS)
+        early_passes(0, 0, BANKS - held(0))
 
-        last = GROUPS - 1
-        HOLD = [2,1,1,1,2]
-        early_passes(0, 0, 4 - HOLD[0])
-        for g in range(2, last - 1):
-            banks[g + 1] = staggered(g + 1)
-            for i, slabs in enumerate(banks[g + 1]):
-                turn(slabs, turn_tags[i])
-                copy_docs(slabs)
-            early_passes(g - 2, 4 - HOLD[g - 2], 4)
-            for slabs in banks[g][(0 if g < AHEAD else 1) :]:
-                quantize_docs(*slabs)
+        for g in range(2, LAST - 1):
+            turn_group(g + 1)
+            early_passes(g - 2, BANKS - held(g - 2), BANKS)
+            for slabs in staggered(g)[(1 if g >= AHEAD_FROM else 0) :]:
+                quantize_docs(slabs)
             interleave(g - 1, EARLY, on_vector)
-            for t in range(PACK):
-                scores(PACK * g + t, turn_tags[t])
-                relevance(PACK * g + t)
+            score_group(g)
+            ahead = staggered(g + 1)
             n = PACK * (g + 2)
             widen_tile(n)
-            quantize_rel(g - 1, EARLY)
-            if g < last - 2:
+            if g + 2 < LAST:
+                quantize_rel(g - 1, EARLY)
                 widen_tile(n + 1)
                 widen_tile(n + 2)
-                if g + 1 >= AHEAD:
-                    quantize_docs(*banks[g + 1][0])
+                quantize_docs(ahead[0])
                 widen_tile(n + 3)
             else:
-                quantize_docs(*banks[g + 1][0])
-                quantize_docs(*banks[g + 1][1])
+                quantize_docs(ahead[0])
+                quantize_rel(g - 1, EARLY)
+                quantize_docs(ahead[1])
                 widen_tile(n + 1)
-                quantize_docs(*banks[g + 1][2])
-                quantize_docs(*banks[g + 1][3])
+                quantize_docs(ahead[2])
+                quantize_docs(ahead[3])
                 widen_tile(n + 2)
                 widen_tile(n + 3)
-            early_passes(g - 1, 0, 4 - HOLD[g - 1])
-        g = last - 1
-        for t in range(PACK):
-            scores(PACK * g + t, turn_tags[t])
-            relevance(PACK * g + t)
-        early_passes(g - 2, 4 - HOLD[g - 2], 4)
-        banks[last] = staggered(last)
-        for i, slabs in enumerate(banks[last]):
-            turn(slabs, turn_tags[i])
-            copy_docs(slabs)
-        interleave(g - 1, EARLY, on_vector)
-        interleave(0, LATE, on_vector)
-        quantize_rel(g - 1, EARLY)
+            early_passes(g - 1, 0, BANKS - held(g - 1))
 
-        interleave(g, EARLY, on_vector)
+        score_group(LAST - 1)
+        early_passes(LAST - 3, BANKS - held(LAST - 3), BANKS)
+        turn_group(LAST)
+        final = staggered(LAST)
+        interleave(LAST - 2, EARLY, on_vector)
+        interleave(0, LATE, on_vector)
+        quantize_rel(LAST - 2, EARLY)
+        interleave(LAST - 1, EARLY, on_vector)
         quantize_rel(0, LATE)
-        quantize_docs(*banks[last][0])
-        quantize_docs(*banks[last][1])
-        quantize_rel(g, EARLY)
-        quantize_docs(*banks[last][2])
-        quantize_docs(*banks[last][3])
-        early_passes(g - 1, 0, 4)
-        for t in range(PACK):
-            scores(PACK * last + t, turn_tags[t])
-            relevance(PACK * last + t)
+        quantize_docs(final[0])
+        quantize_docs(final[1])
+        quantize_rel(LAST - 1, EARLY)
+        quantize_docs(final[2])
+        quantize_docs(final[3])
+        early_passes(LAST - 2, 0, BANKS)
+        score_group(LAST)
+
         interleave(1, LATE, on_vector)
         interleave(2, LATE, on_vector)
         quantize_rel(1, LATE)
         interleave(3, LATE, on_vector)
         quantize_rel(2, LATE)
-        interleave(last, EARLY, on_vector)
+        interleave(LAST, EARLY, on_vector)
         quantize_rel(3, LATE)
-        quantize_rel(last, EARLY)
-        interleave(5, LATE, on_scalar)
-        interleave(last, LATE, on_scalar)
+        quantize_rel(LAST, EARLY)
+        for g in (5, 7):
+            interleave(g, LATE, on_scalar)
         for g in (4, 6):
             interleave(g, LATE, on_vector)
             quantize_rel(g + 1, LATE)
             quantize_rel(g, LATE)
 
-        early_passes(last - 1, 0, 4)
+        early_passes(LAST - 1, 0, BANKS)
         for g in range(GROUPS):
             if g == LATE_BEFORE_CLOSE:
-                early_passes(last, 0, 4)
+                early_passes(LAST, 0, BANKS)
                 for j, first in early_sums:
                     store(j, first, N_TILE, on_scalar)
             for first in range(0, N, N_TILE):
                 pool_pass(g, 2, first, N_TILE, turn_tags[first // N_TILE])
-            if g < 6:
+            if g < GROUPS - LATE_STAGGER:
                 pool_pass(g, 3, 0, N_TILE, turn_tags[2])
         store(2, 0, N_TILE, on_vector)
         store(2, N_TILE, N_TILE, on_scalar)
-        for g in range(6, GROUPS):
+        for g in range(GROUPS - LATE_STAGGER, GROUPS):
             pool_pass(g, 3, 0, N_TILE, turn_tags[2])
         store(3, 0, N_TILE, on_scalar)
         first = N_TILE
         for i, width in enumerate(LAST_WIDTHS):
             for g in range(GROUPS):
-                pool_pass(g, 3, first, width, sum_tags[(i + 2) % 4])
+                pool_pass(g, 3, first, width, sum_tags[i])
             store(3, first, width, on_scalar)
             first = first + width

from contextlib import ExitStack

import concourse.mybir as mybir
from concourse.masks import make_identity

T, K, B, N, G = 4096, 1024, 512, 1024, 128
FLOPS = 2 * T * K * B + 2 * B * T * N

F32 = mybir.dt.float32
BF16 = mybir.dt.bfloat16
I32 = mybir.dt.int32
U32 = mybir.dt.uint32
U8 = mybir.dt.uint8
FP8 = mybir.dt.float8_e4m3fn
FP8X4 = mybir.dt.float8_e4m3fn_x4
FP4X4 = mybir.dt.float4_e2m1fn_x4
ACT = mybir.ActivationFunctionType
ALU = mybir.AluOpType

P = 128
QUADRANT = 32
SCALE_ROWS = 4
PACK = 4
PASS = P * PACK
GROUPS = T // PASS
LAST = GROUPS - 1
K_PASSES = K // PASS
SLAB_BLOCKS = PASS // G
Q_TILES = B // P
N_TILE = 512
BANKS = 4
HALF = B // 2
EARLY, LATE = 0, 1
ALIGN = 64

FIRST_WORDS = 513
SECOND_WORDS = 189
HELD_LONG, HELD = 2, 1
AHEAD_FROM = 3
LATE_BEFORE_CLOSE = 3
LATE_STAGGER = 2
LAST_WIDTHS = [2 * P, P, P]


def tile_archived_docs_feedback_d4_kernel(tc, docs_bytes, docs_scale, queries, norms, v_words, v_scales, out):
    nc = tc.nc
    with ExitStack() as ctx:
        keep = ctx.enter_context(tc.tile_pool(name="keep", bufs=1))
        work = ctx.enter_context(tc.tile_pool(name="work", bufs=2))
        psum = ctx.enter_context(tc.psum_pool(name="psum", bufs=1))
        ctx.enter_context(tc.manual_schedule())

        ident_raw = keep.tile([P, P], F32, name="ident_raw")
        make_identity(nc, ident_raw[:])
        ident = keep.tile([P, P], F32, name="ident")

        v_scale = keep.tile([P, GROUPS, N], U8, name="v_scale", align_bytes=ALIGN)
        filler = v_scale[:].rearrange("p g n -> p (g n)").bitcast(I32)
        filler_words = GROUPS * N // 4
        second_end = filler_words - FIRST_WORDS
        nc.vector.memset(filler[:, second_end:], 0)
        nc.vector.memset(filler[:, second_end - SECOND_WORDS : second_end], 0)
        nc.vector.memset(filler[:, : second_end - SECOND_WORDS], 0)
        zeros = filler[:, filler_words - N_TILE :]

        docs_rows = docs_bytes.rearrange("(g m t) k -> g m t k", m=P, t=PACK)
        scale_rows = docs_scale.rearrange("(g m t) i -> m g (t i)", m=P, t=PACK)
        norm_rows = norms.rearrange("(g m t) -> m g t", m=P, t=PACK)
        v_scale_rows = v_scales.rearrange("g (q r) n -> r q g n", r=SCALE_ROWS)
        doc_bytes = {}
        doc_scale = {}
        q_raw = {}
        v_codes = {}
        norms_raw = {}

        def load_docs(first_tile, count):
            g, t = divmod(first_tile, PACK)
            tile = keep.tile([P, count, K], U8, name="doc_bytes_%d" % first_tile, align_bytes=ALIGN)
            nc.sync.dma_start(out=tile[:], in_=docs_rows[g, :, t : t + count, :])
            for i in range(count):
                for s in range(K_PASSES):
                    doc_bytes[(first_tile + i, s)] = tile[:, i, s * PASS : (s + 1) * PASS]

        def load_group(g):
            load_docs(PACK * g, PACK)

        def load_scales(g0, g1, queue):
            tile = keep.tile([P, g1 - g0, PACK * K // G], F32, name="doc_scale_%d" % g0)
            queue.dma_start(out=tile[:], in_=scale_rows[:, g0:g1, :])
            for g in range(g0, g1):
                doc_scale[g] = tile[:, g - g0, :]

        def load_queries(j):
            q_raw[j] = keep.tile([P, K], BF16, name="q_raw_%d" % j, align_bytes=ALIGN)
            nc.sync.dma_start(out=q_raw[j][:], in_=queries[j * P : (j + 1) * P, :])

        def load_v(g0, g1):
            tile = keep.tile([P, g1 - g0, 2 * N], U8, name="v_codes_%d" % g0, align_bytes=ALIGN)
            nc.sync.dma_start(out=tile[:].bitcast(I32), in_=v_words[g0:g1].rearrange("g p n -> p g n").bitcast(I32))
            for g in range(g0, g1):
                v_codes[g] = tile[:, g - g0, :]

        def load_norms(g0, g1):
            norms_raw[g0] = keep.tile([P, g1 - g0, PACK], BF16, name="norms_raw_%d" % g0)
            nc.sync.dma_start(out=norms_raw[g0][:], in_=norm_rows[:, g0:g1, :])

        def load_v_scales():
            for r in range(SCALE_ROWS):
                nc.sync.dma_start(out=v_scale[r:P:QUADRANT, :, :].bitcast(I32), in_=v_scale_rows[r].bitcast(I32))

        load_scales(0, 1, nc.scalar)
        nc.scalar.activation(out=ident[:], in_=ident_raw[:], func=ACT.Relu)
        load_docs(0, 1)
        load_docs(1, 1)
        load_docs(2, 2)
        load_queries(0)
        load_scales(1, 2, nc.sync)
        load_docs(4, 2)
        load_queries(1)
        load_docs(6, 2)
        load_scales(2, 3, nc.sync)
        load_norms(0, 2)
        load_docs(8, 2)
        load_docs(10, 2)
        load_queries(2)
        load_queries(3)
        load_group(3)

        def load_the_rest():
            load_scales(3, 4, nc.sync)
            load_v(0, 2)
            load_v_scales()
            load_norms(2, GROUPS)
            load_scales(4, GROUPS, nc.sync)
            load_group(4)
            load_group(5)
            load_v(2, GROUPS)
            load_group(6)
            load_group(7)

        inv_norms = keep.tile([P, GROUPS * PACK], F32, name="inv_norms")
        q_turned = [keep.tile([P, K_PASSES, HALF, 2], F32, name="q_turned_%d" % half, align_bytes=ALIGN) for half in range(2)]
        q_codes = keep.tile([P, K_PASSES, B], U32, name="q_codes", align_bytes=ALIGN)
        q_scales = keep.tile([P, K_PASSES, B], U8, name="q_scales", align_bytes=ALIGN)

        to_turn = {}
        turn_bank = {}
        turned = {}
        doc_codes = {}
        score_bank = {}
        half_bank = {}
        rel_planes = {}
        rel_half = {}
        rel_packed = {}
        rel_codes = {}
        sums = {}

        def scale_of(slab, i):
            n, s = slab
            col = (n % PACK) * (K // G) + s * SLAB_BLOCKS + i
            return doc_scale[n // PACK][:, col : col + 1]

        def widen(slab):
            tile = work.tile([P, 2, P, 2], BF16, name="wide", tag="wide", bufs=4 * PACK, align_bytes=ALIGN)
            words = tile[:].rearrange("p u w e -> p (u w e)").bitcast(F32)
            to_turn[slab] = [words[:, u * P : (u + 1) * P] for u in range(2)]
            per = G // PACK
            for i in range(SLAB_BLOCKS):
                src = doc_bytes[slab][:, G * i : G * (i + 1)].bitcast(FP8).rearrange("p (w u e) -> p u w e", u=2, e=2)
                nc.vector.tensor_scalar(
                    out=tile[:, :, per * i : per * (i + 1), :],
                    in0=src,
                    scalar1=scale_of(slab, i),
                    scalar2=None,
                    op0=ALU.mult,
                )

        def widen_on_scalar(slab):
            plain = keep.tile([P, PASS], BF16, name="plain_%d_%d" % slab, align_bytes=ALIGN)
            words = plain[:].bitcast(F32)
            to_turn[slab] = [words[:, u : 2 * P : 2] for u in range(2)]
            for i in range(SLAB_BLOCKS):
                nc.scalar.activation(
                    out=plain[:, G * i : G * (i + 1)],
                    in_=doc_bytes[slab][:, G * i : G * (i + 1)].bitcast(FP8),
                    func=ACT.Copy,
                    scale=scale_of(slab, i),
                )

        def whole(key):
            return ((key, 0), (key, 1))

        def widen_tile(n):
            for slab in whole(n):
                widen(slab)

        def staggered(g):
            n = PACK * g
            return [((n, 0), (n + 1, 0)), ((n, 1), (n + 2, 0)), ((n + 1, 1), (n + 3, 0)), ((n + 2, 1), (n + 3, 1))]

        def turn(slabs, tag):
            turn_bank[slabs] = psum.tile([P, 2, 2, P], F32, name=tag, tag=tag)
            for i, slab in enumerate(slabs):
                for u in range(2):
                    nc.tensor.transpose(turn_bank[slabs][:, i, u, :], to_turn[slab][u], ident[:])

        def copy_turned(slabs, dst):
            nc.scalar.copy(out=dst, in_=turn_bank[slabs][:].rearrange("p s u d -> p s d u"))

        def copy_docs(slabs):
            turned[slabs] = work.tile([P, 2, P, 2], F32, name="turned", tag="turned", bufs=2 * BANKS + 2, align_bytes=ALIGN)
            copy_turned(slabs, turned[slabs][:])

        def quantize_docs(slabs):
            codes = work.tile([P, 2 * P], U32, name="doc_codes", tag="doc_codes", bufs=2 * BANKS + 2, align_bytes=ALIGN)
            scales = work.tile([P, 2 * P], U8, name="doc_scales", tag="doc_scales", bufs=2 * BANKS + 2, align_bytes=ALIGN)
            for i, slab in enumerate(slabs):
                doc_codes[slab] = (codes[:, i * P : (i + 1) * P], scales[:, i * P : (i + 1) * P])
            nc.vector.quantize_mx(
                out=codes[:].bitcast(FP8X4),
                scales=scales[:],
                in_=turned[slabs][:].rearrange("p s d u -> p (s d u)").bitcast(BF16),
            )

        def turn_queries(j, tag):
            words = q_raw[j][:].bitcast(F32)
            for s in range(K_PASSES):
                to_turn[(("q", j), s)] = [words[:, 2 * P * s + u : 2 * P * (s + 1) : 2] for u in range(2)]
            turn(whole(("q", j)), tag)

        def copy_queries(j):
            copy_turned(whole(("q", j)), q_turned[j // 2][:, :, (j % 2) * P : (j % 2 + 1) * P, :])

        def quantize_queries(half):
            cols = slice(half * HALF, (half + 1) * HALF)
            for s in range(K_PASSES):
                nc.vector.quantize_mx(
                    out=q_codes[:, s, cols].bitcast(FP8X4),
                    scales=q_scales[:, s, cols],
                    in_=q_turned[half][:, s, :, :].rearrange("p b u -> p (b u)").bitcast(BF16),
                )

        def warm_up(dtype):
            operand = zeros.bitcast(dtype)
            nc.tensor.matmul(out=spare, lhsT=operand[:, 0:P], rhs=operand[:, 0:N_TILE], start=True, stop=True)

        def score_passes(n, dst, cols):
            for s in range(K_PASSES):
                codes, scales = doc_codes[(n, s)]
                nc.tensor.matmul_mx(
                    out=dst,
                    lhsT=codes.bitcast(FP8X4),
                    lhsT_scale=scales,
                    rhs=q_codes[:, s, cols].bitcast(FP8X4),
                    rhs_scale=q_scales[:, s, cols],
                    start=(s == 0),
                    stop=(s == K_PASSES - 1),
                )

        def scores(n, tag):
            score_bank[n] = psum.tile([P, B], F32, name=tag, tag=tag)
            score_passes(n, score_bank[n][:], slice(0, B))

        def half_scores(g, half, tags):
            for n in range(PACK * g, PACK * (g + 1)):
                if n % 2 == 0:
                    tag = tags[n % PACK // 2]
                    half_bank[(n // 2, half)] = psum.tile([P, 2, HALF], F32, name=tag, tag=tag)
                score_passes(n, half_bank[(n // 2, half)][:, n % 2, :], slice(half * HALF, (half + 1) * HALF))

        def invert_norms(g0, g1):
            nc.vector.reciprocal(out=inv_norms[:, g0 * PACK : g1 * PACK], in_=norms_raw[g0][:].rearrange("p g t -> p (g t)"))

        def relevance(n):
            g, t = divmod(n, PACK)
            if t == 0:
                rel_planes[g] = keep.tile([P, PACK, B], BF16, name="rel_planes_%d" % g, align_bytes=ALIGN)
                for half in (EARLY, LATE):
                    rel_half[(g, half)] = rel_planes[g][:, :, half * HALF : (half + 1) * HALF]
            nc.scalar.activation(
                out=rel_planes[g][:, t, :], in_=score_bank[n][:], func=ACT.Relu, scale=inv_norms[:, n : n + 1]
            )

        def half_relevance(g, half):
            planes = keep.tile([P, PACK, HALF], BF16, name="rel_planes_%d_%d" % (g, half), align_bytes=ALIGN)
            rel_half[(g, half)] = planes[:]
            for t in range(PACK):
                n = PACK * g + t
                nc.scalar.activation(
                    out=planes[:, t, :],
                    in_=half_bank[(n // 2, half)][:, n % 2, :],
                    func=ACT.Relu,
                    scale=inv_norms[:, n : n + 1],
                )

        def score_group(g):
            for t in range(PACK):
                scores(PACK * g + t, turn_tags[t])
                relevance(PACK * g + t)

        def interleave(g, half, copy):
            tile = work.tile([P, HALF, PACK], BF16, name="rel_packed", tag="rel_packed", bufs=6, align_bytes=ALIGN)
            rel_packed[(g, half)] = tile
            copy(
                out=tile[:].rearrange("p (c i) t -> p c t i", i=8),
                in_=rel_half[(g, half)].rearrange("p t (c i) -> p c t i", i=8),
            )

        def quantize_rel(g, half):
            codes = keep.tile([P, HALF], U32, name="rel_codes_%d_%d" % (g, half), align_bytes=ALIGN)
            scales = keep.tile([P, HALF], U8, name="rel_scales_%d_%d" % (g, half), align_bytes=ALIGN)
            rel_codes[(g, half)] = (codes, scales)
            nc.vector.quantize_mx(
                out=codes[:].bitcast(FP8X4), scales=scales[:], in_=rel_packed[(g, half)][:].rearrange("p b t -> p (b t)")
            )

        def pool_pass(g, j, first, width, tag):
            if g == 0:
                sums[(j, first)] = psum.tile([P, width], F32, name=tag, tag=tag)
            codes, scales = rel_codes[(g, j // 2)]
            cols = slice((j % 2) * P, (j % 2 + 1) * P)
            nc.tensor.matmul_mx(
                out=sums[(j, first)][:],
                lhsT=codes[:, cols].bitcast(FP8X4),
                lhsT_scale=scales[:, cols],
                rhs=v_codes[g][:, 2 * first : 2 * (first + width)].bitcast(FP4X4),
                rhs_scale=v_scale[:, g, first : first + width],
                start=(g == 0),
                stop=(g == LAST),
            )

        def store(j, first, width, copy):
            tag = "result%d" % width
            result = work.tile([P, width], F32, name=tag, tag=tag, bufs=7 if width == N_TILE else 2)
            copy(out=result[:], in_=sums[(j, first)][:])
            queue = nc.scalar if (j, first + width) == (Q_TILES - 1, N) else nc.sync
            queue.dma_start(out=out[j * P : (j + 1) * P, first : first + width], in_=result[:])

        turn_tags = ["rot%d" % i for i in range(BANKS)]
        sum_tags = ["acc%d" % i for i in range(BANKS)]
        first_free, last_free = sum_tags[:2], sum_tags[2:]
        early_sums = [(j, first) for j in range(Q_TILES // 2) for first in range(0, N, N_TILE)]

        def early_passes(g, lo, hi):
            for i in range(lo, hi):
                j, first = early_sums[i]
                pool_pass(g, j, first, N_TILE, sum_tags[i])

        def held(g):
            return HELD_LONG if g in (0, LAST - 3) else HELD

        def turn_group(g):
            for i, slabs in enumerate(staggered(g)):
                turn(slabs, turn_tags[i])
                copy_docs(slabs)

        on_vector, on_scalar = nc.vector.tensor_copy, nc.scalar.copy

        widen_tile(0)
        widen((1, 0))
        widen_on_scalar((1, 1))
        spare = psum.tile([P, N_TILE], F32, name=last_free[0], tag=last_free[0])[:]
        warm_up(F32)
        turn(whole(0), turn_tags[0])
        copy_docs(whole(0))
        warm_up(BF16)
        turn(whole(1), turn_tags[1])
        copy_docs(whole(1))
        warm_up(BF16)
        widen_tile(2)
        widen_tile(3)
        turn(whole(2), turn_tags[2])
        copy_docs(whole(2))
        turn_queries(0, first_free[0])
        copy_queries(0)
        turn(whole(3), turn_tags[3])
        warm_up(BF16)
        quantize_docs(whole(0))
        widen_tile(4)
        quantize_docs(whole(1))
        widen((5, 0))
        widen_on_scalar((5, 1))
        turn_queries(1, first_free[1])
        copy_queries(1)
        copy_docs(whole(3))
        group_1, group_2 = staggered(1), staggered(2)
        turn(group_1[0], turn_tags[0])
        copy_docs(group_1[0])
        quantize_docs(whole(2))
        widen_tile(6)
        widen_tile(7)
        quantize_queries(EARLY)
        quantize_docs(whole(3))
        invert_norms(0, 2)
        for i in range(1, BANKS):
            if i < BANKS - 1:
                warm_up(BF16)
            turn(group_1[i], turn_tags[i])
            copy_docs(group_1[i])
        load_the_rest()

        half_scores(0, EARLY, last_free)
        widen_tile(8)
        widen_tile(9)
        for slabs in group_1:
            quantize_docs(slabs)
        widen_tile(10)
        widen_tile(11)
        half_relevance(0, EARLY)
        for j, tag in zip((2, 3), first_free):
            turn_queries(j, tag)
            copy_queries(j)
        half_scores(1, EARLY, last_free)
        for i, slabs in enumerate(group_2):
            turn(slabs, turn_tags[i])
        quantize_queries(LATE)
        interleave(0, EARLY, on_vector)
        half_relevance(1, EARLY)
        copy_docs(group_2[0])
        copy_docs(group_2[1])
        half_scores(0, LATE, first_free)
        half_relevance(0, LATE)
        half_scores(1, LATE, last_free)
        copy_docs(group_2[2])
        copy_docs(group_2[3])
        half_relevance(1, LATE)
        widen_tile(12)
        quantize_rel(0, EARLY)
        for n in range(13, 16):
            widen_tile(n)
        invert_norms(2, GROUPS)
        early_passes(0, 0, BANKS - held(0))

        for g in range(2, LAST - 1):
            turn_group(g + 1)
            early_passes(g - 2, BANKS - held(g - 2), BANKS)
            for slabs in staggered(g)[(1 if g >= AHEAD_FROM else 0) :]:
                quantize_docs(slabs)
            interleave(g - 1, EARLY, on_vector)
            score_group(g)
            ahead = staggered(g + 1)
            n = PACK * (g + 2)
            widen_tile(n)
            if g + 2 < LAST:
                quantize_rel(g - 1, EARLY)
                widen_tile(n + 1)
                widen_tile(n + 2)
                quantize_docs(ahead[0])
                widen_tile(n + 3)
            else:
                quantize_docs(ahead[0])
                quantize_rel(g - 1, EARLY)
                quantize_docs(ahead[1])
                widen_tile(n + 1)
                quantize_docs(ahead[2])
                quantize_docs(ahead[3])
                widen_tile(n + 2)
                widen_tile(n + 3)
            early_passes(g - 1, 0, BANKS - held(g - 1))

        score_group(LAST - 1)
        early_passes(LAST - 3, BANKS - held(LAST - 3), BANKS)
        turn_group(LAST)
        final = staggered(LAST)
        interleave(LAST - 2, EARLY, on_vector)
        interleave(0, LATE, on_vector)
        quantize_rel(LAST - 2, EARLY)
        interleave(LAST - 1, EARLY, on_vector)
        quantize_rel(0, LATE)
        quantize_docs(final[0])
        quantize_docs(final[1])
        quantize_rel(LAST - 1, EARLY)
        quantize_docs(final[2])
        quantize_docs(final[3])
        early_passes(LAST - 2, 0, BANKS)
        score_group(LAST)

        interleave(1, LATE, on_vector)
        interleave(2, LATE, on_vector)
        quantize_rel(1, LATE)
        interleave(3, LATE, on_vector)
        quantize_rel(2, LATE)
        interleave(LAST, EARLY, on_vector)
        quantize_rel(3, LATE)
        quantize_rel(LAST, EARLY)
        for g in (5, 7):
            interleave(g, LATE, on_scalar)
        for g in (4, 6):
            interleave(g, LATE, on_vector)
            quantize_rel(g + 1, LATE)
            quantize_rel(g, LATE)

        early_passes(LAST - 1, 0, BANKS)
        for g in range(GROUPS):
            if g == LATE_BEFORE_CLOSE:
                early_passes(LAST, 0, BANKS)
                for j, first in early_sums:
                    store(j, first, N_TILE, on_scalar)
            for first in range(0, N, N_TILE):
                pool_pass(g, 2, first, N_TILE, turn_tags[first // N_TILE])
            if g < GROUPS - LATE_STAGGER:
                pool_pass(g, 3, 0, N_TILE, turn_tags[2])
        store(2, 0, N_TILE, on_vector)
        store(2, N_TILE, N_TILE, on_scalar)
        for g in range(GROUPS - LATE_STAGGER, GROUPS):
            pool_pass(g, 3, 0, N_TILE, turn_tags[2])
        store(3, 0, N_TILE, on_scalar)
        first = N_TILE
        for i, width in enumerate(LAST_WIDTHS):
            for g in range(GROUPS):
                pool_pass(g, 3, first, width, sum_tags[i])
            store(3, first, width, on_scalar)
            first = first + width
